import numpy as np, ml_dtypes
CORES = [5,29,101,125,133,157,229,253]
N = 8
BF = ml_dtypes.bfloat16
def gentries(a):
    return np.ascontiguousarray(a.reshape(8, 16, -1).transpose(0, 2, 1)).reshape(8, -1)
def gtable(e):
    e = np.asarray(e); return np.ascontiguousarray(e.reshape(8, -1, 16).transpose(0, 2, 1)).reshape(128, -1).astype(np.int32)
W, S, M, K, R, D = 3072, 3, 1024, 832, 3, 2
def places(rng):
    o = np.argsort(rng.random((N, 8, W)), axis=-1)[..., :2 * K]
    return np.array(o[..., :K]), np.array(o[..., K:])
def keys(rng):
    x = np.array(np.argsort(rng.random((N, 8, M)), axis=-1)[..., :K]).astype(np.int64)
    o = 2 * rng.integers(0, M // 2, (N, 8, 1)) + 1; e = rng.integers(0, M // 2, (N, 8, 1)); f = rng.integers(0, M // 2, (N, 8, 1))
    return (o + 2 * e * x + 2 * f * x * x) & (M - 1), x
def pack(m, th, A, B, a, b):
    return {"mk": np.ascontiguousarray(m.reshape(N, 128, W)).astype(np.float32).astype(BF), "th": np.ascontiguousarray(np.repeat(th, 16, axis=1).reshape(N, 128, 1)).astype(np.int32),
            "la": np.stack([gtable(v) for v in A]), "lb": np.stack([gtable(v) for v in B]), "ka": np.stack([gtable(v) for v in a]), "kb": np.stack([gtable(v) for v in b])}
def setup_inputs(rng):
    A, B = places(rng); a, b = keys(rng)
    return pack(rng.integers(0, 16, (N, 8, 16, W)), rng.integers(112, 160, (N, 8)), A, B, a, b)
def far(rng, back):
    G = max(g for g in range(1, W - 2 * K + 1) if g + max(0, (g - 1 + S // 2) // S - (M - K)) <= W - 2 * K)
    h = (G - 1 + S // 2) // S; mv = max(0, h - (M - K))
    x = int(rng.integers(1, K // 2))
    while ((W - 1 - S // 2 if back else 0) - (K - mv + x + G - 2)) % S: x += 1
    u = K - 1 - mv + x; base = u + G + K - x; e = u + G - 1; e = W - 1 - e if back else e; c = e // S
    near = c + np.arange(1, h + 1) * (1 if back else -1); rest = np.setdiff1d(np.arange(M), np.append(near, c))
    o = [rng.permutation(K) for q in range(N)]
    s = np.stack([np.concatenate([np.array([c]), rng.permutation(near)[:mv], rng.permutation(rest)[:K - 1 - mv]])[o[q]] for q in range(N)])
    A, B = np.zeros((N, K), np.int64), np.zeros((N, K), np.int64)
    for r in range(N):
        P = np.concatenate([np.array([u - 1]), base + 2 + 2 * np.arange(mv), rng.permutation(np.append(np.arange(x, u - 1), base))])
        Q = rng.permutation(np.concatenate([np.arange(x), u + G + np.arange(K - x)]))
        if back: A[r], B[r] = W - 1 - Q, W - 1 - P[o[(r - D) % N]]
        else: A[r], B[r] = P[o[r]], Q
    return A, B, s
def setup_inputs_full(rng):
    A, B = places(rng); a, b = keys(rng); th = np.full((N, 8), 241); lone = []
    for q in range(N):
        for g in range(6):
            k = (g + q) & 7; o = rng.permutation(2 * K)
            if k == 0:
                i = int(np.argmax(o)); o[i], o[K] = int(o[K]), int(o[i]); A[q, g], B[q, g] = o[:K], o[K:]
            elif k == 1:
                i = int(np.argmin(o)); o[i], o[0] = int(o[0]), int(o[i]); A[q, g], B[q, g] = W - 2 * K + o[:K], W - 2 * K + o[K:]
            elif k == 2:
                A[q, g] = rng.permutation(K); B[q, g] = W - K + rng.permutation(K)
            elif k == 3:
                A[q, g] = W - K + rng.permutation(K); B[q, g] = rng.permutation(K); j = int(rng.integers(0, 16))
                if q % 3 < 2: th[q, g] = 240; lone.append((q, g, K + j if q % 3 == 0 else W - 1 - K - j))
            elif k == 4:
                A[q, g] = S * rng.permutation(M)[:K]; B[q, g] = S * rng.permutation(M)[:K] + S // 2
            elif k == 5:
                A[q, g] = 2 * rng.permutation(K); B[q, g] = 2 * rng.permutation(K) + 1; th[q, g] = rng.integers(112, 160)
            else:
                p = 1 + rng.permutation(W - 2)[:2 * K]; A[q, g], B[q, g] = p[:K], p[K:]; i = rng.integers(0, K); j = rng.integers(0, K)
                A[q, g, i] = (W - 1, 0)[k - 6]; B[q, g, j] = (0, W - 1)[k - 6]
    for g in (6, 7):
        A[:, g], B[:, g], s = far(rng, g == 7)
        a[:, g] = 2 * rng.integers(0, M // 2, (N, 1)) + 1; b[:, g] = (s - 2 * a[:, g]) & (M - 1)
    m = rng.integers(0, 16, (N, 8, 16, W))
    m = np.where((rng.random((N, 8, 1, W)) < 0.25) & (th[:, :, None, None] == 241), 15, m)
    for q, g, w in lone: m[q, g, :, w] = 15
    return pack(m, th, A, B, a, b)
def setup_inputs_sites(rng):
    A, B = places(rng); a, b = keys(rng); th = np.tile(np.array([130, 1, 1, 1, 1, 240, 1, 1]), (N, 1)); t = np.arange(K)
    a[:, 0] = 1; b[:, 0] = t; a[:, 1] = M - 1; b[:, 1] = M - 1 - t
    a[:, 4] = 2 * rng.integers(0, M // 2, (N, 1)) + 1
    F = 1 << ((W - 1).bit_length() - 1); L = W - F
    f1 = rng.permutation(np.arange(-(-F // S), (F + L // 2 - 8) // S, 2))[:16]; f2 = rng.permutation(np.arange(L // 2 // S + 8, (L - 16) // S, 2))[:16]
    pl = np.concatenate([f1, f2]); n = len(pl); rest = np.setdiff1d(np.arange(M), pl); o4 = [rng.permutation(K) for q in range(N)]
    pa = np.concatenate([S * f1 - F, S * f2 - 1]); pb = np.concatenate([S * f1 + S // 2 + 1, S * f2 + S // 2 + F])
    other = np.setdiff1d(np.arange(W), np.concatenate([pa, pb, S * pl, S * pl + S // 2]))
    for q in range(N):
        b[q, 4] = (np.concatenate([pl, rng.permutation(rest)[:K - n]])[o4[q]] - 2 * a[q, 4]) & (M - 1)
        w = rng.permutation(other)
        A[q, 4] = np.concatenate([pa, w[:K - n]])[o4[q]]; B[q, 4] = np.concatenate([pb, w[K - n:2 * (K - n)]])[o4[(q - D) % N]]
    lim = 3 * (M - K) // 2; v = np.arange(M); v = v[(v % 3 == 1) | (v >= lim)]
    a[:, 5] = 3 * (2 * rng.integers(0, 4, (N, 1)) + 1); b[:, 5] = (np.stack([rng.permutation(v) for q in range(N)]) - 2 * a[:, 5]) & (M - 1)
    s = (a * 2 + b) & (M - 1); z = np.roll(s, D, axis=0)
    A[:, 2] = S * s[:, 2]; B[:, 2] = S * z[:, 2] + S // 2
    A[:, 3] = S * np.roll(s[:, 3], -1, axis=-1); B[:, 3] = S * np.roll(z[:, 3], -1, axis=-1) + S // 2
    s5, z5 = s[:, 5], z[:, 5]; go = (s5 % 3 == 1) & ((s5 < lim) | (S > 2)); kind = rng.integers(0, 3, (N, K))
    ga = (go & (kind != 2)).astype(np.int64); gb = np.roll(go & (kind != 1), D, axis=0).astype(np.int64)
    A[:, 5] = np.where(s5 % 3 == 2, S * s5 + S // 2, S * s5 - ga); B[:, 5] = np.where(z5 % 3 == 2, S * z5, S * z5 + S // 2 + gb)
    for q in range(N):
        for g in (6, 7):
            w = rng.random(W); w[S * s[q, g]] += 8 - g; w[S * z[q, g] + S // 2] += g - 5
            o = rng.permutation(np.argsort(w)[:2 * K]); A[q, g], B[q, g] = o[:K], o[K:]
    m = rng.integers(0, 16, (N, 8, 16, W)); m[:, 5] = np.where(taken(A, B)[:, 5][:, None, :], m[:, 5], 15)
    return pack(m, th, A, B, a, b)
def setup_inputs_spread(rng):
    A, B = places(rng); a, b = keys(rng)
    m = np.floor(rng.random((N, 8, 16, W)) * (rng.integers(0, 16, (N, 8, 1, W)) + 1)).astype(np.int64)
    return pack(m, rng.integers(1, 242, (N, 8)), A, B, a, b)
def setup_inputs_stall(rng):
    A, B = places(rng); a, b = keys(rng); th = np.full((N, 8), 1); th[((np.arange(N) // np.gcd(D, N)) & 1) == 1, 1::2] = 241
    m = rng.integers(0, 16, (N, 8, 16, W)) * (rng.random((N, 8, 1, W)) > 0.125)
    return pack(m, th, A, B, a, b)
def setup_inputs_ties(rng):
    A, B = places(rng); a, b = keys(rng); th = rng.integers(20, 220, (N, 8))
    T = th[:, :, None] + rng.choice(np.array([-2, -1, -1, -1, 0, 1]), (N, 8, W)); q = T // 16
    m = q[:, :, None, :] + (np.argsort(rng.random((N, 8, 16, W), dtype=np.float32), axis=2) < (T - 16 * q)[:, :, None, :])
    lo, hi = m[:, :, :8], m[:, :, 8:]; d = np.floor(rng.random(lo.shape) * (np.minimum(lo, 15 - hi) + 1)).astype(np.int64)
    return pack(np.concatenate([lo - d, hi + d], axis=2), th, A, B, a, b)
def check_inputs(d):
    bad = []
    x = d["mk"].astype(np.float32)
    if not np.all((x >= 0) & (x <= 15) & (x == np.floor(x))): bad.append("marks")
    for k, lo, hi in (("th", 1, 241), ("la", 0, W - 1), ("lb", 0, W - 1), ("ka", 1, M - 1), ("kb", 0, M - 1)):
        if np.min(d[k]) < lo or np.max(d[k]) > hi: bad.append("range of " + k)
    h = d["th"].reshape(N, 8, 16)
    if np.any(h != h[:, :, :1]): bad.append("th alike in a group")
    if np.any((d["ka"] & 1) == 0): bad.append("odd keys")
    A, B, a, b = [np.stack([gentries(v) for v in d[k]]).astype(np.int64) for k in ("la", "lb", "ka", "kb")]
    if np.any(np.diff(np.sort(np.concatenate([A, B], axis=2), axis=-1), axis=-1) == 0): bad.append("different places")
    for c in range(2, R + 1):
        if np.any(np.diff(np.sort((a * c + b) & (M - 1), axis=-1), axis=-1) == 0): bad.append("different sites in step " + str(c))
    return bad
def taken(A, B):
    o = np.zeros((N, 8, W), bool)
    np.put_along_axis(o, A, True, 2); np.put_along_axis(o, B, True, 2)
    return o
def reference(mk, th, la, lb, ka, kb):
    m = mk.astype(np.float32).astype(np.int64).reshape(N, 8, 16, W); t = th.astype(np.int64).reshape(N, 8, 16)[:, :, :1]
    A, B, a, b = [np.stack([gentries(v) for v in w]).astype(np.int64) for w in (la, lb, ka, kb)]
    at = np.arange(W); still = np.zeros((N, 8, K), bool)
    for c in range(1, R + 1):
        A0, B0 = A, B; held = taken(A, B)
        s = (a * c + b) & (M - 1); sa = S * s; sb = S * np.roll(s, D, axis=0) + S // 2
        A = np.where(still & ~np.take_along_axis(held, sa, 2), sa, A)
        B = np.where(np.roll(still, D, axis=0) & ~np.take_along_axis(held, sb, 2), sb, B)
        bar = np.add.reduce(m, axis=2) >= t
        up = np.maximum.accumulate(np.where(bar | taken(A, B), at + 1, 0), axis=2)
        up = np.concatenate([np.zeros((N, 8, 1), np.int64), up[..., :-1]], axis=2)
        A = np.take_along_axis(up, A, 2)
        dn = np.minimum.accumulate(np.where(bar | taken(A, B), at - 1, W - 1)[..., ::-1], axis=2)[..., ::-1]
        dn = np.concatenate([dn[..., 1:], np.full((N, 8, 1), W - 1)], axis=2)
        B = np.take_along_axis(dn, B, 2)
        ia, ib = A[:, :, None, :], B[:, :, None, :]
        va = np.take_along_axis(m, ia, 3); vb = np.take_along_axis(m, ib, 3)
        np.put_along_axis(m, ia, (va + np.roll(vb, -D, axis=0) + 1) & 15, 3)
        np.put_along_axis(m, ib, (vb + np.roll(va, D, axis=0) + 1) & 15, 3)
        still = (A == A0) & np.roll(B == B0, -D, axis=0)
    return {"ym": m.reshape(N, 128, W).astype(np.float32).astype(BF), "ya": np.stack([gtable(v) for v in A]).astype(np.float32), "yb": np.stack([gtable(v) for v in B]).astype(np.float32)}

@@ -1,0 +1,629 @@
+from concourse.bass import DstId, RemoteDMATransfer
+from concourse.mybir import AluOpType, AxisListType, ActivationFunctionType
+
+W, K, KC, Q = 3072, 832, 52, 192
+NL = 2 * K
+HB = 416
+F0 = NL + 1
+OFF = 64.0
+BIG = 2.0 ** 24
+FW = (48.0, 16.0)
+
+SCRATCH = {}
+
+
+def _b(names, cols, d="float32", where="sbuf"):
+    for x in names.split():
+        SCRATCH[x] = (where, [128, cols], d)
+
+
+_b("TT", W + 3 * NL, "bfloat16")
+_b("ZF", 3344, "bfloat16")
+_b("WW", W, "int32")
+_b("W1 W2", W)
+_b("W3", 2048)
+_b("GG YY", W, "bfloat16")
+_b("LG", K, "float16")
+_b("FG", NL, "bfloat16")
+_b("UU0 UU1 XO1 XO2 XO3 XI1 XI2 XI3 YO1 YO2 YO3 YI1 YI2 YI3", K, "bfloat16")
+_b("SO1 SO2 SI1 SI2", 2 * KC, "bfloat16")
+_b("VAL", K)
+_b("E2", 2048, "bfloat16")
+_b("INI", 208, "int32")
+_b("THI COLI", 4, "int32")
+_b("COL M16", 16)
+_b("ONE BD1 BD NBD ID IB NI N8", 128, "bfloat16")
+_b("ZB", 144, "bfloat16")
+_b("ZH", 144, "float16")
+_b("KEEP", 32)
+_b("WK VB NB", 194)
+_b("THB BF BG HH", Q, "bfloat16")
+_b("XX X2", 418)
+_b("Y1 Y2", 96)
+_b("Z1 Z2 U1 U2", 64)
+_b("ZERO AA XM IL IR T1 T2 T3 RL RR IE JID PP CJ2 CJ3 DL DR", Q)
+_b("KI", Q, "int32")
+_b("KH KP", 2 * Q, "int32")
+_b("PK2", 3 * Q, "bfloat16")
+_b("J16", Q, "uint16")
+_b("S16 P16 C16", 104, "uint16")
+_b("ST16", 208, "uint16")
+_b("STF", 208)
+_b("SS1 SS2 SS3 LI LP SI32", 104, "int32")
+_b("L1 DS KO KN MV", 104)
+_b("SB", 104, "bfloat16")
+_b("IVR IVO IVN", 128)
+_b("IVI", 128, "int32")
+BANKS = ("PA0", "PA1", "PB0", "PB1", "PC", "PE", "PX", "PD")
+_b(" ".join(BANKS), 512, "float32", "psum")
+
+NDMA = 48
+SEMAPHORES = ["qv", "qa", "qt", "qg", "sent"] + ["d%d" % i for i in range(NDMA)] + \
+    ["rk", "ri2", "ri3", "ra1", "ra2", "rx1", "rx2", "rx3", "ry1", "ry2", "ry3", "rs1", "rs2"]
+
+A = AluOpType
+AF = ActivationFunctionType
+
+
+def rank_program(g, core, T, topo):
+    rank = T.rank_of(core)
+    if rank is None:
+        return
+    n = len(T.cores)
+    up, down = T.cores[(rank + 2) % n], T.cores[(rank - 2) % n]
+    eng = {"v": g.vector, "a": g.scalar, "t": g.tensor, "g": g, "s": g.sync}
+    qsem = {"v": "qv", "a": "qa", "t": "qt", "g": "qg"}
+    count = {s: 0 for s in SEMAPHORES}
+    known = {q: {} for q in eng}
+    writer, readers = {}, {}
+    ndma = [0]
+
+    def need(q, ev):
+        sem, val, src, snap = ev
+        if known[q].get(sem, 0) >= val or (q == "t" and src == "t"):
+            return
+        eng[q].wait_ge(T.sem[sem], val)
+        for s, x in snap.items():
+            if known[q].get(s, 0) < x:
+                known[q][s] = x
+        known[q][sem] = val
+
+    def sync(q, r, w):
+        evs = []
+        for k in r:
+            if k in writer:
+                evs.append(writer[k])
+            if k in BANKS:
+                evs += [ev for ev in readers.get(k, []) if ev[2] != q]
+        for k in w:
+            if k in writer:
+                evs.append(writer[k])
+            evs += readers.get(k, [])
+        evs.sort(key=lambda ev: -ev[1])
+        for ev in evs:
+            need(q, ev)
+
+    def done(ev, r, w):
+        for k in r:
+            readers.setdefault(k, []).append(ev)
+        for k in w:
+            writer[k] = ev
+            readers[k] = []
+
+    def op(q, fn, r, w):
+        r, w = r.split(), w.split()
+        sync(q, r, w)
+        ins = fn()
+        s = qsem[q]
+        count[s] += 1
+        ins.then_inc(T.sem[s], 1)
+        done((s, count[s], q, dict(known[q])), r, w)
+
+    def dma(q, out, in_, r, w):
+        r, w = r.split(), w.split()
+        sync(q, r, w)
+        s = "d%d" % ndma[0]
+        ndma[0] += 1
+        eng[q].dma_start(out, in_).then_inc(T.sem[s], 16)
+        count[s] = 16
+        done((s, 16, "dma", dict(known[q])), r, w)
+
+    def send(dst, src, out, in_, sem, r, key):
+        sync("g", r.split(), [])
+        rid, pid = topo.addr(dst, core)
+        g.remote_dma(out, in_, T.sem[sem], T.sem["sent"], pid, rid, topo.mask(core, dst))
+        count["sent"] += len(topo.engines(core, dst))
+        count[sem] = len(topo.engines(src, core))
+        writer[key] = (sem, count[sem], "dma", {})
+        readers[key] = []
+
+    def mms(lst, r, w):
+        def fn():
+            for x in lst:
+                ins = g.tensor.matmul(*x)
+            return ins
+        op("t", fn, r, w)
+
+    def ts(out, in0, s1, s2, o0, o1, r, w):
+        op("v", lambda: g.vector.tensor_scalar(out, in0, s1, s2, o0, o1), r, w)
+
+    def t1(out, in0, s1, o0, r, w):
+        op("v", lambda: g.vector.tensor_scalar(out, in0, s1, None, o0), r, w)
+
+    def tt(out, in0, in1, o, r, w):
+        op("v", lambda: g.vector.tensor_tensor(out, in0, in1, o), r, w)
+
+    def cp(out, in_, r, w):
+        op("v", lambda: g.vector.tensor_copy(out, in_), r, w)
+
+    def ms(ap, val, w):
+        op("v", lambda: g.vector.memset(ap, val), "", w)
+
+    def scan(out, d0, d1, init, o0, o1, r, w):
+        op("v", lambda: g.vector.tensor_tensor_scan(out, d0, d1, init, o0, o1), r, w)
+
+    def red(out, in_, o, r, w):
+        op("v", lambda: g.vector.tensor_reduce(out, in_, AxisListType.X, o), r, w)
+
+    def tr(out, in_, r, w):
+        op("v", lambda: g.vector.transpose(out, in_), r, w)
+
+    def act(out, in_, f, r, w, **kw):
+        op("a", lambda: g.scalar.activation(out, in_, f, **kw), r, w)
+
+    def iota(out, pat, base, cm, w, **kw):
+        op("g", lambda: g.iota(out, pat, base, cm, **kw), "", w)
+
+    def sel(out, in_, pat, o, base, cm, r, w):
+        op("g", lambda: g.affine_select(out, in_, pat, o, 0.0, base, cm), r, w)
+
+    def col(j):
+        return T.COL[:, j:j + 1]
+    cI, cI192, cNF, cNL, cT2, cT3, cTH, cCL, cCR, cWL, cWR, cFb, cCE, cFa, cT1 = range(15)
+    cF, cL = T.M16[:, 0:1], T.M16[:, 15:16]
+
+    def E(b):
+        return T.ZB[:, 15 - b:143 - b]
+
+    def EH(b):
+        return T.ZH[:, 15 - b:143 - b]
+
+    small = dict(allow_small_or_imprecise_dtypes=True)
+    dma("s", T.INI[:, 52:104], T.lb[:], "", "INb")
+    dma("a", T.INI[:, 0:52], T.la[:], "", "INa")
+    ms(T.ZERO[:], 0.0, "ZERO")
+    iota(T.VAL[:], [[1, K]], int(OFF) + 1, 0, "VAL", **small)
+    dma("s", T.W2[0::16, :], T.ZERO[:], "ZERO", "W2")
+    dma("a", T.W1[0::16, :], T.ZERO[:], "ZERO", "W1")
+    dma("a", T.THI[:, 0:1], T.th[:], "", "THI")
+    dma("a", T.INI[:, 104:156], T.ka[:], "", "INc")
+    dma("s", T.INI[:, 156:208], T.kb[:], "", "INd")
+    dma("s", T.W3[0::16, :], T.ZERO[:, 0:128], "ZERO", "W3")
+    dma("s", T.TT[:, 0:W // 2], T.mk[:, 0:W // 2], "", "M0a")
+    dma("s", T.TT[:, W // 2:W], T.mk[:, W // 2:W], "", "M0b")
+    ms(T.ONE[:], 1.0, "ONE")
+    ms(T.ZB[:], 0.0, "ZB")
+    ms(T.ZH[:], 0.0, "ZH")
+    ms(T.XX[:], 0.0, "XK XK0 XN XR XR1")
+    ms(T.X2[:], 0.0, "X2F X2N X2R")
+    ms(T.Z1[:], 0.0, "Z1a Z1b")
+    ms(T.Z2[:], 0.0, "Z2a Z2b")
+    ms(T.KEEP[:], 1.0, "KEEP")
+    ms(T.ZF[:, NL:NL + 1], 0.0, "ZF0")
+    ms(T.KEEP[:, 15:16], 0.0, "KEEP")
+    WWK = "WW0 WW1 "
+    GGK = "GG0 GG1 GG2 GG3 "
+    iota(T.COLI[:, 0:1], [[0, 1]], 0, 1, "COLI0")
+    iota(T.M16[:], [[1, 16]], 0, 0, "M16", **small)
+    sel(T.BD1[:], T.ONE[:], [[-16, 8], [0, 16]], A.is_ge, 0, 1, "ONE", "BD1")
+    sel(T.ID[:], T.ONE[:], [[-1, 128]], A.is_equal, 0, 1, "ONE", "ID")
+    sel(T.BD[:], T.BD1[:], [[16, 8], [0, 16]], A.is_ge, 15, -1, "BD1", "BD")
+    iota(T.WK[:], [[4096, 194]], -4096, 0, "WK", **small)
+    iota(T.WW[:], [[0, W]], 0, 0, WWK)
+    cp(T.S16[:, 52:104], T.INI[:, 52:104], "INb", "S16b")
+    act(T.W2[:, :].indirect(T.S16[:, 52:104]), T.VAL[:], AF.Silu, "VAL S16b", "W2")
+    cp(T.S16[:, 0:52], T.INI[:, 0:52], "INa", "S16a")
+    cp(T.W1[:, :].indirect(T.S16[:, 0:52]), T.VAL[:], "VAL S16a", "W1")
+    dma("s", T.DL[:], T.W1[0::16, :], "W1", "DL")
+    dma("s", T.DR[:], T.W2[0::16, :], "W2", "DR")
+    dma("s", T.GG[:], T.mk[:], "", GGK)
+    ts(col(cT1), T.THI[:, 0:1], -1.0, 1.0, A.mult, A.add, "THI", "cT1")
+    t1(T.ZB[:, 15:143:16], T.BD[:, 0::16], BIG, A.mult, "BD", "ZB")
+    t1(T.IB[:], T.ID[:], BIG, A.mult, "ID", "IB")
+    t1(T.THB[:], T.ZERO[:], col(cT1), A.add, "ZERO cT1", "THB")
+    mms([(T.PC[:, 0:Q], T.IB[:], T.THB[:], True, False)] +
+        [(T.PC[:, 0:Q], E(b), T.TT[:, Q * b:Q * (b + 1)], False, False) for b in range(16)], "IB ZB M0a M0b THB", "PC")
+    for o, c in ((0, 2), (52, 3)):
+        t1(T.L1[:, o:o + 52], T.INI[:, 104:156], float(c), A.mult, "INc", "L1" + "ab"[c - 2])
+    for o, c in ((0, 2), (52, 3)):
+        tt(T.LI[:, o:o + 52], T.L1[:, o:o + 52], T.INI[:, 156:208], A.add, "INd L1" + "ab"[c - 2], "LI" + "ab"[c - 2])
+    t1(T.COLI[:, 1:2], T.COLI[:, 0:1], 15, A.bitwise_and, "COLI0", "COLI1")
+    t1(T.SI32[:], T.LI[:], 1023, A.bitwise_and, "LIa LIb", "SI32")
+    cp(col(cI), T.COLI[:, 1:2], "COLI1", "cI")
+    cp(T.C16[:], T.SI32[:], "SI32", "C16")
+    act(T.W3[:, 0:1024].indirect(T.C16[:, 0:52]), T.VAL[:], AF.Silu, "VAL C16", "W3")
+    dma("a", T.IVR[:, 0:64], T.W3[0::16, 0:1024], "W3", "IVR2")
+    t1(T.M16[:], T.M16[:], col(cI), A.is_equal, "M16 cI", "M16")
+    t1(col(cI192), T.COLI[:, 1:2], 192.0 * 4096, A.mult, "COLI1", "cI192")
+    t1(T.KO[:], T.SI32[:], 3.0, A.mult, "SI32", "KO")
+    send(up, down, T.KN[:], T.KO[:], "rk", "KO", "KN")
+    ts(col(cT2), col(cT1), 249.0, BIG, A.add, A.mult, "cT1", "cT2")
+    ts(col(cT3), col(cT1), 759.0, BIG, A.add, A.mult, "cT1", "cT3")
+    t1(col(cTH), col(cT1), -1.0, A.mult, "cT1", "cTH")
+    t1(T.WK[:], T.WK[:], col(cI192), A.add, "WK cI192", "WK")
+    cp(T.ZH[:, 15:143:16], T.BD[:, 0::16], "BD", "ZH")
+    ts(col(cNF), cF, -1.0, 1.0, A.mult, A.add, "M16", "cNF")
+    ts(col(cNL), cL, -1.0, 1.0, A.mult, A.add, "M16", "cNL")
+    cp(T.VB[:], T.WK[:], "WK", "VB VB0 VB1")
+    cp(T.NB[:, 0:1], col(cNF), "cNF", "NB0")
+    cp(T.NB[:, 193:194], col(cNL), "cNL", "NB1")
+
+    def ends():
+        t1(T.XX[:, 0:1], T.VB[:, 1:2], cF, A.mult, "VB M16", "XK0")
+        t1(col(cCE), T.VB[:, 192:193], cL, A.mult, "VB M16", "cCE")
+    ends()
+    ts(T.BF[:], T.DL[:], 1.0, 16 * FW[0], A.is_ge, A.mult, "DL", "BF")
+    mms([(T.PC[:, 0:Q], T.IB[:], T.BF[:], False, False)], "BF", "PC")
+    ts(T.T2[:], T.DL[:], OFF, 0.0, A.subtract, A.max, "DL", "T2")
+    ts(col(cWL), T.M16[:, 1:2], 2.0 ** -12, cF, A.mult, A.add, "M16", "cWL")
+    t1(col(cWR), col(cI), 2.5, A.is_lt, "cI", "cWR")
+    ts(col(cCL), T.M16[:, 1:2], 128.0, 1536.0, A.mult, A.add, "M16", "cCL")
+    t1(col(cCR), col(cI), 1.5, A.is_lt, "cI", "cCR")
+    t1(col(cFa), cF, FW[0], A.mult, "M16", "cFa")
+    t1(col(cFb), cF, FW[1], A.mult, "M16", "cFb")
+    ts(T.BG[:], T.DR[:], 1.0, 16 * FW[1], A.is_ge, A.mult, "DR", "BG")
+    mms([(T.PC[:, 0:Q], T.IB[:], T.BG[:], False, True)], "BG", "PC")
+
+    def numbers():
+        ts(T.KP[:, 0:Q], T.DR[:], OFF, 0.0, A.subtract, A.max, "DR", "KPa")
+        ts(T.PX[:, Q:2 * Q], T.DR[:], 1.0, float(K), A.is_ge, A.mult, "DR", "PX")
+        tt(T.PC[:, Q:2 * Q], T.PX[:, Q:2 * Q], T.KP[:, 0:Q], A.add, "PX KPa", "PC")
+        tt(T.JID[:], T.PC[:, Q:2 * Q], T.T2[:], A.add, "PC T2", "JID")
+
+    act(T.N8[:], T.ID[:], AF.Copy, "ID", "N8", scale=-8.0)
+    act(T.NI[:], T.ID[:], AF.Copy, "ID", "NI", scale=-1.0)
+    act(T.NBD[:], T.BD[:], AF.Copy, "BD", "NBD", scale=-1.0)
+    for b in range(16):
+        act(T.E2[:, 128 * b:128 * (b + 1)], T.BD[:], AF.Copy, "BD M16", "E2%d" % b, scale=T.M16[:, b:b + 1])
+    E2K = " ".join("E2%d" % b for b in range(16))
+
+    def candidates(c):
+        sl = slice(64 * c - 128, 64 * c - 64)
+        ts(T.IVI[:, sl], T.IVR[:, sl], OFF, 0.0, A.subtract, A.max, "IVR%d" % c, "IVI")
+        cp(T.IVO[:, sl], T.IVI[:, sl], "IVI", "IVO%d" % c)
+        send(up, down, T.IVN[:, sl], T.IVO[:, sl], "ri%d" % c, "IVO%d" % c, "IVN%d" % c)
+
+    def candidates2():
+        for o in (0, 52):
+            cp(T.STF[:, 2 * o:2 * o + 52], T.KO[:, o:o + 52], "KO", "STa%d" % o)
+            t1(T.STF[:, 2 * o + 52:2 * o + 104], T.KN[:, o:o + 52], 1.0, A.add, "KN", "STb%d" % o)
+        cp(T.ST16[:], T.STF[:], "STa0 STb0 STa52 STb52", "ST16")
+
+    def candidates3(c):
+        cj = T["CJ%d" % c]
+        o = (c - 2) * 64
+        ts(T.IVR[:, o:o + 64], T.IVN[:, o:o + 64], 0.5, float(K), A.is_ge, A.mult, "IVN%d" % c, "IVR%d" % c)
+        ms(cj[:, 2::3], 0.0, "CJa%d" % c)
+        cp(cj[:, 0::3], T.IVO[:, o:o + 64], "IVO%d" % c, "CJb%d" % c)
+        tt(cj[:, 1::3], T.IVR[:, o:o + 64], T.IVN[:, o:o + 64], A.add, "IVR%d IVN%d" % (c, c), "CJc%d" % c)
+
+    V, Vs, Vm = T.VB[:, 1:193], T.VB[:, 2:194], T.VB[:, 0:192]
+    C = T.PC[:, 0:Q]
+    q1, q2 = T.PC[:, Q:2 * Q], T.PE[:, Q:2 * Q]
+    nb, nbr = T.NB[:, 1:193], T.NB[:, 192:0:-1]
+    KE, RT = T.KI[:, 0:Q], T.PD[:, 256:256 + Q]
+
+    def half(s, h):
+        return ("PA%d" if s else "PB%d") % h
+
+    def clean(c):
+        for s in (0, 1):
+            for h in (0, 1):
+                a = s * K + h * HB
+                p = half(s, h)
+                mms([(T[p][:, 0:HB], T.ID[:], T.ZF[:, a:a + HB], True, False),
+                     (T[p][:, 0:HB], T.ID[:], T.ZF[:, F0 + a:F0 + a + HB], False, False),
+                     (T[p][:, 0:HB], T.NBD[:], T.FG[:, a:a + HB], False, True)],
+                    "ID NBD ZF%d%d FF%d%d FG%s" % (s, h, s, h, "ab"[s]), p)
+                o = W + (c - 1) * NL + a
+                act(T.TT[:, o:o + HB], T[p][:, 0:HB], AF.Identity, p, "Z%d%d%d" % (c, s, h), bias=-FW[s])
+
+    def reload(c):
+        so, s1 = (c - 1) * 104, "SS%da SS%db" % (c, c)
+        S1 = T["SS%d" % c]
+        tt(T.MV[:], T.PX[:, 0:104], T.SB[:], A.is_lt, "PX SBa SBb", "MV")
+        tt(T.DS[:], T.STF[:, so:so + 104], S1[:], A.subtract, s1 + " STa%d STb%d" % (so // 2, so // 2), "DS")
+        tt(T.PX[:, 128:232], T.DS[:], T.MV[:], A.mult, "DS MV", "PX")
+        tt(T.DS[:], T.PX[:, 128:232], S1[:], A.add, "PX " + s1, "DS")
+        cp(T.S16[:], T.DS[:], "DS", "S16a S16b")
+
+    for c in (1, 2, 3):
+        S0, S1 = (T.INI if c == 1 else T["SS%d" % (c - 1)]), T["SS%d" % c]
+        s0, s1 = ("IN" if c == 1 else "SS%d" % (c - 1)), "SS%d" % c
+        XO, XI, YO, YI = T["XO%d" % c], T["XI%d" % c], T["YO%d" % c], T["YI%d" % c]
+        tabk = "M0a M0b " + "".join("Z%d00 Z%d01 Z%d10 Z%d11 " % (j, j, j, j) for j in range(1, c))
+        tab = T.TT[:, 0:W + (c - 1) * NL]
+        if c == 2:
+            act(T.W3[:, 1024:2048].indirect(T.C16[:, 52:104]), T.VAL[:], AF.Silu, "VAL C16", "W3")
+            dma("a", T.IVR[:, 64:128], T.W3[0::16, 1024:2048], "W3", "IVR3")
+        tt(T.AA[:], C, Vm, A.min, "PC VB VB0", "AA")
+        ts(q2, C, col(cT3), BIG, A.is_ge, A.mult, "PC cT3", "PE")
+        t1(nb, C, 0.5, A.is_lt, "PC", "NB")
+        scan(T.XX[:, 1:193], C, Vs, T.XX[:, 0:1], A.max, A.min, "PC VB VB1 XK0", "XK")
+        tt(T.XM[:], T.AA[:], q2, A.subtract, "PE AA", "XM")
+        red(T.XX[:, 193:194], T.NB[:, 1:194], A.min, "NB NB1", "XN")
+        scan(T.XX[:, 416:224:-1], nbr, T.XM[:, ::-1], col(cCE), A.mult, A.max, "NB XM cCE", "XR")
+        tr(T.Y1[:], T.XX[:, 161:257], "XK XN XR", "Y1")
+        scan(T.Z1[:, 62:31:-1], T.Y1[:, 63:32:-1], T.Y1[:, 95:64:-1], 0.0, A.mult, A.add, "Y1", "Z1b")
+        scan(T.Z1[:, 1:32], T.Y1[:, 0:31], T.KEEP[:, 0:31], 0.0, A.max, A.mult, "Y1 KEEP", "Z1a")
+        tr(T.U1[:], T.Z1[:], "Z1a Z1b", "U1")
+        ts(T.XX[:, 417:418], T.U1[:, 32:33], col(cNL), col(cCE), A.mult, A.max, "U1 cNL cCE", "XR1")
+        t1(KE, T.XX[:, 0:192], T.U1[:, 31:32], A.max, "XK XK0 U1", "KIa")
+        cp(T.PD[:, Q:Q + 1], T.XX[:, 417:418], "XR1", "PD")
+        t1(T.KH[:, 0:Q], KE, 12, A.arith_shift_right, "KIa", "KHa")
+        dma("s", T.WW[0::16, :], T.KH[:, 0:Q], "KHa", "WW0")
+        if c > 1:
+            t1(T.KP[:, 0:Q], KE, 4095, A.bitwise_and, "KIa", "KPa")
+            dma("s", T.WW[1::16, :], T.KP[:, 0:Q], "KPa", "WW1")
+        scan(T.PD[:, Q - 1::-1], nbr, T.XM[:, ::-1], T.XX[:, 417:418], A.mult, A.max, "NB XM XR1", "PD")
+        tt(RT, T.PD[:, 1:Q + 1], V, A.max, "PD VB", "PD")
+        cp(T.PK2[:, 0:Q], RT, "PD", "PK2")
+        dma("s", T.GG[0::16, :], T.PK2[:, 0:Q], "PK2", "GG0")
+        if c == 1:
+            tt(T.PK2[:, Q:2 * Q], RT, T.PK2[:, 0:Q], A.subtract, "PD PK2", "PKb")
+            dma("s", T.GG[1::16, :], T.PK2[:, Q:2 * Q], "PKb", "GG1")
+            numbers()
+        else:
+            tt(T.PD[:, 0:Q], RT, T.PK2[:, 0:Q], A.subtract, "PD PK2", "PD")
+            cp(T.PK2[:, Q:2 * Q], T.PD[:, 0:Q], "PD", "PKb")
+            dma("s", T.GG[1::16, :], T.PK2[:, Q:2 * Q], "PKb", "GG1")
+            tt(T.PK2[:, 2 * Q:3 * Q], T.PD[:, 0:Q], T.PK2[:, Q:2 * Q], A.subtract, "PD PKb", "PKc")
+            dma("s", T.GG[2::16, :], T.PK2[:, 2 * Q:3 * Q], "PKc", "GG2")
+            clean(c - 1)
+            reload(c - 1)
+
+        def move1():
+            t1(q1, C, col(cT2), A.is_ge, "PC cT2", "PC")
+            tt(T.IL[:], q2, T.JID[:], A.min, "PE JID", "IL")
+            tt(q1, q1, T.JID[:], A.mult, "PC JID", "PC")
+            scan(T.X2[:, 415:223:-1], nbr, T.IL[:, ::-1], 0.0, A.mult, A.add, "NB IL", "X2R")
+            tt(T.IR[:], q1, T.IL[:], A.subtract, "PC IL", "IR")
+
+        def move2():
+            red(T.X2[:, 223:224], T.NB[:, 0:193], A.min, "NB NB0", "X2N")
+            scan(T.X2[:, 0:192], nb, T.IR[:], 0.0, A.mult, A.add, "NB IR", "X2F")
+            tt(q2, RT, V, A.is_equal, "PD VB", "PE")
+            tt(q1, KE, V, A.is_equal, "KIa VB", "PC")
+
+        def move3():
+            tr(T.Y2[:], T.X2[:, 160:256], "X2F X2N X2R", "Y2")
+            scan(T.Z2[:, 62:31:-1], T.Y1[:, 63:32:-1], T.Y2[:, 95:64:-1], 0.0, A.mult, A.add, "Y1 Y2", "Z2b")
+            scan(T.Z2[:, 1:32], T.Y2[:, 32:63], T.Y2[:, 0:31], 0.0, A.mult, A.add, "Y2", "Z2a")
+            tr(T.U2[:], T.Z2[:], "Z2a Z2b", "U2 U2a U2b")
+            t1(T.U2[:, 0:1], T.U2[:, 32:33], col(cNL), A.mult, "U2 cNL", "U2a")
+            t1(T.U2[:, 1:2], T.U2[:, 31:32], col(cNF), A.mult, "U2 cNF", "U2b")
+
+        def move4():
+            scan(T.RL[:, ::-1], nbr, T.IL[:, ::-1], T.U2[:, 0:1], A.mult, A.add, "NB IL U2a", "RL")
+            act(T.T1[:], T.RL[:], AF.Copy, "RL", "T1", scale=4096.0)
+            scan(T.RR[:], nb, T.IR[:], T.U2[:, 1:2], A.mult, A.add, "NB IR U2b", "RR")
+            tt(q1, q1, T.RL[:], A.mult, "PC RL", "PC")
+            tt(q2, q2, T.RR[:], A.mult, "PE RR", "PE")
+            tt(T.T2[:], q2, T.T1[:], A.subtract, "PE T1", "T2")
+            tt(T.IE[:], q1, T.T2[:], A.max, "PC T2", "IE")
+
+        def lookup(s):
+            if s:
+                act(T.UU1[:], T.GG[:, :].indirect(T.S16[:, 52:104]), AF.Copy, GGK + "S16b cWR cCR", "UU10 UU11",
+                    scale=col(cWR if c > 1 else cCR))
+                mms([(T.PA0[:, 0:52], E(b), T.UU1[:, b::16], b == 0, b == 15) for b in range(16)], "ZB UU10", "PA0")
+            else:
+                ts(T.LG[:], T.WW[:, :].indirect(T.S16[:, 0:52]), col(cCL), col(cWL) if c > 1 else cF,
+                   A.subtract, A.mult, WWK + "cCL cWL S16a", "LG")
+                mms([(T.PX[:, 0:52], EH(b), T.LG[:, b::16], b == 0, b == 15) for b in range(16)], "ZH LG", "PX")
+
+        def lists(s):
+            x = "ab"[s]
+            p = "PA0" if s else "PX"
+            sl = slice(s * 52, (s + 1) * 52)
+            if c == 1:
+                k, o = (2.0 ** -36, A.mult) if s else (1536.0, A.add)
+                t1(T.P16[:, sl], T[p][:, 0:52], k, o, p, "P16" + x)
+                t1(S1[:, sl], T[p][:, 0:52], k, o, p, s1 + x)
+            else:
+                k = (0.0, 1.0 / BIG) if s else (1536.0 + 1664.0 / 4096, 4096.0)
+                ts(T.LI[:, sl], T[p][:, 0:52], k[0], k[1], A.add, A.mult, p, "LI" + x)
+                t1(T.LP[:, sl], T.LI[:, sl], 4095, A.bitwise_and, "LI" + x, "LP" + x)
+                t1(S1[:, sl], T.LI[:, sl], 12, A.arith_shift_right, "LI" + x, s1 + x)
+                ts(T.L1[:, sl], T.LP[:, sl], 1.0, float(W - 1), A.min, A.mult, "LP" + x, "L1" + x)
+                tt(T.L1[:, sl], T.L1[:, sl], T.LP[:, sl], A.add, "L1" + x + " LP" + x, "L1" + x)
+                tt(T.L1[:, sl], T.L1[:, sl], S1[:, sl], A.max, "L1" + x + " " + s1 + x, "L1" + x)
+                cp(T.P16[:, sl], T.L1[:, sl], "L1" + x, "P16" + x)
+
+        def add(s, lhs, rhs, off, keys, start=False, stop=False):
+            for h in (0, 1):
+                p = half(s, h)
+                mms([(T[p][:, 0:HB], lhs, rhs[:, off + h * HB:off + (h + 1) * HB], start, stop)], keys[h], p)
+
+        def pair(x, key, start):
+            for h, p in ((0, "PD"), (1, "PX")):
+                mms([(T[p][:, 0:HB], T.ID[:], x[:, h * HB:(h + 1) * HB], start, not start)], key, p)
+
+        def over(s):
+            U = T["UU%d" % s]
+            ts(U[:, 0:HB], T.PD[:, 0:HB], 14.5, 2.0, A.is_ge, A.mult, "PD", "UU%d0" % s)
+            act(U[:, HB:K], T.PX[:, 0:HB], AF.Sign, "PX", "UU%d1" % s, bias=-14.5)
+
+        def fold(s):
+            add(s, T.N8[:], T["UU%d" % s], 0, ("N8 UU%d0" % s, "UU%d1" % s), stop=True)
+
+        def out(s):
+            fc = 0.0 if c == 3 else FW[s]
+            if c < 3:
+                o0, o1 = T.ZF[:, s * K:s * K + HB], T.ZF[:, s * K + HB:(s + 1) * K]
+                k0, k1 = "ZF%d0" % s, "ZF%d1" % s
+            else:
+                z = W + 2 * NL + s * K
+                o0, o1 = T.TT[:, z:z + HB], T.TT[:, z + HB:z + K]
+                k0, k1 = "Z3%d0" % s, "Z3%d1" % s
+            t1(o0, T[half(s, 0)][:, 0:HB], 1.0 + fc, A.add, half(s, 0), k0)
+            act(o1, T[half(s, 1)][:, 0:HB], AF.Identity, half(s, 1), k1, bias=fc - 7.0)
+
+        if c == 2:
+            act(T.PP[:], T.IE[:], AF.Copy, "IE", "PP")
+        if c == 1:
+            move1()
+        if c < 3:
+            candidates(c + 1)
+        lookup(0)
+        lookup(1)
+        if c > 1:
+            move1()
+        else:
+            move2()
+        lists(0)
+        act(XO[:], tab.indirect(T.P16[:, 0:52]), AF.Copy, tabk + "P16a", "XO")
+        lists(1)
+        if c < 3:
+            SO, SI = T["SO%d" % c], T["SI%d" % c]
+            tt(SO[:], S1[:], S0[:, 0:104], A.is_equal, s1 + "a " + s0 + "a " + s1 + "b " + s0 + "b", "SO")
+            sync("g", ["SO"], [])
+            trs = []
+            for s, d, src, sm in ((0, up, down, "ra%d" % c), (1, down, up, "rs%d" % c)):
+                rid, pid = topo.addr(d, core)
+                es = topo.engines(core, d)
+                es = es[s * len(es) // 2:(s + 1) * len(es) // 2]
+                trs.append(RemoteDMATransfer(dst_ids=[DstId(rid=rid, pnc=pid)], dma_engine_mask=sum(1 << e for e in es),
+                                             remote_sem=T.sem[sm], src=SO[:, 52 * s:52 * s + 52],
+                                             dst=SI[:, 52 - 52 * s:104 - 52 * s]))
+                count["sent"] += len(es)
+                count[sm] = len(topo.engines(src, core)) // 2
+                writer["SI" + "ba"[s]] = (sm, count[sm], "dma", {})
+            g.remote_dma_fused(trs, local_sem=T.sem["sent"])
+        send(up, down, XI[:], XO[:], "rx%d" % c, "XO", "XI")
+        act(YO[:], tab.indirect(T.P16[:, 52:104]), AF.Copy, tabk + "P16b", "YO")
+        send(down, up, YI[:], YO[:], "ry%d" % c, "YO", "YI")
+        add(0, T.ID[:], XO, 0, ("ID XO", "XO"), start=True)
+        add(1, T.ID[:], YO, 0, ("YO", "YO"), start=True)
+        if c > 1:
+            move2()
+        move3()
+        move4()
+
+        if c < 3:
+            so = (c - 1) * 104
+            t1(T.HH[:], T.IE[:], 0.5, A.is_ge, "IE", "HH")
+            dma("s", T.GG[0::16, :], T.HH[:], "HH", GGK)
+            act(q2, T.IE[:], AF.Relu, "IE", "PE", scale=-1.0, bias=1.0)
+
+            def still(s):
+                x, sl = "ab"[s], slice(s * 52, (s + 1) * 52)
+                tt(T.SB[:, sl], SO[:, sl], SI[:, sl], A.mult, "SO SI" + x, "SB" + x)
+                for h, p in ((0, "PD"), (1, "PX")):
+                    o = s * 52 + h * 26
+                    mms([(T[p][:, b:HB:16], T.E2[:, 128 * b:128 * (b + 1)], T.SB[:, o:o + 26], b == 0, b == 15)
+                         for b in range(16)], E2K + " SB" + x, p)
+                    fo = F0 + s * K + h * HB
+                    act(T.ZF[:, fo:fo + HB], T[p][:, 0:HB], AF.Copy, p, "FF%d%d" % (s, h), scale=FW[s])
+            still(1)
+            still(0)
+            if c == 1:
+                candidates2()
+                tt(V, T.IE[:], T.WK[:, 1:193], A.add, "IE WK", "VB")
+            else:
+                t1(q1, T.HH[:], float(NL), A.mult, "HH", "PC")
+                tt(q1, q1, T.IE[:], A.add, "PC IE", "PC")
+                tt(T.PP[:], q1, T.PP[:], A.max, "PP PC", "PP")
+                tt(V, T.PP[:], T.WK[:, 1:193], A.add, "PP WK", "VB")
+            dma("s", T.VB[1:128, 0:1], T.VB[0:127, 192:193], "VB", "VB0")
+            dma("s", T.VB[0:127, 193:194], T.VB[1:128, 1:2], "VB", "VB1")
+            candidates3(c + 1)
+            cjk = "CJa%d CJb%d CJc%d" % (c + 1, c + 1, c + 1)
+            tt(q1, q2, T["CJ%d" % (c + 1)][:], A.mult, "PE " + cjk, "PC")
+            t1(T.FG[:, 0:K], T.GG[:, :].indirect(T.ST16[:, so:so + 52]), col(cFa), A.mult, GGK + "ST16 cFa", "FGa")
+            act(T.FG[:, K:NL], T.GG[:, :].indirect(T.ST16[:, so + 52:so + 104]), AF.Copy, GGK + "ST16 cFb", "FGb",
+                scale=col(cFb))
+            add(1, T.NI[:], T.ZF, F0 + K, ("NI FF10", "FF11"))
+            pair(YO, "YO", True)
+            pair(XI, "XI", False)
+            over(1)
+            add(1, T.ID[:], XI, 0, ("XI", "XI"))
+            add(0, T.NI[:], T.ZF, F0, ("FF00", "FF01"))
+            pair(XO, "XO", True)
+            pair(YI, "YI", False)
+            tt(T.JID[:], q1, T.IE[:], A.add, "PC IE", "JID")
+            ts(q1, q2, float(F0), -1.0, A.mult, A.add, "PE", "PC")
+            ts(T.KP[:, 0:Q], C, 1.0 / BIG, col(cTH), A.mult, A.add, "PC cTH", "KPa")
+            tt(T.T3[:], q1, T.JID[:], A.add, "PC JID", "T3")
+            over(0)
+            add(1, T.BD[:], T.FG, K, ("FGb", "FGb"))
+            fold(1)
+            add(0, T.ID[:], YI, 0, ("YI", "YI"))
+            add(0, T.BD[:], T.FG, 0, ("FGa", "FGa"))
+            fold(0)
+            t1(T.KP[:, Q:2 * Q], T.KP[:, 0:Q], 255, A.bitwise_and, "KPa", "KPb")
+            cp(T.J16[:], T.T3[:], "T3", "J16")
+            out(1)
+            tt(T.BF[:], q2, T.KP[:, Q:2 * Q], A.mult, "PE KPb", "BF")
+            ends()
+            out(0)
+            ZK = "ZF00 ZF01 ZF10 ZF11 ZF0 FF00 FF01 FF10 FF11 J16"
+            win = T.ZF[:, 0:F0 + NL]
+            cp(T.GG[:, 0:1024], win.indirect(T.J16[:, 0:64]), ZK, "GG0")
+            act(T.GG[:, 2048:3072], win.indirect(T.J16[:, 128:192]), AF.Copy, ZK, "GG3")
+            cp(T.GG[:, 1024:1536], win.indirect(T.J16[:, 64:96]), ZK, "GG1")
+            act(T.GG[:, 1536:2048], win.indirect(T.J16[:, 96:128]), AF.Copy, ZK, "GG2")
+            mms([(T.PX[:, 0:104], E(b), T.FG[:, b::16], b == 0, b == 15) for b in range(16)], "ZB FGa FGb", "PX")
+            for j, ks in ((0, "GG0"), (2, "GG3"), (1, "GG1 GG2")):
+                o = T.PC[:, 64 * j:64 * j + 64]
+                mms([(o, T.IB[:], T.THB[:, 0:64], True, False), (o, T.IB[:], T.BF[:, 64 * j:64 * j + 64], False, False)] +
+                    [(o, E(b), T.GG[:, 1024 * j + b:1024 * (j + 1):16], False, b == 15) for b in range(16)],
+                    "IB BF ZB GG0 " + ks, "PC")
+        else:
+            ts(q1, T.IE[:], 0.5, float(2 * NL), A.is_ge, A.mult, "IE", "PC")
+            act(T.T3[:], T.WK[:, 1:193], AF.Copy, "WK", "T3", scale=2.0 ** -12)
+            tt(q1, q1, T.IE[:], A.add, "PC IE", "PC")
+            tt(T.PP[:], q1, T.PP[:], A.max, "PP PC", "PP")
+            ts(q2, T.PP[:], 0.5, float(W - 1), A.is_ge, A.mult, "PP", "PE")
+            tt(q2, q2, T.PP[:], A.add, "PE PP", "PE")
+            tt(T.KP[:, 0:Q], q2, T.T3[:], A.max, "PE T3", "KPa")
+            t1(T.KH[:, 0:Q], T.KP[:, 0:Q], 63, A.bitwise_and, "KPa", "KHa")
+            t1(T.KH[:, Q:2 * Q], T.KP[:, 0:Q], 8128, A.bitwise_and, "KPa", "KHb")
+            cp(T.PK2[:, 0:2 * Q], T.KH[:], "KHa KHb", "PK2 PKb")
+            dma("s", T.GG[0::16, :], T.PK2[:, 0:Q], "PK2", "GG0 GG1")
+            dma("s", T.GG[1::16, :], T.PK2[:, Q:2 * Q], "PKb", "GG2 GG3")
+            pair(YO, "YO", True)
+            pair(XI, "XI", False)
+            over(1)
+            add(1, T.ID[:], XI, 0, ("XI", "XI"))
+            fold(1)
+            pair(XO, "XO", True)
+            t1(col(cI), col(cCR), 1.0 / BIG, A.mult, "cCR", "cI")
+            t1(T.ZB[:], T.ZB[:], col(cI), A.mult, "ZB cI", "ZB")
+            out(1)
+            pair(YI, "YI", False)
+            over(0)
+            add(0, T.ID[:], YI, 0, ("YI", "YI"))
+            fold(0)
+            for j, p in enumerate(("PC", "PD", "PX")):
+                mms([(T[p][:, 0:64], E(b), T.GG[:, 1024 * j + b:1024 * (j + 1):16], b == 0, b == 15) for b in range(16)],
+                    "ZB " + GGK, p)
+            cp(T.DS[:], S1[:], s1 + "a " + s1 + "b", "DS")
+            dma("s", T.ya[:], T.DS[:, 0:52], "DS", "ya")
+            dma("s", T.yb[:], T.DS[:, 52:104], "DS", "yb")
+            out(0)
+            cp(T.J16[:, 0:64], T.PC[:, 0:64], "PC", "J0 J16")
+            for j in range(3):
+                ZK = tabk + "Z300 Z301 Z310 Z311 J%d" % j
+                a = 64 * j
+                cp(T.YY[:, 16 * a:16 * a + 512], T.TT[:, :].indirect(T.J16[:, a:a + 32]), ZK, "YY%d" % j)
+                dma("s", T.ym[:, 16 * a:16 * a + 512], T.YY[:, 16 * a:16 * a + 512], "YY%d" % j, "ym%d" % j)
+                if j < 2:
+                    p = ("PD", "PX")[j]
+                    cp(T.J16[:, a + 64:a + 128], T[p][:, 0:64], p, "J%d" % (j + 1))
+                a = a + 32
+                act(T.YY[:, 16 * a:16 * a + 512], T.TT[:, :].indirect(T.J16[:, a:a + 32]), AF.Copy, ZK, "YZ%d" % j)
+                dma("s", T.ym[:, 16 * a:16 * a + 512], T.YY[:, 16 * a:16 * a + 512], "YZ%d" % j, "yn%d" % j)
+    for s in SEMAPHORES:
+        if count[s]:
+            g.sync.wait_ge(T.sem[s], count[s])

@@ -4,10 +4,8 @@ from concourse.mybir import AluOpType, AxisListType, ActivationFunctionType
 W, K, KC, Q = 3072, 832, 52, 192
 NL = 2 * K
 HB = 416
-F0 = NL + 1
-OFF = 64.0
-BIG = 2.0 ** 24
-FW = (48.0, 16.0)
+BIG = 8192.0
+M = 4098.0
 
 SCRATCH = {}
 
@@ -17,49 +15,41 @@ def _b(names, cols, d="float32", where="sbuf"):
         SCRATCH[x] = (where, [128, cols], d)
 
 
-_b("TT", W + 3 * NL, "bfloat16")
-_b("ZF", 3344, "bfloat16")
-_b("WW", W, "int32")
-_b("W1 W2", W)
-_b("W3", 2048)
-_b("GG YY", W, "bfloat16")
+_b("TB1 TB2 TB3", W + NL, "bfloat16")
+_b("WL1 WL2 WL3 WR1 WR2 WR3 WW", W)
+_b("GG YY U8", W, "bfloat16")
 _b("LG", K, "float16")
-_b("FG", NL, "bfloat16")
-_b("UU0 UU1 XO1 XO2 XO3 XI1 XI2 XI3 YO1 YO2 YO3 YI1 YI2 YI3", K, "bfloat16")
+_b("FG UU", NL, "bfloat16")
+_b("RG XO1 XO2 XO3 XI1 XI2 XI3 YO1 YO2 YO3 YI1 YI2 YI3", K, "bfloat16")
 _b("SO1 SO2 SI1 SI2", 2 * KC, "bfloat16")
 _b("VAL", K)
-_b("E2", 2048, "bfloat16")
 _b("INI", 208, "int32")
 _b("THI COLI", 4, "int32")
-_b("COL M16", 16)
-_b("ONE BD1 BD NBD ID IB NI N8", 128, "bfloat16")
-_b("ZB", 144, "bfloat16")
-_b("ZH", 144, "float16")
-_b("KEEP", 32)
-_b("WK VB NB", 194)
-_b("THB BF BG HH", Q, "bfloat16")
-_b("XX X2", 418)
-_b("Y1 Y2", 96)
-_b("Z1 Z2 U1 U2", 64)
-_b("ZERO AA XM IL IR T1 T2 T3 RL RR IE JID PP CJ2 CJ3 DL DR", Q)
-_b("KI", Q, "int32")
-_b("KH KP", 2 * Q, "int32")
-_b("PK2", 3 * Q, "bfloat16")
+_b("COL", 16)
+_b("ONE ID IB N8", 128, "bfloat16")
+_b("BD1 BD", 8, "bfloat16")
+_b("EE", 4 * 144, "bfloat16")
+_b("EH", 144, "float16")
+_b("CL", 208, "bfloat16")
+_b("WK MK NB XM GI PR", 194)
+_b("DR", 196)
+_b("KQ", 4)
+_b("JK", 624)
+_b("Y1 Z1 U1", 64)
+_b("THB C112 HI LO HJ LJ", Q, "bfloat16")
+_b("ZERO FILL DL DH FN RL AA POS OC T1", Q)
 _b("J16", Q, "uint16")
-_b("S16 P16 C16", 104, "uint16")
+_b("S16 P16", 104, "uint16")
 _b("ST16", 208, "uint16")
 _b("STF", 208)
-_b("SS1 SS2 SS3 LI LP SI32", 104, "int32")
-_b("L1 DS KO KN MV", 104)
-_b("SB", 104, "bfloat16")
-_b("IVR IVO IVN", 128)
-_b("IVI", 128, "int32")
-BANKS = ("PA0", "PA1", "PB0", "PB1", "PC", "PE", "PX", "PD")
+_b("LI SI32", 104, "int32")
+_b("L1 KO SS1 SS2 SS3 DS G1 G2", 104)
+BANKS = ("PC", "PL", "PV", "PS", "MA", "MB", "MT", "MF")
 _b(" ".join(BANKS), 512, "float32", "psum")
 
-NDMA = 48
+NDMA = 56
 SEMAPHORES = ["qv", "qa", "qt", "qg", "sent"] + ["d%d" % i for i in range(NDMA)] + \
-    ["rk", "ri2", "ri3", "ra1", "ra2", "rx1", "rx2", "rx3", "ry1", "ry2", "ry3", "rs1", "rs2"]
+    ["rk", "ra1", "ra2", "rs1", "rs2", "rx1", "rx2", "rx3", "ry1", "ry2", "ry3"]
 
 A = AluOpType
 AF = ActivationFunctionType
@@ -75,8 +65,23 @@ def rank_program(g, core, T, topo):
     qsem = {"v": "qv", "a": "qa", "t": "qt", "g": "qg"}
     count = {s: 0 for s in SEMAPHORES}
     known = {q: {} for q in eng}
-    writer, readers = {}, {}
+    hist = {}
     ndma = [0]
+
+    def v(name, a=None, b=None, s=None, r=None):
+        cols = range(*slice(a, b, s).indices(SCRATCH[name][1][1]))
+        ap = T[name][slice(None) if r is None else slice(r, None, 16), slice(a, b, s)]
+        return (ap, [(name, min(cols), max(cols) + 1, abs(s or 1), r)])
+
+    def ind(win, off):
+        return (win[0].indirect(off[0]), win[1], off[1])
+
+    def meet(x, y):
+        if x[1] >= y[2] or y[1] >= x[2]:
+            return False
+        if x[4] is not None and y[4] is not None and x[4] != y[4]:
+            return False
+        return not (x[3] == y[3] and (x[1] - y[1]) % x[3])
 
     def need(q, ev):
         sem, val, src, snap = ev
@@ -88,542 +93,361 @@ def rank_program(g, core, T, topo):
                 known[q][s] = x
         known[q][sem] = val
 
+    def regions(outs, ins):
+        w = [x for o in outs for x in o[1]]
+        r = [x for o in ins if isinstance(o, tuple) for x in o[1]]
+        r += [x for o in list(outs) + list(ins) if isinstance(o, tuple) and len(o) > 2 for x in o[2]]
+        return r, w
+
     def sync(q, r, w):
         evs = []
-        for k in r:
-            if k in writer:
-                evs.append(writer[k])
-            if k in BANKS:
-                evs += [ev for ev in readers.get(k, []) if ev[2] != q]
-        for k in w:
-            if k in writer:
-                evs.append(writer[k])
-            evs += readers.get(k, [])
+        for xs, wr in ((r, False), (w, True)):
+            for x in xs:
+                for y, ev, yw in hist.get(x[0], []):
+                    if (x[0] in BANKS and ev[2] != q) or ((wr or yw) and meet(x, y)):
+                        evs.append(ev)
         evs.sort(key=lambda ev: -ev[1])
         for ev in evs:
             need(q, ev)
 
     def done(ev, r, w):
-        for k in r:
-            readers.setdefault(k, []).append(ev)
-        for k in w:
-            writer[k] = ev
-            readers[k] = []
+        for xs, wr in ((r, False), (w, True)):
+            for x in xs:
+                hist.setdefault(x[0], []).append((x, ev, wr))
 
-    def op(q, fn, r, w):
-        r, w = r.split(), w.split()
+    def ap(x):
+        return x[0] if isinstance(x, tuple) else x
+
+    def op(q, fn, outs, ins):
+        r, w = regions(outs, ins)
         sync(q, r, w)
-        ins = fn()
+        ins_ = fn()
         s = qsem[q]
         count[s] += 1
-        ins.then_inc(T.sem[s], 1)
+        ins_.then_inc(T.sem[s], 1)
         done((s, count[s], q, dict(known[q])), r, w)
 
-    def dma(q, out, in_, r, w):
-        r, w = r.split(), w.split()
+    def hbm(x):
+        return (x, [])
+
+    def dma(q, out, in_):
+        r, w = regions([out], [in_])
         sync(q, r, w)
         s = "d%d" % ndma[0]
         ndma[0] += 1
-        eng[q].dma_start(out, in_).then_inc(T.sem[s], 16)
+        eng[q].dma_start(out[0], in_[0]).then_inc(T.sem[s], 16)
         count[s] = 16
         done((s, 16, "dma", dict(known[q])), r, w)
 
-    def send(dst, src, out, in_, sem, r, key):
-        sync("g", r.split(), [])
-        rid, pid = topo.addr(dst, core)
-        g.remote_dma(out, in_, T.sem[sem], T.sem["sent"], pid, rid, topo.mask(core, dst))
-        count["sent"] += len(topo.engines(core, dst))
-        count[sem] = len(topo.engines(src, core))
-        writer[key] = (sem, count[sem], "dma", {})
-        readers[key] = []
+    def send(trs):
+        sync("g", [x for t in trs for x in t[3][1]], [])
+        lst = []
+        for j, (dst, src, out, in_, sem) in enumerate(trs):
+            rid, pid = topo.addr(dst, core)
+            es = topo.engines(core, dst)
+            es = es[j * len(es) // len(trs):(j + 1) * len(es) // len(trs)]
+            lst.append(RemoteDMATransfer(dst_ids=[DstId(rid=rid, pnc=pid)], dma_engine_mask=sum(1 << e for e in es),
+                                         remote_sem=T.sem[sem], src=in_[0], dst=out[0]))
+            count["sent"] += len(es)
+            count[sem] += len(topo.engines(src, core)) // len(trs)
+        g.remote_dma_fused(lst, local_sem=T.sem["sent"])
+        for dst, src, out, in_, sem in trs:
+            done((sem, count[sem], "dma", {}), [], out[1])
 
-    def mms(lst, r, w):
+    def mms(lst):
         def fn():
-            for x in lst:
-                ins = g.tensor.matmul(*x)
-            return ins
-        op("t", fn, r, w)
+            for o, l, r, st, sp in lst:
+                ins_ = g.tensor.matmul(o[0], l[0], r[0], st, sp)
+            return ins_
+        op("t", fn, [x[0] for x in lst], [x[1] for x in lst] + [x[2] for x in lst])
 
-    def ts(out, in0, s1, s2, o0, o1, r, w):
-        op("v", lambda: g.vector.tensor_scalar(out, in0, s1, s2, o0, o1), r, w)
+    def ts(out, in0, s1, s2, o0, o1):
+        op("v", lambda: g.vector.tensor_scalar(out[0], in0[0], ap(s1), ap(s2), o0, o1), [out], [in0, s1, s2])
 
-    def t1(out, in0, s1, o0, r, w):
-        op("v", lambda: g.vector.tensor_scalar(out, in0, s1, None, o0), r, w)
+    def t1(out, in0, s1, o0):
+        op("v", lambda: g.vector.tensor_scalar(out[0], in0[0], ap(s1), None, o0), [out], [in0, s1])
 
-    def tt(out, in0, in1, o, r, w):
-        op("v", lambda: g.vector.tensor_tensor(out, in0, in1, o), r, w)
+    def tt(out, in0, in1, o):
+        op("v", lambda: g.vector.tensor_tensor(out[0], in0[0], in1[0], o), [out], [in0, in1])
 
-    def cp(out, in_, r, w):
-        op("v", lambda: g.vector.tensor_copy(out, in_), r, w)
+    def cp(out, in_):
+        op("v", lambda: g.vector.tensor_copy(out[0], in_[0]), [out], [in_])
 
-    def ms(ap, val, w):
-        op("v", lambda: g.vector.memset(ap, val), "", w)
+    def ms(out, val):
+        op("v", lambda: g.vector.memset(out[0], val), [out], [])
 
-    def scan(out, d0, d1, init, o0, o1, r, w):
-        op("v", lambda: g.vector.tensor_tensor_scan(out, d0, d1, init, o0, o1), r, w)
+    def scan(out, d0, d1, init, o0, o1):
+        op("v", lambda: g.vector.tensor_tensor_scan(out[0], d0[0], d1[0], ap(init), o0, o1), [out], [d0, d1, init])
 
-    def red(out, in_, o, r, w):
-        op("v", lambda: g.vector.tensor_reduce(out, in_, AxisListType.X, o), r, w)
+    def tr(out, in_):
+        op("v", lambda: g.vector.transpose(out[0], in_[0]), [out], [in_])
 
-    def tr(out, in_, r, w):
-        op("v", lambda: g.vector.transpose(out, in_), r, w)
+    def act(out, in_, f, **kw):
+        op("a", lambda: g.scalar.activation(out[0], in_[0], f, **{k: ap(x) for k, x in kw.items()}), [out],
+           [in_] + list(kw.values()))
 
-    def act(out, in_, f, r, w, **kw):
-        op("a", lambda: g.scalar.activation(out, in_, f, **kw), r, w)
+    def iota(out, pat, base, cm, **kw):
+        op("g", lambda: g.iota(out[0], pat, base, cm, **kw), [out], [])
 
-    def iota(out, pat, base, cm, w, **kw):
-        op("g", lambda: g.iota(out, pat, base, cm, **kw), "", w)
-
-    def sel(out, in_, pat, o, base, cm, r, w):
-        op("g", lambda: g.affine_select(out, in_, pat, o, 0.0, base, cm), r, w)
+    def sel(out, in_, pat, o, base, cm):
+        op("g", lambda: g.affine_select(out[0], in_[0], pat, o, 0.0, base, cm), [out], [in_])
 
     def col(j):
-        return T.COL[:, j:j + 1]
-    cI, cI192, cNF, cNL, cT2, cT3, cTH, cCL, cCR, cWL, cWR, cFb, cCE, cFa, cT1 = range(15)
-    cF, cL = T.M16[:, 0:1], T.M16[:, 15:16]
+        return v("COL", j, j + 1)
+    cI, cI192, cF, cL, cNF1, c01, c03, c23, cT1, cX = range(10)
+    ES, E8, E01, E23 = range(4)
 
-    def E(b):
-        return T.ZB[:, 15 - b:143 - b]
-
-    def EH(b):
-        return T.ZH[:, 15 - b:143 - b]
+    def E(k, b):
+        return v("EE", 144 * k + 15 - b, 144 * k + 143 - b)
 
     small = dict(allow_small_or_imprecise_dtypes=True)
-    dma("s", T.INI[:, 52:104], T.lb[:], "", "INb")
-    dma("a", T.INI[:, 0:52], T.la[:], "", "INa")
-    ms(T.ZERO[:], 0.0, "ZERO")
-    iota(T.VAL[:], [[1, K]], int(OFF) + 1, 0, "VAL", **small)
-    dma("s", T.W2[0::16, :], T.ZERO[:], "ZERO", "W2")
-    dma("a", T.W1[0::16, :], T.ZERO[:], "ZERO", "W1")
-    dma("a", T.THI[:, 0:1], T.th[:], "", "THI")
-    dma("a", T.INI[:, 104:156], T.ka[:], "", "INc")
-    dma("s", T.INI[:, 156:208], T.kb[:], "", "INd")
-    dma("s", T.W3[0::16, :], T.ZERO[:, 0:128], "ZERO", "W3")
-    dma("s", T.TT[:, 0:W // 2], T.mk[:, 0:W // 2], "", "M0a")
-    dma("s", T.TT[:, W // 2:W], T.mk[:, W // 2:W], "", "M0b")
-    ms(T.ONE[:], 1.0, "ONE")
-    ms(T.ZB[:], 0.0, "ZB")
-    ms(T.ZH[:], 0.0, "ZH")
-    ms(T.XX[:], 0.0, "XK XK0 XN XR XR1")
-    ms(T.X2[:], 0.0, "X2F X2N X2R")
-    ms(T.Z1[:], 0.0, "Z1a Z1b")
-    ms(T.Z2[:], 0.0, "Z2a Z2b")
-    ms(T.KEEP[:], 1.0, "KEEP")
-    ms(T.ZF[:, NL:NL + 1], 0.0, "ZF0")
-    ms(T.KEEP[:, 15:16], 0.0, "KEEP")
-    WWK = "WW0 WW1 "
-    GGK = "GG0 GG1 GG2 GG3 "
-    iota(T.COLI[:, 0:1], [[0, 1]], 0, 1, "COLI0")
-    iota(T.M16[:], [[1, 16]], 0, 0, "M16", **small)
-    sel(T.BD1[:], T.ONE[:], [[-16, 8], [0, 16]], A.is_ge, 0, 1, "ONE", "BD1")
-    sel(T.ID[:], T.ONE[:], [[-1, 128]], A.is_equal, 0, 1, "ONE", "ID")
-    sel(T.BD[:], T.BD1[:], [[16, 8], [0, 16]], A.is_ge, 15, -1, "BD1", "BD")
-    iota(T.WK[:], [[4096, 194]], -4096, 0, "WK", **small)
-    iota(T.WW[:], [[0, W]], 0, 0, WWK)
-    cp(T.S16[:, 52:104], T.INI[:, 52:104], "INb", "S16b")
-    act(T.W2[:, :].indirect(T.S16[:, 52:104]), T.VAL[:], AF.Silu, "VAL S16b", "W2")
-    cp(T.S16[:, 0:52], T.INI[:, 0:52], "INa", "S16a")
-    cp(T.W1[:, :].indirect(T.S16[:, 0:52]), T.VAL[:], "VAL S16a", "W1")
-    dma("s", T.DL[:], T.W1[0::16, :], "W1", "DL")
-    dma("s", T.DR[:], T.W2[0::16, :], "W2", "DR")
-    dma("s", T.GG[:], T.mk[:], "", GGK)
-    ts(col(cT1), T.THI[:, 0:1], -1.0, 1.0, A.mult, A.add, "THI", "cT1")
-    t1(T.ZB[:, 15:143:16], T.BD[:, 0::16], BIG, A.mult, "BD", "ZB")
-    t1(T.IB[:], T.ID[:], BIG, A.mult, "ID", "IB")
-    t1(T.THB[:], T.ZERO[:], col(cT1), A.add, "ZERO cT1", "THB")
-    mms([(T.PC[:, 0:Q], T.IB[:], T.THB[:], True, False)] +
-        [(T.PC[:, 0:Q], E(b), T.TT[:, Q * b:Q * (b + 1)], False, False) for b in range(16)], "IB ZB M0a M0b THB", "PC")
-    for o, c in ((0, 2), (52, 3)):
-        t1(T.L1[:, o:o + 52], T.INI[:, 104:156], float(c), A.mult, "INc", "L1" + "ab"[c - 2])
-    for o, c in ((0, 2), (52, 3)):
-        tt(T.LI[:, o:o + 52], T.L1[:, o:o + 52], T.INI[:, 156:208], A.add, "INd L1" + "ab"[c - 2], "LI" + "ab"[c - 2])
-    t1(T.COLI[:, 1:2], T.COLI[:, 0:1], 15, A.bitwise_and, "COLI0", "COLI1")
-    t1(T.SI32[:], T.LI[:], 1023, A.bitwise_and, "LIa LIb", "SI32")
-    cp(col(cI), T.COLI[:, 1:2], "COLI1", "cI")
-    cp(T.C16[:], T.SI32[:], "SI32", "C16")
-    act(T.W3[:, 0:1024].indirect(T.C16[:, 0:52]), T.VAL[:], AF.Silu, "VAL C16", "W3")
-    dma("a", T.IVR[:, 0:64], T.W3[0::16, 0:1024], "W3", "IVR2")
-    t1(T.M16[:], T.M16[:], col(cI), A.is_equal, "M16 cI", "M16")
-    t1(col(cI192), T.COLI[:, 1:2], 192.0 * 4096, A.mult, "COLI1", "cI192")
-    t1(T.KO[:], T.SI32[:], 3.0, A.mult, "SI32", "KO")
-    send(up, down, T.KN[:], T.KO[:], "rk", "KO", "KN")
-    ts(col(cT2), col(cT1), 249.0, BIG, A.add, A.mult, "cT1", "cT2")
-    ts(col(cT3), col(cT1), 759.0, BIG, A.add, A.mult, "cT1", "cT3")
-    t1(col(cTH), col(cT1), -1.0, A.mult, "cT1", "cTH")
-    t1(T.WK[:], T.WK[:], col(cI192), A.add, "WK cI192", "WK")
-    cp(T.ZH[:, 15:143:16], T.BD[:, 0::16], "BD", "ZH")
-    ts(col(cNF), cF, -1.0, 1.0, A.mult, A.add, "M16", "cNF")
-    ts(col(cNL), cL, -1.0, 1.0, A.mult, A.add, "M16", "cNL")
-    cp(T.VB[:], T.WK[:], "WK", "VB VB0 VB1")
-    cp(T.NB[:, 0:1], col(cNF), "cNF", "NB0")
-    cp(T.NB[:, 193:194], col(cNL), "cNL", "NB1")
+    dma("s", v("INI", 52, 104), hbm(T.lb[:]))
+    dma("a", v("INI", 0, 52), hbm(T.la[:]))
+    ms(v("ZERO"), 0.0)
+    ms(v("FILL"), BIG)
+    iota(v("COLI", 0, 1), [[0, 1]], 0, 1)
+    iota(v("VAL"), [[1, K]], W + K, 0, **small)
+    dma("s", v("WR1", r=0), v("ZERO"))
+    dma("s", v("WL1", r=0), v("FILL"))
+    ms(v("ONE"), 1.0)
+    act(v("CL", 0, 52), v("ONE", 0, 52), AF.Silu, scale=1536.0)
+    dma("s", v("THI", 0, 1), hbm(T.th[:]))
+    dma("s", v("INI", 104, 156), hbm(T.ka[:]))
+    dma("s", v("INI", 156, 208), hbm(T.kb[:]))
+    dma("s", v("TB1", 0, W // 2), hbm(T.mk[:, 0:W // 2]))
+    dma("s", v("TB1", W // 2, W), hbm(T.mk[:, W // 2:W]))
+    ms(v("EE"), 0.0)
+    ms(v("EH"), 0.0)
+    ms(v("JK", 560, 624), 0.0)
+    ms(v("Z1"), 0.0)
+    ms(v("DR", 0, 4), 0.0)
+    ms(v("C112"), -112.0)
+    ms(v("CL", 52, 104), -2.0)
+    ms(v("CL", 104, 208), 0.25)
+    t1(v("COLI", 1, 2), v("COLI", 0, 1), 15, A.bitwise_and)
+    cp(col(cI), v("COLI", 1, 2))
+    t1(col(cI192), v("COLI", 1, 2), 192.0, A.mult)
+    t1(col(cF), col(cI), 0.5, A.is_lt)
+    t1(col(cL), col(cI), 14.5, A.is_ge)
+    t1(col(c01), col(cI), 1.5, A.is_lt)
+    t1(col(c03), col(cI), 3.5, A.is_lt)
+    sel(v("BD1"), v("ONE", 0, 8), [[-16, 8]], A.is_ge, 0, 1)
+    sel(v("BD"), v("BD1"), [[16, 8]], A.is_ge, 15, -1)
+    sel(v("ID"), v("ONE"), [[-1, 128]], A.is_equal, 0, 1)
+    iota(v("WK"), [[1, 194]], 1, 0, **small)
 
-    def ends():
-        t1(T.XX[:, 0:1], T.VB[:, 1:2], cF, A.mult, "VB M16", "XK0")
-        t1(col(cCE), T.VB[:, 192:193], cL, A.mult, "VB M16", "cCE")
-    ends()
-    ts(T.BF[:], T.DL[:], 1.0, 16 * FW[0], A.is_ge, A.mult, "DL", "BF")
-    mms([(T.PC[:, 0:Q], T.IB[:], T.BF[:], False, False)], "BF", "PC")
-    ts(T.T2[:], T.DL[:], OFF, 0.0, A.subtract, A.max, "DL", "T2")
-    ts(col(cWL), T.M16[:, 1:2], 2.0 ** -12, cF, A.mult, A.add, "M16", "cWL")
-    t1(col(cWR), col(cI), 2.5, A.is_lt, "cI", "cWR")
-    ts(col(cCL), T.M16[:, 1:2], 128.0, 1536.0, A.mult, A.add, "M16", "cCL")
-    t1(col(cCR), col(cI), 1.5, A.is_lt, "cI", "cCR")
-    t1(col(cFa), cF, FW[0], A.mult, "M16", "cFa")
-    t1(col(cFb), cF, FW[1], A.mult, "M16", "cFb")
-    ts(T.BG[:], T.DR[:], 1.0, 16 * FW[1], A.is_ge, A.mult, "DR", "BG")
-    mms([(T.PC[:, 0:Q], T.IB[:], T.BG[:], False, True)], "BG", "PC")
+    def scatter(c):
+        act(ind(v("WR%d" % c), v("S16", 52, 104)), v("VAL"), AF.Silu)
+        ts(ind(v("WL%d" % c), v("S16", 0, 52)), v("VAL"), -1.0, float(K), A.mult, A.add)
+        dma("s", v("DL"), v("WL%d" % c, r=0))
+        dma("s", v("DR", 4, 196), v("WR%d" % c, r=0))
 
-    def numbers():
-        ts(T.KP[:, 0:Q], T.DR[:], OFF, 0.0, A.subtract, A.max, "DR", "KPa")
-        ts(T.PX[:, Q:2 * Q], T.DR[:], 1.0, float(K), A.is_ge, A.mult, "DR", "PX")
-        tt(T.PC[:, Q:2 * Q], T.PX[:, Q:2 * Q], T.KP[:, 0:Q], A.add, "PX KPa", "PC")
-        tt(T.JID[:], T.PC[:, Q:2 * Q], T.T2[:], A.add, "PC T2", "JID")
+    cp(v("S16"), v("INI", 0, 104))
+    scatter(1)
+    act(v("EE", 144 * ES + 15, 144 * ES + 143, 16), v("BD"), AF.Copy, scale=BIG)
+    act(v("IB"), v("ID"), AF.Copy, scale=BIG)
+    ts(col(cT1), v("THI", 0, 1), -1.0, 1.0, A.mult, A.add)
+    t1(v("WK"), v("WK"), col(cI192), A.add)
+    t1(v("THB"), v("ZERO"), col(cT1), A.add)
+    ts(v("MK"), v("WK"), -1.0, M - 1, A.mult, A.add)
+    cp(v("PS", 0, 194), v("WK"))
+    ts(v("NB", 0, 1), col(cF), -1.0, 1.0, A.mult, A.add)
+    ts(v("NB", 193, 194), col(cL), -1.0, 1.0, A.mult, A.add)
+    t1(v("XM", 193, 194), col(cL), W + 1.0, A.mult)
+    tt(col(cX), v("NB", 0, 1), v("NB", 193, 194), A.mult)
+    t1(col(cNF1), col(cF), -1.0, A.mult)
+    tt(col(c23), col(c03), col(c01), A.subtract)
+    ts(v("KQ"), v("ONE", 0, 4), v("MK", 0, 1), col(cX), A.mult, A.mult)
 
-    act(T.N8[:], T.ID[:], AF.Copy, "ID", "N8", scale=-8.0)
-    act(T.NI[:], T.ID[:], AF.Copy, "ID", "NI", scale=-1.0)
-    act(T.NBD[:], T.BD[:], AF.Copy, "BD", "NBD", scale=-1.0)
-    for b in range(16):
-        act(T.E2[:, 128 * b:128 * (b + 1)], T.BD[:], AF.Copy, "BD M16", "E2%d" % b, scale=T.M16[:, b:b + 1])
-    E2K = " ".join("E2%d" % b for b in range(16))
+    def sums(tb, blocks, first, last):
+        lst = [(v("PC", 0, Q), v("IB"), v("THB"), True, False)] if first else []
+        lst += [(v("PC", 0, Q), E(ES, b), v(tb, Q * b, Q * (b + 1)), False, last and b == blocks[-1]) for b in blocks]
+        mms(lst)
+    sums("TB1", range(16), True, True)
+    act(v("WW"), v("TB1", 0, W), AF.Copy, scale=0.0)
+    ms(v("GG"), 0.0)
+    cp(v("PS", 194, 386), v("MK", 0, Q))
+    t1(v("POS"), v("WK", 0, Q), -1.0, A.add)
+    cp(v("EH", 15, 143, 16), v("BD"))
+    act(v("EE", 144 * E01 + 15, 144 * E01 + 143, 16), v("BD"), AF.Copy, scale=col(c01))
+    act(v("EE", 144 * E23 + 15, 144 * E23 + 143, 16), v("BD"), AF.Copy, scale=col(c23))
+    act(v("EE", 144 * E8 + 15, 144 * E8 + 143, 16), v("BD"), AF.Copy, scale=-8 * BIG)
+    act(v("N8"), v("ID"), AF.Copy, scale=-8.0)
+    for c in (2, 3):
+        dma("s", v("WR%d" % c, r=0), v("ZERO"))
+        dma("s", v("WL%d" % c, r=0), v("WK", 0, Q))
 
-    def candidates(c):
-        sl = slice(64 * c - 128, 64 * c - 64)
-        ts(T.IVI[:, sl], T.IVR[:, sl], OFF, 0.0, A.subtract, A.max, "IVR%d" % c, "IVI")
-        cp(T.IVO[:, sl], T.IVI[:, sl], "IVI", "IVO%d" % c)
-        send(up, down, T.IVN[:, sl], T.IVO[:, sl], "ri%d" % c, "IVO%d" % c, "IVN%d" % c)
-
-    def candidates2():
+    def sites():
+        for o, c in ((0, 2), (52, 3)):
+            t1(v("L1", o, o + 52), v("INI", 104, 156), float(c), A.mult)
         for o in (0, 52):
-            cp(T.STF[:, 2 * o:2 * o + 52], T.KO[:, o:o + 52], "KO", "STa%d" % o)
-            t1(T.STF[:, 2 * o + 52:2 * o + 104], T.KN[:, o:o + 52], 1.0, A.add, "KN", "STb%d" % o)
-        cp(T.ST16[:], T.STF[:], "STa0 STb0 STa52 STb52", "ST16")
+            tt(v("LI", o, o + 52), v("L1", o, o + 52), v("INI", 156, 208), A.add)
+        t1(v("SI32"), v("LI"), 1023, A.bitwise_and)
+        ts(v("KO"), v("SI32"), 3.0, 1.0, A.mult, A.add)
+        send([(up, down, v("STF", 2 * o + 52, 2 * o + 104), v("KO", o, o + 52), "rk") for o in (0, 52)])
+        for o in (0, 52):
+            t1(v("STF", 2 * o, 2 * o + 52), v("SI32", o, o + 52), 3.0, A.mult)
 
-    def candidates3(c):
-        cj = T["CJ%d" % c]
-        o = (c - 2) * 64
-        ts(T.IVR[:, o:o + 64], T.IVN[:, o:o + 64], 0.5, float(K), A.is_ge, A.mult, "IVN%d" % c, "IVR%d" % c)
-        ms(cj[:, 2::3], 0.0, "CJa%d" % c)
-        cp(cj[:, 0::3], T.IVO[:, o:o + 64], "IVO%d" % c, "CJb%d" % c)
-        tt(cj[:, 1::3], T.IVR[:, o:o + 64], T.IVN[:, o:o + 64], A.add, "IVR%d IVN%d" % (c, c), "CJc%d" % c)
+    C, D = v("PC", 0, Q), v("PC", Q, 2 * Q)
+    p1, p2 = v("PV", 0, Q), v("PV", Q, 2 * Q)
+    DRv = v("DR", 4, 196)
 
-    V, Vs, Vm = T.VB[:, 1:193], T.VB[:, 2:194], T.VB[:, 0:192]
-    C = T.PC[:, 0:Q]
-    q1, q2 = T.PC[:, Q:2 * Q], T.PE[:, Q:2 * Q]
-    nb, nbr = T.NB[:, 1:193], T.NB[:, 192:0:-1]
-    KE, RT = T.KI[:, 0:Q], T.PD[:, 256:256 + Q]
-
-    def half(s, h):
-        return ("PA%d" if s else "PB%d") % h
-
-    def clean(c):
-        for s in (0, 1):
-            for h in (0, 1):
-                a = s * K + h * HB
-                p = half(s, h)
-                mms([(T[p][:, 0:HB], T.ID[:], T.ZF[:, a:a + HB], True, False),
-                     (T[p][:, 0:HB], T.ID[:], T.ZF[:, F0 + a:F0 + a + HB], False, False),
-                     (T[p][:, 0:HB], T.NBD[:], T.FG[:, a:a + HB], False, True)],
-                    "ID NBD ZF%d%d FF%d%d FG%s" % (s, h, s, h, "ab"[s]), p)
-                o = W + (c - 1) * NL + a
-                act(T.TT[:, o:o + HB], T[p][:, 0:HB], AF.Identity, p, "Z%d%d%d" % (c, s, h), bias=-FW[s])
-
-    def reload(c):
-        so, s1 = (c - 1) * 104, "SS%da SS%db" % (c, c)
-        S1 = T["SS%d" % c]
-        tt(T.MV[:], T.PX[:, 0:104], T.SB[:], A.is_lt, "PX SBa SBb", "MV")
-        tt(T.DS[:], T.STF[:, so:so + 104], S1[:], A.subtract, s1 + " STa%d STb%d" % (so // 2, so // 2), "DS")
-        tt(T.PX[:, 128:232], T.DS[:], T.MV[:], A.mult, "DS MV", "PX")
-        tt(T.DS[:], T.PX[:, 128:232], S1[:], A.add, "PX " + s1, "DS")
-        cp(T.S16[:], T.DS[:], "DS", "S16a S16b")
+    def columns(tb, out, who, a, b):
+        src = ind(v(tb), v("J16", 12 * a, 12 * b))
+        if who == "v":
+            cp(v(out, Q * a, Q * b), src)
+        else:
+            act(v(out, Q * a, Q * b), src, AF.Copy)
 
     for c in (1, 2, 3):
-        S0, S1 = (T.INI if c == 1 else T["SS%d" % (c - 1)]), T["SS%d" % c]
-        s0, s1 = ("IN" if c == 1 else "SS%d" % (c - 1)), "SS%d" % c
-        XO, XI, YO, YI = T["XO%d" % c], T["XI%d" % c], T["YO%d" % c], T["YI%d" % c]
-        tabk = "M0a M0b " + "".join("Z%d00 Z%d01 Z%d10 Z%d11 " % (j, j, j, j) for j in range(1, c))
-        tab = T.TT[:, 0:W + (c - 1) * NL]
-        if c == 2:
-            act(T.W3[:, 1024:2048].indirect(T.C16[:, 52:104]), T.VAL[:], AF.Silu, "VAL C16", "W3")
-            dma("a", T.IVR[:, 64:128], T.W3[0::16, 1024:2048], "W3", "IVR3")
-        tt(T.AA[:], C, Vm, A.min, "PC VB VB0", "AA")
-        ts(q2, C, col(cT3), BIG, A.is_ge, A.mult, "PC cT3", "PE")
-        t1(nb, C, 0.5, A.is_lt, "PC", "NB")
-        scan(T.XX[:, 1:193], C, Vs, T.XX[:, 0:1], A.max, A.min, "PC VB VB1 XK0", "XK")
-        tt(T.XM[:], T.AA[:], q2, A.subtract, "PE AA", "XM")
-        red(T.XX[:, 193:194], T.NB[:, 1:194], A.min, "NB NB1", "XN")
-        scan(T.XX[:, 416:224:-1], nbr, T.XM[:, ::-1], col(cCE), A.mult, A.max, "NB XM cCE", "XR")
-        tr(T.Y1[:], T.XX[:, 161:257], "XK XN XR", "Y1")
-        scan(T.Z1[:, 62:31:-1], T.Y1[:, 63:32:-1], T.Y1[:, 95:64:-1], 0.0, A.mult, A.add, "Y1", "Z1b")
-        scan(T.Z1[:, 1:32], T.Y1[:, 0:31], T.KEEP[:, 0:31], 0.0, A.max, A.mult, "Y1 KEEP", "Z1a")
-        tr(T.U1[:], T.Z1[:], "Z1a Z1b", "U1")
-        ts(T.XX[:, 417:418], T.U1[:, 32:33], col(cNL), col(cCE), A.mult, A.max, "U1 cNL cCE", "XR1")
-        t1(KE, T.XX[:, 0:192], T.U1[:, 31:32], A.max, "XK XK0 U1", "KIa")
-        cp(T.PD[:, Q:Q + 1], T.XX[:, 417:418], "XR1", "PD")
-        t1(T.KH[:, 0:Q], KE, 12, A.arith_shift_right, "KIa", "KHa")
-        dma("s", T.WW[0::16, :], T.KH[:, 0:Q], "KHa", "WW0")
-        if c > 1:
-            t1(T.KP[:, 0:Q], KE, 4095, A.bitwise_and, "KIa", "KPa")
-            dma("s", T.WW[1::16, :], T.KP[:, 0:Q], "KPa", "WW1")
-        scan(T.PD[:, Q - 1::-1], nbr, T.XM[:, ::-1], T.XX[:, 417:418], A.mult, A.max, "NB XM XR1", "PD")
-        tt(RT, T.PD[:, 1:Q + 1], V, A.max, "PD VB", "PD")
-        cp(T.PK2[:, 0:Q], RT, "PD", "PK2")
-        dma("s", T.GG[0::16, :], T.PK2[:, 0:Q], "PK2", "GG0")
+        S0, S1 = (v("INI", 0, 104) if c == 1 else v("SS%d" % (c - 1))), v("SS%d" % c)
+        XO, XI, YO, YI = "XO%d" % c, "XI%d" % c, "YO%d" % c, "YI%d" % c
+        TB = "TB%d" % c
         if c == 1:
-            tt(T.PK2[:, Q:2 * Q], RT, T.PK2[:, 0:Q], A.subtract, "PD PK2", "PKb")
-            dma("s", T.GG[1::16, :], T.PK2[:, Q:2 * Q], "PKb", "GG1")
-            numbers()
-        else:
-            tt(T.PD[:, 0:Q], RT, T.PK2[:, 0:Q], A.subtract, "PD PK2", "PD")
-            cp(T.PK2[:, Q:2 * Q], T.PD[:, 0:Q], "PD", "PKb")
-            dma("s", T.GG[1::16, :], T.PK2[:, Q:2 * Q], "PKb", "GG1")
-            tt(T.PK2[:, 2 * Q:3 * Q], T.PD[:, 0:Q], T.PK2[:, Q:2 * Q], A.subtract, "PD PKb", "PKc")
-            dma("s", T.GG[2::16, :], T.PK2[:, 2 * Q:3 * Q], "PKc", "GG2")
-            clean(c - 1)
-            reload(c - 1)
-
-        def move1():
-            t1(q1, C, col(cT2), A.is_ge, "PC cT2", "PC")
-            tt(T.IL[:], q2, T.JID[:], A.min, "PE JID", "IL")
-            tt(q1, q1, T.JID[:], A.mult, "PC JID", "PC")
-            scan(T.X2[:, 415:223:-1], nbr, T.IL[:, ::-1], 0.0, A.mult, A.add, "NB IL", "X2R")
-            tt(T.IR[:], q1, T.IL[:], A.subtract, "PC IL", "IR")
-
-        def move2():
-            red(T.X2[:, 223:224], T.NB[:, 0:193], A.min, "NB NB0", "X2N")
-            scan(T.X2[:, 0:192], nb, T.IR[:], 0.0, A.mult, A.add, "NB IR", "X2F")
-            tt(q2, RT, V, A.is_equal, "PD VB", "PE")
-            tt(q1, KE, V, A.is_equal, "KIa VB", "PC")
-
-        def move3():
-            tr(T.Y2[:], T.X2[:, 160:256], "X2F X2N X2R", "Y2")
-            scan(T.Z2[:, 62:31:-1], T.Y1[:, 63:32:-1], T.Y2[:, 95:64:-1], 0.0, A.mult, A.add, "Y1 Y2", "Z2b")
-            scan(T.Z2[:, 1:32], T.Y2[:, 32:63], T.Y2[:, 0:31], 0.0, A.mult, A.add, "Y2", "Z2a")
-            tr(T.U2[:], T.Z2[:], "Z2a Z2b", "U2 U2a U2b")
-            t1(T.U2[:, 0:1], T.U2[:, 32:33], col(cNL), A.mult, "U2 cNL", "U2a")
-            t1(T.U2[:, 1:2], T.U2[:, 31:32], col(cNF), A.mult, "U2 cNF", "U2b")
-
-        def move4():
-            scan(T.RL[:, ::-1], nbr, T.IL[:, ::-1], T.U2[:, 0:1], A.mult, A.add, "NB IL U2a", "RL")
-            act(T.T1[:], T.RL[:], AF.Copy, "RL", "T1", scale=4096.0)
-            scan(T.RR[:], nb, T.IR[:], T.U2[:, 1:2], A.mult, A.add, "NB IR U2b", "RR")
-            tt(q1, q1, T.RL[:], A.mult, "PC RL", "PC")
-            tt(q2, q2, T.RR[:], A.mult, "PE RR", "PE")
-            tt(T.T2[:], q2, T.T1[:], A.subtract, "PE T1", "T2")
-            tt(T.IE[:], q1, T.T2[:], A.max, "PC T2", "IE")
-
-        def lookup(s):
-            if s:
-                act(T.UU1[:], T.GG[:, :].indirect(T.S16[:, 52:104]), AF.Copy, GGK + "S16b cWR cCR", "UU10 UU11",
-                    scale=col(cWR if c > 1 else cCR))
-                mms([(T.PA0[:, 0:52], E(b), T.UU1[:, b::16], b == 0, b == 15) for b in range(16)], "ZB UU10", "PA0")
-            else:
-                ts(T.LG[:], T.WW[:, :].indirect(T.S16[:, 0:52]), col(cCL), col(cWL) if c > 1 else cF,
-                   A.subtract, A.mult, WWK + "cCL cWL S16a", "LG")
-                mms([(T.PX[:, 0:52], EH(b), T.LG[:, b::16], b == 0, b == 15) for b in range(16)], "ZH LG", "PX")
-
-        def lists(s):
-            x = "ab"[s]
-            p = "PA0" if s else "PX"
-            sl = slice(s * 52, (s + 1) * 52)
-            if c == 1:
-                k, o = (2.0 ** -36, A.mult) if s else (1536.0, A.add)
-                t1(T.P16[:, sl], T[p][:, 0:52], k, o, p, "P16" + x)
-                t1(S1[:, sl], T[p][:, 0:52], k, o, p, s1 + x)
-            else:
-                k = (0.0, 1.0 / BIG) if s else (1536.0 + 1664.0 / 4096, 4096.0)
-                ts(T.LI[:, sl], T[p][:, 0:52], k[0], k[1], A.add, A.mult, p, "LI" + x)
-                t1(T.LP[:, sl], T.LI[:, sl], 4095, A.bitwise_and, "LI" + x, "LP" + x)
-                t1(S1[:, sl], T.LI[:, sl], 12, A.arith_shift_right, "LI" + x, s1 + x)
-                ts(T.L1[:, sl], T.LP[:, sl], 1.0, float(W - 1), A.min, A.mult, "LP" + x, "L1" + x)
-                tt(T.L1[:, sl], T.L1[:, sl], T.LP[:, sl], A.add, "L1" + x + " LP" + x, "L1" + x)
-                tt(T.L1[:, sl], T.L1[:, sl], S1[:, sl], A.max, "L1" + x + " " + s1 + x, "L1" + x)
-                cp(T.P16[:, sl], T.L1[:, sl], "L1" + x, "P16" + x)
-
-        def add(s, lhs, rhs, off, keys, start=False, stop=False):
-            for h in (0, 1):
-                p = half(s, h)
-                mms([(T[p][:, 0:HB], lhs, rhs[:, off + h * HB:off + (h + 1) * HB], start, stop)], keys[h], p)
-
-        def pair(x, key, start):
-            for h, p in ((0, "PD"), (1, "PX")):
-                mms([(T[p][:, 0:HB], T.ID[:], x[:, h * HB:(h + 1) * HB], start, not start)], key, p)
-
-        def over(s):
-            U = T["UU%d" % s]
-            ts(U[:, 0:HB], T.PD[:, 0:HB], 14.5, 2.0, A.is_ge, A.mult, "PD", "UU%d0" % s)
-            act(U[:, HB:K], T.PX[:, 0:HB], AF.Sign, "PX", "UU%d1" % s, bias=-14.5)
-
-        def fold(s):
-            add(s, T.N8[:], T["UU%d" % s], 0, ("N8 UU%d0" % s, "UU%d1" % s), stop=True)
-
-        def out(s):
-            fc = 0.0 if c == 3 else FW[s]
-            if c < 3:
-                o0, o1 = T.ZF[:, s * K:s * K + HB], T.ZF[:, s * K + HB:(s + 1) * K]
-                k0, k1 = "ZF%d0" % s, "ZF%d1" % s
-            else:
-                z = W + 2 * NL + s * K
-                o0, o1 = T.TT[:, z:z + HB], T.TT[:, z + HB:z + K]
-                k0, k1 = "Z3%d0" % s, "Z3%d1" % s
-            t1(o0, T[half(s, 0)][:, 0:HB], 1.0 + fc, A.add, half(s, 0), k0)
-            act(o1, T[half(s, 1)][:, 0:HB], AF.Identity, half(s, 1), k1, bias=fc - 7.0)
-
+            tt(v("DH"), v("DL"), v("PS", 0, Q), A.min)
         if c == 2:
-            act(T.PP[:], T.IE[:], AF.Copy, "IE", "PP")
+            tt(p2, DRv, v("PS", 1, Q + 1), A.min)
+        tt(p1, C, DRv, A.max)
+        tt(v("XM", 1, 193), p1, v("DH" if c == 1 else "DL"), A.min)
+        if c != 2:
+            tt(p2, DRv, v("PS", 1, Q + 1), A.min)
+        t1(v("NB", 1, 193), v("XM", 1, 193), 0.0, A.is_equal)
+        scan(v("JK", 0, 579, 3), v("NB", 0, 193), v("MK", 0, 193), 0.0, A.mult, A.max)
+        scan(v("JK", 2, 579, 3), v("NB", 193, 0, -1), v("XM", 193, 0, -1), 0.0, A.mult, A.add)
+        scan(v("JK", 1, 579, 3), v("NB", 0, 193), v("DR", 3, 196), 0.0, A.mult, A.max)
+        t1(v("JK", 608, 611), v("KQ", 0, 3), v("JK", 576, 577), A.is_equal)
+        tr(v("Y1"), v("JK", 560, 624))
+        scan(v("Z1", 62, 31, -1), v("Y1", 63, 32, -1), v("Y1", 31, 0, -1), 0.0, A.mult, A.add)
+        scan(v("Z1", 1, 32), v("Y1", 32, 63), v("Y1", 0, 31), 0.0, A.mult, A.max)
+        tr(v("U1"), v("Z1"))
+        scan(v("GI", 193, 0, -1), v("NB", 193, 0, -1), v("XM", 193, 0, -1), v("U1", 50, 51), A.mult, A.add)
+        scan(v("FN"), v("NB", 0, Q), v("MK", 0, Q), v("U1", 16, 17), A.mult, A.max)
+        tt(p1, v("GI", 2, 194), p2, A.max)
+        dma("s", v("WW", r=0), v("FN"))
+        cp(v("HI"), p1)
+        dma("s", v("GG", r=0), v("HI"))
+        tt(v("LO"), p1, v("HI"), A.subtract)
+        dma("s", v("GG", r=1), v("LO"))
+        mms([(v("PL", 0, 104), v("ID"), v("CL", 0, 104), True, False)])
+        if c == 2:
+            act(v("U8"), v(TB, 0, W), AF.Sign, bias=-7.5)
+            mms([(D, v("IB"), v("C112"), True, False)] +
+                [(D, E(ES, b), v(TB, Q * b, Q * (b + 1)), False, False) for b in range(16)] +
+                [(D, E(E8, b), v("U8", Q * b, Q * (b + 1)), False, b == 15) for b in range(16)])
+        act(v("RL"), v("GI", 1, 193), AF.Relu, scale=-1.0)
+        if c == 3:
+            columns("TB2", TB, "a", 0, 16)
+
+        scan(v("PR", 0, 193), v("NB", 0, 193), v("DR", 3, 196), v("U1", 17, 18), A.mult, A.max)
+        tt(p2, p1, v("WK", 1, 193), A.is_equal)
+        tt(p1, v("FN"), v("PS", 194, 386), A.is_equal)
+        tt(v("AA"), p2, v("PR", 1, 193), A.mult)
+        tt(p1, p1, v("RL"), A.mult)
         if c == 1:
-            move1()
-        if c < 3:
-            candidates(c + 1)
-        lookup(0)
-        lookup(1)
-        if c > 1:
-            move1()
-        else:
-            move2()
-        lists(0)
-        act(XO[:], tab.indirect(T.P16[:, 0:52]), AF.Copy, tabk + "P16a", "XO")
-        lists(1)
-        if c < 3:
-            SO, SI = T["SO%d" % c], T["SI%d" % c]
-            tt(SO[:], S1[:], S0[:, 0:104], A.is_equal, s1 + "a " + s0 + "a " + s1 + "b " + s0 + "b", "SO")
-            sync("g", ["SO"], [])
-            trs = []
-            for s, d, src, sm in ((0, up, down, "ra%d" % c), (1, down, up, "rs%d" % c)):
-                rid, pid = topo.addr(d, core)
-                es = topo.engines(core, d)
-                es = es[s * len(es) // 2:(s + 1) * len(es) // 2]
-                trs.append(RemoteDMATransfer(dst_ids=[DstId(rid=rid, pnc=pid)], dma_engine_mask=sum(1 << e for e in es),
-                                             remote_sem=T.sem[sm], src=SO[:, 52 * s:52 * s + 52],
-                                             dst=SI[:, 52 - 52 * s:104 - 52 * s]))
-                count["sent"] += len(es)
-                count[sm] = len(topo.engines(src, core)) // 2
-                writer["SI" + "ba"[s]] = (sm, count[sm], "dma", {})
-            g.remote_dma_fused(trs, local_sem=T.sem["sent"])
-        send(up, down, XI[:], XO[:], "rx%d" % c, "XO", "XI")
-        act(YO[:], tab.indirect(T.P16[:, 52:104]), AF.Copy, tabk + "P16b", "YO")
-        send(down, up, YI[:], YO[:], "ry%d" % c, "YO", "YI")
-        add(0, T.ID[:], XO, 0, ("ID XO", "XO"), start=True)
-        add(1, T.ID[:], YO, 0, ("YO", "YO"), start=True)
-        if c > 1:
-            move2()
-        move3()
-        move4()
+            sites()
+        tt(p1, p1, v("AA"), A.max)
+        tt(p2, p1, v("POS"), A.max)
+        cp(v("HJ"), p2)
+        tt(v("LJ"), p2, v("HJ"), A.subtract)
+        if c == 2:
+            t1(v("OC"), p2, W - 0.5, A.is_ge)
+
+        act(v("RG"), ind(v("GG"), v("S16", 52, 104)), AF.Copy)
+        ts(v("LG"), ind(v("WW"), v("S16", 0, 52)), M - 1538, col(cNF1), A.subtract, A.mult)
+        dma("s", v("GG", r=2), v("HJ"))
+        dma("s", v("GG", r=3), v("LJ"))
+        mms([(v("PL", 0, 52), v("EH", 15 - b, 143 - b), v("LG", b, None, 16), False, False) for b in range(16)])
+        mms([(v("PL", 52, 104), E(E01, b), v("RG", b, None, 16), False, b == 15) for b in range(16)])
+        PL = v("PL", 0, 104)
+
+        def flags():
+            SO, SI = "SO%d" % c, "SI%d" % c
+            tt(v(SO), PL, S0, A.is_equal)
+            send([(up, down, v(SI, 52, 104), v(SO, 0, 52), "ra%d" % c), (down, up, v(SI, 0, 52), v(SO, 52, 104), "rs%d" % c)])
+        if c == 2:
+            flags()
+        cp(v("P16"), PL)
+        act(v(YO), ind(v(TB, 0, W), v("P16", 52, 104)), AF.Identity, bias=0.5)
+        if c == 1:
+            flags()
+        t1(v(XO), ind(v(TB, 0, W), v("P16", 0, 52)), 0.5, A.add)
+        send([(up, down, v(XI), v(XO), "rx%d" % c)])
+        send([(down, up, v(YI), v(YO), "ry%d" % c)])
+        cp(S1, PL)
+
+        def own(s, h, banks):
+            mms([(v(b, 0, HB), v("ID"), v(YO if s else XO, h * HB, (h + 1) * HB), True, False) for b in banks.split()])
+        own(1, 0, "MA")
+        own(1, 1, "MT MF")
+        own(0, 0, "MB")
+
+        def jlist():
+            mms([(v("PL", 208, 400), E(E23, b), v("GG", b, None, 16), b == 0, b == 15) for b in range(16)])
+
+        def mix(s, h, banks):
+            o = s * K + h * HB
+            u, z = v("UU", o, o + HB), v(TB, W + o, W + o + HB)
+            bs = [v(b, 0, HB) for b in banks.split()]
+            for j, b in enumerate(bs):
+                mms([(b, v("ID"), v(XI if s else YI, h * HB, (h + 1) * HB), False, j == 0)])
+            if len(bs) == 1:
+                ts(u, bs[0], 15.5, 16.0, A.is_ge, A.mult)
+                tt(z, bs[0], u, A.subtract)
+            else:
+                act(u, bs[0], AF.Sign, bias=-15.5)
+                mms([(bs[1], v("N8"), u, False, True)])
+                act(z, bs[1], AF.Identity, bias=-8.0)
+
+        def mixes():
+            mix(1, 0, "MA")
+            mix(1, 1, "MT MF")
+            own(0, 1, "MT MF")
+            if c == 2:
+                mix(0, 1, "MT MF")
+                own(0, 0, "MT")
+                mix(0, 0, "MT MB")
+            else:
+                mix(0, 0, "MB")
+                mix(0, 1, "MT MF")
 
         if c < 3:
             so = (c - 1) * 104
-            t1(T.HH[:], T.IE[:], 0.5, A.is_ge, "IE", "HH")
-            dma("s", T.GG[0::16, :], T.HH[:], "HH", GGK)
-            act(q2, T.IE[:], AF.Relu, "IE", "PE", scale=-1.0, bias=1.0)
-
-            def still(s):
-                x, sl = "ab"[s], slice(s * 52, (s + 1) * 52)
-                tt(T.SB[:, sl], SO[:, sl], SI[:, sl], A.mult, "SO SI" + x, "SB" + x)
-                for h, p in ((0, "PD"), (1, "PX")):
-                    o = s * 52 + h * 26
-                    mms([(T[p][:, b:HB:16], T.E2[:, 128 * b:128 * (b + 1)], T.SB[:, o:o + 26], b == 0, b == 15)
-                         for b in range(16)], E2K + " SB" + x, p)
-                    fo = F0 + s * K + h * HB
-                    act(T.ZF[:, fo:fo + HB], T[p][:, 0:HB], AF.Copy, p, "FF%d%d" % (s, h), scale=FW[s])
-            still(1)
-            still(0)
             if c == 1:
-                candidates2()
-                tt(V, T.IE[:], T.WK[:, 1:193], A.add, "IE WK", "VB")
+                cp(v("ST16"), v("STF"))
+            act(v("FG", K, NL), ind(v("GG"), v("ST16", so + 52, so + 104)), AF.Copy, scale=2.0 ** -12)
+            t1(v("FG", 0, K), ind(v("GG"), v("ST16", so, so + 52)), 2.0 ** -12, A.mult)
+            tt(v("DS"), v("STF", so, so + 104), S1, A.subtract)
+            mms([(v("PL", 104, 208), v("ID"), v("CL", 104, 208), True, False)] +
+                [(v("PL", 104, 208), E(E23, b), v("FG", b, None, 16), False, b == 15) for b in range(16)])
+            tt(v("G1"), v("PL", 104, 208), v("SO%d" % c), A.is_lt)
+            jlist()
+            tt(v("G2"), v("G1"), v("DS"), A.mult)
+            tt(v("PV", 384, 488), v("G2"), v("SI%d" % c), A.mult)
+            tt(v("DS"), v("PV", 384, 488), S1, A.add)
+            cp(v("S16"), v("DS"))
+            scatter(c + 1)
+            cp(v("J16"), v("PL", 208, 400))
+            if c == 1:
+                mixes()
+                for j, (a, b) in enumerate(((0, 4), (4, 7), (7, 8))):
+                    columns(TB, "TB2", "a", 8 + a, 8 + b)
+                    columns(TB, "TB2", "v", a, b)
+                    sums("TB2", range(a, b), j == 0, False)
+                    sums("TB2", range(8 + a, 8 + b), False, j == 2)
             else:
-                t1(q1, T.HH[:], float(NL), A.mult, "HH", "PC")
-                tt(q1, q1, T.IE[:], A.add, "PC IE", "PC")
-                tt(T.PP[:], q1, T.PP[:], A.max, "PP PC", "PP")
-                tt(V, T.PP[:], T.WK[:, 1:193], A.add, "PP WK", "VB")
-            dma("s", T.VB[1:128, 0:1], T.VB[0:127, 192:193], "VB", "VB0")
-            dma("s", T.VB[0:127, 193:194], T.VB[1:128, 1:2], "VB", "VB1")
-            candidates3(c + 1)
-            cjk = "CJa%d CJb%d CJc%d" % (c + 1, c + 1, c + 1)
-            tt(q1, q2, T["CJ%d" % (c + 1)][:], A.mult, "PE " + cjk, "PC")
-            t1(T.FG[:, 0:K], T.GG[:, :].indirect(T.ST16[:, so:so + 52]), col(cFa), A.mult, GGK + "ST16 cFa", "FGa")
-            act(T.FG[:, K:NL], T.GG[:, :].indirect(T.ST16[:, so + 52:so + 104]), AF.Copy, GGK + "ST16 cFb", "FGb",
-                scale=col(cFb))
-            add(1, T.NI[:], T.ZF, F0 + K, ("NI FF10", "FF11"))
-            pair(YO, "YO", True)
-            pair(XI, "XI", False)
-            over(1)
-            add(1, T.ID[:], XI, 0, ("XI", "XI"))
-            add(0, T.NI[:], T.ZF, F0, ("FF00", "FF01"))
-            pair(XO, "XO", True)
-            pair(YI, "YI", False)
-            tt(T.JID[:], q1, T.IE[:], A.add, "PC IE", "JID")
-            ts(q1, q2, float(F0), -1.0, A.mult, A.add, "PE", "PC")
-            ts(T.KP[:, 0:Q], C, 1.0 / BIG, col(cTH), A.mult, A.add, "PC cTH", "KPa")
-            tt(T.T3[:], q1, T.JID[:], A.add, "PC JID", "T3")
-            over(0)
-            add(1, T.BD[:], T.FG, K, ("FGb", "FGb"))
-            fold(1)
-            add(0, T.ID[:], YI, 0, ("YI", "YI"))
-            add(0, T.BD[:], T.FG, 0, ("FGa", "FGa"))
-            fold(0)
-            t1(T.KP[:, Q:2 * Q], T.KP[:, 0:Q], 255, A.bitwise_and, "KPa", "KPb")
-            cp(T.J16[:], T.T3[:], "T3", "J16")
-            out(1)
-            tt(T.BF[:], q2, T.KP[:, Q:2 * Q], A.mult, "PE KPb", "BF")
-            ends()
-            out(0)
-            ZK = "ZF00 ZF01 ZF10 ZF11 ZF0 FF00 FF01 FF10 FF11 J16"
-            win = T.ZF[:, 0:F0 + NL]
-            cp(T.GG[:, 0:1024], win.indirect(T.J16[:, 0:64]), ZK, "GG0")
-            act(T.GG[:, 2048:3072], win.indirect(T.J16[:, 128:192]), AF.Copy, ZK, "GG3")
-            cp(T.GG[:, 1024:1536], win.indirect(T.J16[:, 64:96]), ZK, "GG1")
-            act(T.GG[:, 1536:2048], win.indirect(T.J16[:, 96:128]), AF.Copy, ZK, "GG2")
-            mms([(T.PX[:, 0:104], E(b), T.FG[:, b::16], b == 0, b == 15) for b in range(16)], "ZB FGa FGb", "PX")
-            for j, ks in ((0, "GG0"), (2, "GG3"), (1, "GG1 GG2")):
-                o = T.PC[:, 64 * j:64 * j + 64]
-                mms([(o, T.IB[:], T.THB[:, 0:64], True, False), (o, T.IB[:], T.BF[:, 64 * j:64 * j + 64], False, False)] +
-                    [(o, E(b), T.GG[:, 1024 * j + b:1024 * (j + 1):16], False, b == 15) for b in range(16)],
-                    "IB BF ZB GG0 " + ks, "PC")
+                tt(v("T1"), D, v("OC"), A.mult)
+                tt(C, C, v("T1"), A.add)
+                mixes()
         else:
-            ts(q1, T.IE[:], 0.5, float(2 * NL), A.is_ge, A.mult, "IE", "PC")
-            act(T.T3[:], T.WK[:, 1:193], AF.Copy, "WK", "T3", scale=2.0 ** -12)
-            tt(q1, q1, T.IE[:], A.add, "PC IE", "PC")
-            tt(T.PP[:], q1, T.PP[:], A.max, "PP PC", "PP")
-            ts(q2, T.PP[:], 0.5, float(W - 1), A.is_ge, A.mult, "PP", "PE")
-            tt(q2, q2, T.PP[:], A.add, "PE PP", "PE")
-            tt(T.KP[:, 0:Q], q2, T.T3[:], A.max, "PE T3", "KPa")
-            t1(T.KH[:, 0:Q], T.KP[:, 0:Q], 63, A.bitwise_and, "KPa", "KHa")
-            t1(T.KH[:, Q:2 * Q], T.KP[:, 0:Q], 8128, A.bitwise_and, "KPa", "KHb")
-            cp(T.PK2[:, 0:2 * Q], T.KH[:], "KHa KHb", "PK2 PKb")
-            dma("s", T.GG[0::16, :], T.PK2[:, 0:Q], "PK2", "GG0 GG1")
-            dma("s", T.GG[1::16, :], T.PK2[:, Q:2 * Q], "PKb", "GG2 GG3")
-            pair(YO, "YO", True)
-            pair(XI, "XI", False)
-            over(1)
-            add(1, T.ID[:], XI, 0, ("XI", "XI"))
-            fold(1)
-            pair(XO, "XO", True)
-            t1(col(cI), col(cCR), 1.0 / BIG, A.mult, "cCR", "cI")
-            t1(T.ZB[:], T.ZB[:], col(cI), A.mult, "ZB cI", "ZB")
-            out(1)
-            pair(YI, "YI", False)
-            over(0)
-            add(0, T.ID[:], YI, 0, ("YI", "YI"))
-            fold(0)
-            for j, p in enumerate(("PC", "PD", "PX")):
-                mms([(T[p][:, 0:64], E(b), T.GG[:, 1024 * j + b:1024 * (j + 1):16], b == 0, b == 15) for b in range(16)],
-                    "ZB " + GGK, p)
-            cp(T.DS[:], S1[:], s1 + "a " + s1 + "b", "DS")
-            dma("s", T.ya[:], T.DS[:, 0:52], "DS", "ya")
-            dma("s", T.yb[:], T.DS[:, 52:104], "DS", "yb")
-            out(0)
-            cp(T.J16[:, 0:64], T.PC[:, 0:64], "PC", "J0 J16")
-            for j in range(3):
-                ZK = tabk + "Z300 Z301 Z310 Z311 J%d" % j
-                a = 64 * j
-                cp(T.YY[:, 16 * a:16 * a + 512], T.TT[:, :].indirect(T.J16[:, a:a + 32]), ZK, "YY%d" % j)
-                dma("s", T.ym[:, 16 * a:16 * a + 512], T.YY[:, 16 * a:16 * a + 512], "YY%d" % j, "ym%d" % j)
-                if j < 2:
-                    p = ("PD", "PX")[j]
-                    cp(T.J16[:, a + 64:a + 128], T[p][:, 0:64], p, "J%d" % (j + 1))
-                a = a + 32
-                act(T.YY[:, 16 * a:16 * a + 512], T.TT[:, :].indirect(T.J16[:, a:a + 32]), AF.Copy, ZK, "YZ%d" % j)
-                dma("s", T.ym[:, 16 * a:16 * a + 512], T.YY[:, 16 * a:16 * a + 512], "YZ%d" % j, "yn%d" % j)
+            jlist()
+            dma("s", hbm(T.ya[:]), v("SS3", 0, 52))
+            dma("s", hbm(T.yb[:]), v("SS3", 52, 104))
+            cp(v("J16"), v("PL", 208, 400))
+            mixes()
+            for a, b in ((0, 3), (3, 6), (6, 8)):
+                for who, o in (("a", 8), ("v", 0)):
+                    columns(TB, "YY", who, o + a, o + b)
+                    dma("s", hbm(T.ym[:, Q * (o + a):Q * (o + b)]), v("YY", Q * (o + a), Q * (o + b)))
     for s in SEMAPHORES:
         if count[s]:
             g.sync.wait_ge(T.sem[s], count[s])

@@ -1,5 +1,5 @@
 from concourse.bass import DstId, RemoteDMATransfer
-from concourse.mybir import AluOpType, AxisListType, ActivationFunctionType
+from concourse.mybir import AluOpType, ActivationFunctionType
 
 W, K, KC, Q = 3072, 832, 52, 192
 NL = 2 * K
@@ -17,18 +17,19 @@ def _b(names, cols, d="float32", where="sbuf"):
 
 _b("TB1 TB2 TB3", W + NL, "bfloat16")
 _b("WL1 WL2 WL3 WR1 WR2 WR3 WW", W)
-_b("GG YY U8", W, "bfloat16")
+_b("GG JW YY U8", W, "bfloat16")
 _b("LG", K, "float16")
 _b("FG UU", NL, "bfloat16")
-_b("RG XO1 XO2 XO3 XI1 XI2 XI3 YO1 YO2 YO3 YI1 YI2 YI3", K, "bfloat16")
+_b("RG", K, "bfloat16")
+_b("XI1 XI2 XI3 YI1 YI2 YI3 XP1 XP2 XP3 YP1 YP2 YP3 XH YH XQ YQ CT", HB, "bfloat16")
 _b("SO1 SO2 SI1 SI2", 2 * KC, "bfloat16")
 _b("VAL", K)
 _b("INI", 208, "int32")
 _b("THI COLI", 4, "int32")
 _b("COL", 16)
-_b("ONE ID IB N8", 128, "bfloat16")
+_b("ONE ID IB N8 N16 NI I16", 128, "bfloat16")
 _b("BD1 BD", 8, "bfloat16")
-_b("EE", 4 * 144, "bfloat16")
+_b("EE", 3 * 144, "bfloat16")
 _b("EH", 144, "float16")
 _b("CL", 208, "bfloat16")
 _b("WK MK NB XM GI PR", 194)
@@ -44,10 +45,10 @@ _b("ST16", 208, "uint16")
 _b("STF", 208)
 _b("LI SI32", 104, "int32")
 _b("L1 KO SS1 SS2 SS3 DS G1 G2", 104)
-BANKS = ("PC", "PL", "PV", "PS", "MA", "MB", "MT", "MF")
+BANKS = ("PC", "PL", "PV", "MG", "MA", "MB", "MT", "MF")
 _b(" ".join(BANKS), 512, "float32", "psum")
 
-NDMA = 56
+NDMA = 48
 SEMAPHORES = ["qv", "qa", "qt", "qg", "sent"] + ["d%d" % i for i in range(NDMA)] + \
     ["rk", "ra1", "ra2", "rs1", "rs2", "rx1", "rx2", "rx3", "ry1", "ry2", "ry3"]
 
@@ -194,47 +195,47 @@ def rank_program(g, core, T, topo):
 
     def col(j):
         return v("COL", j, j + 1)
-    cI, cI192, cF, cL, cNF1, c01, c03, c23, cT1, cX = range(10)
-    ES, E8, E01, E23 = range(4)
+    cI192, cNF1, c01, cT1, cX = range(5)
+    ES, E8, E01 = range(3)
 
     def E(k, b):
         return v("EE", 144 * k + 15 - b, 144 * k + 143 - b)
 
+    def Ecols(k):
+        return v("EE", 144 * k + 15, 144 * k + 143, 16)
+
     small = dict(allow_small_or_imprecise_dtypes=True)
     dma("s", v("INI", 52, 104), hbm(T.lb[:]))
     dma("a", v("INI", 0, 52), hbm(T.la[:]))
-    ms(v("ZERO"), 0.0)
     ms(v("FILL"), BIG)
+    dma("a", v("WL1", r=0), v("FILL"))
+    ms(v("ZERO"), 0.0)
+    dma("s", v("WR1", r=0), v("ZERO"))
+    ms(v("ONE"), 1.0)
     iota(v("COLI", 0, 1), [[0, 1]], 0, 1)
     iota(v("VAL"), [[1, K]], W + K, 0, **small)
-    dma("s", v("WR1", r=0), v("ZERO"))
-    dma("s", v("WL1", r=0), v("FILL"))
-    ms(v("ONE"), 1.0)
     act(v("CL", 0, 52), v("ONE", 0, 52), AF.Silu, scale=1536.0)
-    dma("s", v("THI", 0, 1), hbm(T.th[:]))
     dma("s", v("INI", 104, 156), hbm(T.ka[:]))
     dma("s", v("INI", 156, 208), hbm(T.kb[:]))
-    dma("s", v("TB1", 0, W // 2), hbm(T.mk[:, 0:W // 2]))
-    dma("s", v("TB1", W // 2, W), hbm(T.mk[:, W // 2:W]))
+    dma("s", v("TB1", 0, W), hbm(T.mk[:]))
+    dma("s", v("THI", 0, 1), hbm(T.th[:]))
     ms(v("EE"), 0.0)
-    ms(v("EH"), 0.0)
+    ms(v("DR", 0, 4), 0.0)
+    cI = v("COLI", 1, 2)
+    t1(cI, v("COLI", 0, 1), 15, A.bitwise_and)
+    t1(col(cI192), cI, 192.0, A.mult)
+    t1(col(c01), cI, 1.5, A.is_lt)
+    ts(v("NB", 0, 1), cI, 0.5, 1.0, A.is_ge, A.mult)
+    ts(v("NB", 193, 194), cI, 14.5, 1.0, A.is_lt, A.mult)
+    ts(v("XM", 193, 194), cI, 14.5, W + 1.0, A.is_ge, A.mult)
+    ts(col(cNF1), cI, 0.5, -1.0, A.is_lt, A.mult)
     ms(v("JK", 560, 624), 0.0)
     ms(v("Z1"), 0.0)
-    ms(v("DR", 0, 4), 0.0)
-    ms(v("C112"), -112.0)
-    ms(v("CL", 52, 104), -2.0)
-    ms(v("CL", 104, 208), 0.25)
-    t1(v("COLI", 1, 2), v("COLI", 0, 1), 15, A.bitwise_and)
-    cp(col(cI), v("COLI", 1, 2))
-    t1(col(cI192), v("COLI", 1, 2), 192.0, A.mult)
-    t1(col(cF), col(cI), 0.5, A.is_lt)
-    t1(col(cL), col(cI), 14.5, A.is_ge)
-    t1(col(c01), col(cI), 1.5, A.is_lt)
-    t1(col(c03), col(cI), 3.5, A.is_lt)
+    iota(v("WK"), [[1, 194]], 1, 0, **small)
     sel(v("BD1"), v("ONE", 0, 8), [[-16, 8]], A.is_ge, 0, 1)
     sel(v("BD"), v("BD1"), [[16, 8]], A.is_ge, 15, -1)
     sel(v("ID"), v("ONE"), [[-1, 128]], A.is_equal, 0, 1)
-    iota(v("WK"), [[1, 194]], 1, 0, **small)
+    iota(v("GG", 0, W // 2), [[0, W // 2]], 0, 0, **small)
 
     def scatter(c):
         act(ind(v("WR%d" % c), v("S16", 52, 104)), v("VAL"), AF.Silu)
@@ -242,53 +243,58 @@ def rank_program(g, core, T, topo):
         dma("s", v("DL"), v("WL%d" % c, r=0))
         dma("s", v("DR", 4, 196), v("WR%d" % c, r=0))
 
-    cp(v("S16"), v("INI", 0, 104))
-    scatter(1)
-    act(v("EE", 144 * ES + 15, 144 * ES + 143, 16), v("BD"), AF.Copy, scale=BIG)
-    act(v("IB"), v("ID"), AF.Copy, scale=BIG)
-    ts(col(cT1), v("THI", 0, 1), -1.0, 1.0, A.mult, A.add)
-    t1(v("WK"), v("WK"), col(cI192), A.add)
-    t1(v("THB"), v("ZERO"), col(cT1), A.add)
-    ts(v("MK"), v("WK"), -1.0, M - 1, A.mult, A.add)
-    cp(v("PS", 0, 194), v("WK"))
-    ts(v("NB", 0, 1), col(cF), -1.0, 1.0, A.mult, A.add)
-    ts(v("NB", 193, 194), col(cL), -1.0, 1.0, A.mult, A.add)
-    t1(v("XM", 193, 194), col(cL), W + 1.0, A.mult)
-    tt(col(cX), v("NB", 0, 1), v("NB", 193, 194), A.mult)
-    t1(col(cNF1), col(cF), -1.0, A.mult)
-    tt(col(c23), col(c03), col(c01), A.subtract)
-    ts(v("KQ"), v("ONE", 0, 4), v("MK", 0, 1), col(cX), A.mult, A.mult)
+    def blank(name, a, b):
+        for j in range(a, b):
+            act(v(name, 768 * j, 768 * (j + 1)), v("VAL", 0, 768), AF.Copy, scale=0.0)
 
-    def sums(tb, blocks, first, last):
-        lst = [(v("PC", 0, Q), v("IB"), v("THB"), True, False)] if first else []
-        lst += [(v("PC", 0, Q), E(ES, b), v(tb, Q * b, Q * (b + 1)), False, last and b == blocks[-1]) for b in blocks]
-        mms(lst)
-    sums("TB1", range(16), True, True)
-    act(v("WW"), v("TB1", 0, W), AF.Copy, scale=0.0)
-    ms(v("GG"), 0.0)
-    cp(v("PS", 194, 386), v("MK", 0, Q))
-    t1(v("POS"), v("WK", 0, Q), -1.0, A.add)
-    cp(v("EH", 15, 143, 16), v("BD"))
-    act(v("EE", 144 * E01 + 15, 144 * E01 + 143, 16), v("BD"), AF.Copy, scale=col(c01))
-    act(v("EE", 144 * E23 + 15, 144 * E23 + 143, 16), v("BD"), AF.Copy, scale=col(c23))
-    act(v("EE", 144 * E8 + 15, 144 * E8 + 143, 16), v("BD"), AF.Copy, scale=-8 * BIG)
-    act(v("N8"), v("ID"), AF.Copy, scale=-8.0)
-    for c in (2, 3):
+    def clear(c):
         dma("s", v("WR%d" % c, r=0), v("ZERO"))
         dma("s", v("WL%d" % c, r=0), v("WK", 0, Q))
 
-    def sites():
-        for o, c in ((0, 2), (52, 3)):
-            t1(v("L1", o, o + 52), v("INI", 104, 156), float(c), A.mult)
-        for o in (0, 52):
-            tt(v("LI", o, o + 52), v("L1", o, o + 52), v("INI", 156, 208), A.add)
-        t1(v("SI32"), v("LI"), 1023, A.bitwise_and)
-        ts(v("KO"), v("SI32"), 3.0, 1.0, A.mult, A.add)
-        send([(up, down, v("STF", 2 * o + 52, 2 * o + 104), v("KO", o, o + 52), "rk") for o in (0, 52)])
-        for o in (0, 52):
-            t1(v("STF", 2 * o, 2 * o + 52), v("SI32", o, o + 52), 3.0, A.mult)
+    C, D = v("PC", 0, Q), v("MT", 0, Q)
 
-    C, D = v("PC", 0, Q), v("PC", Q, 2 * Q)
+    def sums(out, e, tb, blocks, first, last):
+        mms([(out, E(e, b), v(tb, Q * b, Q * (b + 1)), first and b == blocks[0], last and b == blocks[-1]) for b in blocks])
+
+    cp(v("S16"), v("INI", 0, 104))
+    scatter(1)
+    act(Ecols(ES), v("BD"), AF.Copy, scale=BIG)
+    sums(C, ES, "TB1", range(16), True, False)
+    t1(v("WK"), v("WK"), col(cI192), A.add)
+    ts(col(cT1), v("THI", 0, 1), -1.0, 1.0, A.mult, A.add)
+    dma("s", v("JW"), hbm(T.mk[:]))
+    act(v("IB"), v("ID"), AF.Copy, scale=BIG)
+    act(v("THB"), v("ZERO"), AF.Identity, bias=col(cT1))
+    mms([(C, v("IB"), v("THB"), False, True)])
+    act(v("MG", 0, Q), v("WK", 1, Q + 1), AF.Copy)
+    for o, c in ((0, 2), (52, 3)):
+        t1(v("L1", o, o + 52), v("INI", 104, 156), float(c), A.mult)
+    ts(v("MK"), v("WK"), -1.0, M - 1, A.mult, A.add)
+    for o in (0, 52):
+        tt(v("LI", o, o + 52), v("L1", o, o + 52), v("INI", 156, 208), A.add)
+    tt(col(cX), v("NB", 0, 1), v("NB", 193, 194), A.mult)
+    t1(v("SI32"), v("LI"), 1023, A.bitwise_and)
+    ts(v("KQ"), v("ONE", 0, 4), v("MK", 0, 1), col(cX), A.mult, A.mult)
+    ts(v("KO"), v("SI32"), 3.0, 1.0, A.mult, A.add)
+    send([(up, down, v("STF", 2 * o + 52, 2 * o + 104), v("KO", o, o + 52), "rk") for o in (0, 52)])
+    ms(v("EH"), 0.0)
+    ms(v("CL", 52, 104), -2.0)
+    cp(v("EH", 15, 143, 16), v("BD"))
+    blank("WW", 0, 4)
+    blank("GG", 2, 4)
+    act(v("POS"), v("WK", 0, Q), AF.Identity, bias=-1.0)
+    act(Ecols(E01), v("BD"), AF.Copy, scale=col(c01))
+
+    def constants():
+        act(v("PC", Q, 2 * Q), v("WK", 1, Q + 1), AF.Copy)
+        act(Ecols(E8), v("BD"), AF.Copy, scale=-8 * BIG)
+        for x, k in (("N8", -8.0), ("N16", -16.0), ("NI", -1.0), ("I16", 1.0 / 16)):
+            act(v(x), v("ID"), AF.Copy, scale=k)
+        act(v("CT"), v("VAL", 0, HB), AF.Identity, scale=0.0, bias=2064.0)
+        act(v("C112"), v("ZERO"), AF.Identity, bias=-112.0)
+        act(v("CL", 104, 208), v("ZERO", 0, 104), AF.Identity, bias=0.25)
+        clear(2)
+
     p1, p2 = v("PV", 0, Q), v("PV", Q, 2 * Q)
     DRv = v("DR", 4, 196)
 
@@ -299,23 +305,30 @@ def rank_program(g, core, T, topo):
         else:
             act(v(out, Q * a, Q * b), src, AF.Copy)
 
+    def stay(c):
+        tt(p2, DRv, v("MG", 0, Q) if c == 1 else v("PC", Q, 2 * Q), A.min)
+
     for c in (1, 2, 3):
-        S0, S1 = (v("INI", 0, 104) if c == 1 else v("SS%d" % (c - 1))), v("SS%d" % c)
-        XO, XI, YO, YI = "XO%d" % c, "XI%d" % c, "YO%d" % c, "YI%d" % c
+        XP, XI, YP, YI = "XP%d" % c, "XI%d" % c, "YP%d" % c, "YI%d" % c
         TB = "TB%d" % c
         if c == 1:
-            tt(v("DH"), v("DL"), v("PS", 0, Q), A.min)
-        if c == 2:
-            tt(p2, DRv, v("PS", 1, Q + 1), A.min)
+            tt(v("DH"), v("DL"), v("WK", 0, Q), A.min)
         tt(p1, C, DRv, A.max)
-        tt(v("XM", 1, 193), p1, v("DH" if c == 1 else "DL"), A.min)
+        if c == 2:
+            act(v("U8"), v(TB, 0, W), AF.Sign, bias=-7.5)
+            mms([(D, v("IB"), v("C112"), True, False)])
+            sums(D, ES, TB, range(16), False, False)
+            sums(D, E8, "U8", range(16), False, True)
+        if c == 3:
+            columns("TB2", TB, "a", 0, 8)
         if c != 2:
-            tt(p2, DRv, v("PS", 1, Q + 1), A.min)
+            stay(c)
+        tt(v("XM", 1, 193), p1, v("DH" if c == 1 else "DL"), A.min)
         t1(v("NB", 1, 193), v("XM", 1, 193), 0.0, A.is_equal)
         scan(v("JK", 0, 579, 3), v("NB", 0, 193), v("MK", 0, 193), 0.0, A.mult, A.max)
         scan(v("JK", 2, 579, 3), v("NB", 193, 0, -1), v("XM", 193, 0, -1), 0.0, A.mult, A.add)
-        scan(v("JK", 1, 579, 3), v("NB", 0, 193), v("DR", 3, 196), 0.0, A.mult, A.max)
         t1(v("JK", 608, 611), v("KQ", 0, 3), v("JK", 576, 577), A.is_equal)
+        scan(v("JK", 1, 579, 3), v("NB", 0, 193), v("DR", 3, 196), 0.0, A.mult, A.max)
         tr(v("Y1"), v("JK", 560, 624))
         scan(v("Z1", 62, 31, -1), v("Y1", 63, 32, -1), v("Y1", 31, 0, -1), 0.0, A.mult, A.add)
         scan(v("Z1", 1, 32), v("Y1", 32, 63), v("Y1", 0, 31), 0.0, A.mult, A.max)
@@ -328,126 +341,151 @@ def rank_program(g, core, T, topo):
         dma("s", v("GG", r=0), v("HI"))
         tt(v("LO"), p1, v("HI"), A.subtract)
         dma("s", v("GG", r=1), v("LO"))
-        mms([(v("PL", 0, 104), v("ID"), v("CL", 0, 104), True, False)])
-        if c == 2:
-            act(v("U8"), v(TB, 0, W), AF.Sign, bias=-7.5)
-            mms([(D, v("IB"), v("C112"), True, False)] +
-                [(D, E(ES, b), v(TB, Q * b, Q * (b + 1)), False, False) for b in range(16)] +
-                [(D, E(E8, b), v("U8", Q * b, Q * (b + 1)), False, b == 15) for b in range(16)])
+        PA, PB = v("PL", 0, 52), v("MB", 0, 52)
+        mms([(PA, v("ID"), v("CL", 0, 52), True, False), (PB, v("ID"), v("CL", 52, 104), True, False)])
         act(v("RL"), v("GI", 1, 193), AF.Relu, scale=-1.0)
+        if c == 1:
+            constants()
         if c == 3:
-            columns("TB2", TB, "a", 0, 16)
+            columns("TB2", TB, "a", 8, 16)
 
         scan(v("PR", 0, 193), v("NB", 0, 193), v("DR", 3, 196), v("U1", 17, 18), A.mult, A.max)
         tt(p2, p1, v("WK", 1, 193), A.is_equal)
-        tt(p1, v("FN"), v("PS", 194, 386), A.is_equal)
+        tt(p1, v("FN"), v("MK", 0, Q), A.is_equal)
         tt(v("AA"), p2, v("PR", 1, 193), A.mult)
         tt(p1, p1, v("RL"), A.mult)
-        if c == 1:
-            sites()
         tt(p1, p1, v("AA"), A.max)
         tt(p2, p1, v("POS"), A.max)
+
+        so = (c - 1) * 104
+        ts(v("LG"), ind(v("WW"), v("S16", 0, 52)), M - 1538, col(cNF1), A.subtract, A.mult)
+        act(v("RG"), ind(v("GG"), v("S16", 52, 104)), AF.Copy)
+        mms([(PA, v("EH", 15 - b, 143 - b), v("LG", b, None, 16), False, b == 15) for b in range(16)])
+        mms([(PB, E(E01, b), v("RG", b, None, 16), False, b == 15) for b in range(16)])
         cp(v("HJ"), p2)
+        dma("s", v("JW", r=0), v("HJ"))
         tt(v("LJ"), p2, v("HJ"), A.subtract)
+        dma("s", v("JW", r=1), v("LJ"))
+        PJ = v("MG" if c < 3 else "PC", 0, Q)
+
+        def jlist(a, b):
+            mms([(PJ, E(E01, x), v("JW", x, None, 16), x == 0, x == 15) for x in range(a, b)])
+        if c < 3:
+            jlist(0, 16)
+        if c == 1:
+            for o in (0, 52):
+                t1(v("STF", 2 * o, 2 * o + 52), v("SI32", o, o + 52), 3.0, A.mult)
+            cp(v("ST16"), v("STF"))
         if c == 2:
             t1(v("OC"), p2, W - 0.5, A.is_ge)
+            tt(v("T1"), D, v("OC"), A.mult)
+        S0, S1 = ("INI" if c == 1 else "SS%d" % (c - 1)), "SS%d" % c
+        SO, SI = "SO%d" % c, "SI%d" % c
+        tab = v(TB, 0, W)
 
-        act(v("RG"), ind(v("GG"), v("S16", 52, 104)), AF.Copy)
-        ts(v("LG"), ind(v("WW"), v("S16", 0, 52)), M - 1538, col(cNF1), A.subtract, A.mult)
-        dma("s", v("GG", r=2), v("HJ"))
-        dma("s", v("GG", r=3), v("LJ"))
-        mms([(v("PL", 0, 52), v("EH", 15 - b, 143 - b), v("LG", b, None, 16), False, False) for b in range(16)])
-        mms([(v("PL", 52, 104), E(E01, b), v("RG", b, None, 16), False, b == 15) for b in range(16)])
-        PL = v("PL", 0, 104)
-
-        def flags():
-            SO, SI = "SO%d" % c, "SI%d" % c
-            tt(v(SO), PL, S0, A.is_equal)
+        cp(v("P16", 0, 52), PA)
+        act(v("XH"), ind(tab, v("P16", 0, 26)), AF.Identity, scale=16.0, bias=1.0)
+        if c < 3:
+            tt(v(SO, 0, 52), PA, v(S0, 0, 52), A.is_equal)
+        cp(v(S1, 0, 52), PA)
+        if c < 3:
+            tt(v(SO, 52, 104), PB, v(S0, 52, 104), A.is_equal)
             send([(up, down, v(SI, 52, 104), v(SO, 0, 52), "ra%d" % c), (down, up, v(SI, 0, 52), v(SO, 52, 104), "rs%d" % c)])
-        if c == 2:
-            flags()
-        cp(v("P16"), PL)
-        act(v(YO), ind(v(TB, 0, W), v("P16", 52, 104)), AF.Identity, bias=0.5)
-        if c == 1:
-            flags()
-        t1(v(XO), ind(v(TB, 0, W), v("P16", 0, 52)), 0.5, A.add)
-        send([(up, down, v(XI), v(XO), "rx%d" % c)])
-        send([(down, up, v(YI), v(YO), "ry%d" % c)])
-        cp(S1, PL)
+        cp(v("P16", 52, 104), PB)
+        act(v("YH"), ind(tab, v("P16", 52, 78)), AF.Identity, scale=16.0, bias=1.0)
+        cp(v(S1, 52, 104), PB)
+        tt(v(XP), ind(tab, v("P16", 26, 52)), v("XH"), A.add)
+        send([(up, down, v(XI), v(XP), "rx%d" % c)])
+        if c < 3:
+            act(v("FG", K, NL), ind(v("JW"), v("ST16", so + 52, so + 104)), AF.Copy, scale=2.0 ** -12)
+            t1(v("FG", 0, K), ind(v("JW"), v("ST16", so, so + 52)), 2.0 ** -12, A.mult)
+        tt(v(YP), ind(tab, v("P16", 78, 104)), v("YH"), A.add)
+        send([(down, up, v(YI), v(YP), "ry%d" % c)])
+        S1 = v(S1)
 
-        def own(s, h, banks):
-            mms([(v(b, 0, HB), v("ID"), v(YO if s else XO, h * HB, (h + 1) * HB), True, False) for b in banks.split()])
-        own(1, 0, "MA")
-        own(1, 1, "MT MF")
-        own(0, 0, "MB")
-
-        def jlist():
-            mms([(v("PL", 208, 400), E(E23, b), v("GG", b, None, 16), b == 0, b == 15) for b in range(16)])
-
-        def mix(s, h, banks):
-            o = s * K + h * HB
-            u, z = v("UU", o, o + HB), v(TB, W + o, W + o + HB)
-            bs = [v(b, 0, HB) for b in banks.split()]
-            for j, b in enumerate(bs):
-                mms([(b, v("ID"), v(XI if s else YI, h * HB, (h + 1) * HB), False, j == 0)])
-            if len(bs) == 1:
-                ts(u, bs[0], 15.5, 16.0, A.is_ge, A.mult)
-                tt(z, bs[0], u, A.subtract)
+        def own(s, h):
+            x, xh = (v(YP), v("YH")) if s else (v(XP), v("XH"))
+            if h:
+                b = v("MA" if s else "MB", 0, HB)
+                mms([(b, v("ID"), v("CT"), True, False), (b, v("NI"), xh, False, False), (b, v("ID"), x, False, False)])
             else:
-                act(u, bs[0], AF.Sign, bias=-15.5)
-                mms([(bs[1], v("N8"), u, False, True)])
-                act(z, bs[1], AF.Identity, bias=-8.0)
+                for b in (("MT", "MF") if s else ("PL", "MG")):
+                    mms([(v(b, 0, HB), v("I16"), xh, True, False)])
 
-        def mixes():
-            mix(1, 0, "MA")
-            mix(1, 1, "MT MF")
-            own(0, 1, "MT MF")
-            if c == 2:
-                mix(0, 1, "MT MF")
-                own(0, 0, "MT")
-                mix(0, 0, "MT MB")
-            else:
-                mix(0, 0, "MB")
-                mix(0, 1, "MT MF")
+        def side(s):
+            x, xq = (v(XI), v("XQ")) if s else (v(YI), v("YQ"))
+            return [x, xq] + [v(b, 0, HB) for b in (("MT", "MA", "MF") if s else ("PL", "MB", "MG"))]
+
+        def landed(s):
+            x, xq, bt, bv, bf = side(s)
+            mms([(bv, v("ID"), x, False, False)])
+
+        def unpack(s):
+            x, xq, bt, bv, bf = side(s)
+            ts(xq, x, 1.0 / 16, 128.46875, A.mult, A.add)
+            mms([(bt, v("ID"), xq, False, True)])
+            mms([(bv, v("N16"), xq, False, True)])
+
+        def test(s):
+            x, xq, bt, bv, bf = side(s)
+            mms([(bf, v("ID"), xq, False, False)])
+            act(v("UU", s * K, s * K + HB), bt, AF.Sign, bias=-143.5625)
+
+        def fold(s):
+            x, xq, bt, bv, bf = side(s)
+            o = s * K
+            mms([(bf, v("N8"), v("UU", o, o + HB), False, True)])
+            ts(v("UU", o + HB, o + K), bv, 15.5, 16.0, A.is_ge, A.mult)
+            tt(v(TB, W + o + HB, W + o + K), bv, v("UU", o + HB, o + K), A.subtract)
+            act(v(TB, W + o, W + o + HB), bf, AF.Identity, bias=-136.0625)
+
+        def owns():
+            for s, h in ((1, 0), (1, 1), (0, 1), (0, 0)) if c < 3 else ((0, 0), (0, 1), (1, 0), (1, 1)):
+                own(s, h)
 
         if c < 3:
-            so = (c - 1) * 104
-            if c == 1:
-                cp(v("ST16"), v("STF"))
-            act(v("FG", K, NL), ind(v("GG"), v("ST16", so + 52, so + 104)), AF.Copy, scale=2.0 ** -12)
-            t1(v("FG", 0, K), ind(v("GG"), v("ST16", so, so + 52)), 2.0 ** -12, A.mult)
             tt(v("DS"), v("STF", so, so + 104), S1, A.subtract)
-            mms([(v("PL", 104, 208), v("ID"), v("CL", 104, 208), True, False)] +
-                [(v("PL", 104, 208), E(E23, b), v("FG", b, None, 16), False, b == 15) for b in range(16)])
-            tt(v("G1"), v("PL", 104, 208), v("SO%d" % c), A.is_lt)
-            jlist()
-            tt(v("G2"), v("G1"), v("DS"), A.mult)
-            tt(v("PV", 384, 488), v("G2"), v("SI%d" % c), A.mult)
+            tt(v("G2"), v(SO), v("DS"), A.mult)
+            cp(v("J16"), PJ)
+            if c == 2:
+                tt(C, C, v("T1"), A.add)
+            mms([(v("PL", 104, 208), v("ID"), v("CL", 104, 208), True, False)])
+            mms([(v("PL", 104, 208), E(E01, b), v("FG", b, None, 16), False, b == 15) for b in range(16)])
+            tt(v("G1"), v("PL", 104, 208), v(SI), A.is_lt)
+            owns()
+            tt(v("PV", 384, 488), v("G2"), v("G1"), A.mult)
             tt(v("DS"), v("PV", 384, 488), S1, A.add)
             cp(v("S16"), v("DS"))
             scatter(c + 1)
-            cp(v("J16"), v("PL", 208, 400))
+            for f in (landed, unpack, test, fold):
+                f(1)
+                f(0)
             if c == 1:
-                mixes()
-                for j, (a, b) in enumerate(((0, 4), (4, 7), (7, 8))):
+                clear(3)
+                stay(2)
+                mms([(C, v("IB"), v("THB"), True, False)])
+                for a, b in ((0, 2), (2, 5), (5, 7), (7, 8)):
                     columns(TB, "TB2", "a", 8 + a, 8 + b)
                     columns(TB, "TB2", "v", a, b)
-                    sums("TB2", range(a, b), j == 0, False)
-                    sums("TB2", range(8 + a, 8 + b), False, j == 2)
-            else:
-                tt(v("T1"), D, v("OC"), A.mult)
-                tt(C, C, v("T1"), A.add)
-                mixes()
+                    sums(C, ES, "TB2", range(a, b), False, False)
+                    sums(C, ES, "TB2", range(8 + a, 8 + b), False, b == 8)
         else:
-            jlist()
+            owns()
+            jlist(0, 8)
             dma("s", hbm(T.ya[:]), v("SS3", 0, 52))
             dma("s", hbm(T.yb[:]), v("SS3", 52, 104))
-            cp(v("J16"), v("PL", 208, 400))
-            mixes()
-            for a, b in ((0, 3), (3, 6), (6, 8)):
-                for who, o in (("a", 8), ("v", 0)):
-                    columns(TB, "YY", who, o + a, o + b)
-                    dma("s", hbm(T.ym[:, Q * (o + a):Q * (o + b)]), v("YY", Q * (o + a), Q * (o + b)))
+            for f in (landed, unpack, test, fold):
+                f(1)
+            jlist(8, 16)
+            landed(0)
+            unpack(0)
+            cp(v("J16"), PJ)
+            test(0)
+            fold(0)
+            for a, m, b in ((0, 2, 4), (4, 7, 10), (10, 13, 16)):
+                columns(TB, "YY", "a", m, b)
+                columns(TB, "YY", "v", a, m)
+                dma("s", hbm(T.ym[:, Q * a:Q * b]), v("YY", Q * a, Q * b))
     for s in SEMAPHORES:
         if count[s]:
             g.sync.wait_ge(T.sem[s], count[s])

@@ -17,7 +17,7 @@ def _b(names, cols, d="float32", where="sbuf"):
 
 _b("TB1 TB2 TB3", W + NL, "bfloat16")
 _b("WL1 WL2 WL3 WR1 WR2 WR3 WW", W)
-_b("GG JW YY U8", W, "bfloat16")
+_b("GG HW YY U8", W, "bfloat16")
 _b("LG", K, "float16")
 _b("FG UU", NL, "bfloat16")
 _b("RG", K, "bfloat16")
@@ -28,7 +28,7 @@ _b("INI", 208, "int32")
 _b("THI COLI", 4, "int32")
 _b("COL", 16)
 _b("ONE ID IB N8 N16 NI I16", 128, "bfloat16")
-_b("BD1 BD", 8, "bfloat16")
+_b("BD1", 8, "bfloat16")
 _b("EE", 3 * 144, "bfloat16")
 _b("EH", 144, "float16")
 _b("CL", 208, "bfloat16")
@@ -37,14 +37,14 @@ _b("DR", 196)
 _b("KQ", 4)
 _b("JK", 624)
 _b("Y1 Z1 U1", 64)
-_b("THB C112 HI LO HJ LJ", Q, "bfloat16")
+_b("THB C112 HI LO H0 L0", Q, "bfloat16")
 _b("ZERO FILL DL DH FN RL AA POS OC T1", Q)
 _b("J16", Q, "uint16")
 _b("S16 P16", 104, "uint16")
 _b("ST16", 208, "uint16")
 _b("STF", 208)
 _b("LI SI32", 104, "int32")
-_b("L1 KO SS1 SS2 SS3 DS G1 G2", 104)
+_b("L1 KO SS1 SS2 SS3 DS G1", 104)
 BANKS = ("PC", "PL", "PV", "MG", "MA", "MB", "MT", "MF")
 _b(" ".join(BANKS), 512, "float32", "psum")
 
@@ -195,7 +195,7 @@ def rank_program(g, core, T, topo):
 
     def col(j):
         return v("COL", j, j + 1)
-    cI192, cNF1, c01, cT1, cX = range(5)
+    cI192, cNF1, c01, cT1, cX, cH, cF = range(7)
     ES, E8, E01 = range(3)
 
     def E(k, b):
@@ -217,28 +217,31 @@ def rank_program(g, core, T, topo):
     act(v("CL", 0, 52), v("ONE", 0, 52), AF.Silu, scale=1536.0)
     dma("s", v("INI", 104, 156), hbm(T.ka[:]))
     dma("s", v("INI", 156, 208), hbm(T.kb[:]))
-    dma("s", v("TB1", 0, W), hbm(T.mk[:]))
     dma("s", v("THI", 0, 1), hbm(T.th[:]))
+    dma("s", v("TB1", 0, W // 2), hbm(T.mk[:, 0:W // 2]))
+    dma("s", v("TB1", W // 2, W), hbm(T.mk[:, W // 2:W]))
     ms(v("EE"), 0.0)
     ms(v("DR", 0, 4), 0.0)
     cI = v("COLI", 1, 2)
     t1(cI, v("COLI", 0, 1), 15, A.bitwise_and)
     t1(col(cI192), cI, 192.0, A.mult)
-    t1(col(c01), cI, 1.5, A.is_lt)
+    ts(col(c01), cI, 1.5, 1 / BIG, A.is_lt, A.mult)
     ts(v("NB", 0, 1), cI, 0.5, 1.0, A.is_ge, A.mult)
     ts(v("NB", 193, 194), cI, 14.5, 1.0, A.is_lt, A.mult)
     ts(v("XM", 193, 194), cI, 14.5, W + 1.0, A.is_ge, A.mult)
     ts(col(cNF1), cI, 0.5, -1.0, A.is_lt, A.mult)
-    ms(v("JK", 560, 624), 0.0)
-    ms(v("Z1"), 0.0)
     iota(v("WK"), [[1, 194]], 1, 0, **small)
-    sel(v("BD1"), v("ONE", 0, 8), [[-16, 8]], A.is_ge, 0, 1)
-    sel(v("BD"), v("BD1"), [[16, 8]], A.is_ge, 15, -1)
+    sel(v("BD1"), v("FILL", 0, 8), [[-16, 8]], A.is_ge, 0, 1)
+    sel(Ecols(ES), v("BD1"), [[16, 8]], A.is_ge, 15, -1)
     sel(v("ID"), v("ONE"), [[-1, 128]], A.is_equal, 0, 1)
     iota(v("GG", 0, W // 2), [[0, W // 2]], 0, 0, **small)
 
-    def scatter(c):
-        act(ind(v("WR%d" % c), v("S16", 52, 104)), v("VAL"), AF.Silu)
+    def scatter(c, between):
+        cut = 30 if between else 52
+        act(ind(v("WR%d" % c), v("S16", 52, 52 + cut)), v("VAL", 0, 16 * cut), AF.Silu)
+        if between:
+            between()
+            act(ind(v("WR%d" % c), v("S16", 52 + cut, 104)), v("VAL", 16 * cut, K), AF.Silu)
         ts(ind(v("WL%d" % c), v("S16", 0, 52)), v("VAL"), -1.0, float(K), A.mult, A.add)
         dma("s", v("DL"), v("WL%d" % c, r=0))
         dma("s", v("DR", 4, 196), v("WR%d" % c, r=0))
@@ -252,48 +255,60 @@ def rank_program(g, core, T, topo):
         dma("s", v("WL%d" % c, r=0), v("WK", 0, Q))
 
     C, D = v("PC", 0, Q), v("MT", 0, Q)
+    KP, MP, KC3 = v("MG", 0, Q), v("MG", Q, 2 * Q), v("PC", Q, 2 * Q)
 
     def sums(out, e, tb, blocks, first, last):
         mms([(out, E(e, b), v(tb, Q * b, Q * (b + 1)), first and b == blocks[0], last and b == blocks[-1]) for b in blocks])
 
     cp(v("S16"), v("INI", 0, 104))
-    scatter(1)
-    act(Ecols(ES), v("BD"), AF.Copy, scale=BIG)
-    sums(C, ES, "TB1", range(16), True, False)
-    t1(v("WK"), v("WK"), col(cI192), A.add)
-    ts(col(cT1), v("THI", 0, 1), -1.0, 1.0, A.mult, A.add)
-    dma("s", v("JW"), hbm(T.mk[:]))
+    scatter(1, None)
+    sums(C, ES, "TB1", range(8), True, False)
+    sums(C, ES, "TB1", range(8, 16), False, False)
+    act(v("WK"), v("WK"), AF.Identity, bias=col(cI192))
+    act(v("MK"), v("WK"), AF.Identity, scale=-1.0, bias=M - 1)
+    dma("s", v("HW", 0, 2304), hbm(T.mk[:, 0:2304]))
     act(v("IB"), v("ID"), AF.Copy, scale=BIG)
+    act(KP, v("WK", 1, Q + 1), AF.Copy)
+    t1(v("L1", 0, 52), v("INI", 104, 156), 2.0, A.mult)
+    tt(v("LI", 0, 52), v("L1", 0, 52), v("INI", 156, 208), A.add)
+    tt(col(cX), v("NB", 0, 1), v("NB", 193, 194), A.mult)
+    tt(v("LI", 52, 104), v("LI", 0, 52), v("INI", 104, 156), A.add)
+    t1(v("SI32"), v("LI"), 1023, A.bitwise_and)
+    ts(v("KO"), v("SI32"), 3.0, 1.0, A.mult, A.add)
+    send([(up, down, v("STF", 104, 208), v("KO"), "rk")])
+    ts(col(cT1), v("THI", 0, 1), -1.0, 1.0, A.mult, A.add)
     act(v("THB"), v("ZERO"), AF.Identity, bias=col(cT1))
     mms([(C, v("IB"), v("THB"), False, True)])
-    act(v("MG", 0, Q), v("WK", 1, Q + 1), AF.Copy)
-    for o, c in ((0, 2), (52, 3)):
-        t1(v("L1", o, o + 52), v("INI", 104, 156), float(c), A.mult)
-    ts(v("MK"), v("WK"), -1.0, M - 1, A.mult, A.add)
-    for o in (0, 52):
-        tt(v("LI", o, o + 52), v("L1", o, o + 52), v("INI", 156, 208), A.add)
-    tt(col(cX), v("NB", 0, 1), v("NB", 193, 194), A.mult)
-    t1(v("SI32"), v("LI"), 1023, A.bitwise_and)
-    ts(v("KQ"), v("ONE", 0, 4), v("MK", 0, 1), col(cX), A.mult, A.mult)
-    ts(v("KO"), v("SI32"), 3.0, 1.0, A.mult, A.add)
-    send([(up, down, v("STF", 2 * o + 52, 2 * o + 104), v("KO", o, o + 52), "rk") for o in (0, 52)])
+    iota(v("GG", 2304, W), [[0, 768]], 0, 0, **small)
+    iota(v("HW", 2304, W), [[0, 768]], 0, 0, **small)
+    iota(v("POS"), [[16, Q]], 0, 0, **small)
+    ms(v("JK", 560, 624), 0.0)
+    ms(v("Z1"), 0.0)
+    ts(col(cH), cI, 0.5, 2.0 ** -12, A.is_lt, A.mult)
+    cp(col(cF), cI)
     ms(v("EH"), 0.0)
-    ms(v("CL", 52, 104), -2.0)
-    cp(v("EH", 15, 143, 16), v("BD"))
+    ts(v("KQ"), v("ONE", 0, 4), v("MK", 0, 1), col(cX), A.mult, A.mult)
+    t1(v("EH", 15, 143, 16), Ecols(ES), 1 / BIG, A.mult)
+    act(MP, v("MK", 0, Q), AF.Copy)
     blank("WW", 0, 4)
-    blank("GG", 2, 4)
-    act(v("POS"), v("WK", 0, Q), AF.Identity, bias=-1.0)
-    act(Ecols(E01), v("BD"), AF.Copy, scale=col(c01))
+    blank("GG", 2, 3)
+    act(Ecols(E01), Ecols(ES), AF.Copy, scale=col(c01))
+    act(v("CL", 52, 104), v("ZERO", 0, 52), AF.Identity, bias=-2.0)
 
     def constants():
-        act(v("PC", Q, 2 * Q), v("WK", 1, Q + 1), AF.Copy)
-        act(Ecols(E8), v("BD"), AF.Copy, scale=-8 * BIG)
-        for x, k in (("N8", -8.0), ("N16", -16.0), ("NI", -1.0), ("I16", 1.0 / 16)):
-            act(v(x), v("ID"), AF.Copy, scale=k)
-        act(v("CT"), v("VAL", 0, HB), AF.Identity, scale=0.0, bias=2064.0)
-        act(v("C112"), v("ZERO"), AF.Identity, bias=-112.0)
+        act(v("STF", 0, 104), v("KO"), AF.Identity, bias=-1.0)
         act(v("CL", 104, 208), v("ZERO", 0, 104), AF.Identity, bias=0.25)
-        clear(2)
+        act(v("CT"), v("VAL", 0, HB), AF.Identity, scale=0.0, bias=2064.0)
+        for x, k in (("NI", -1.0), ("I16", 1.0 / 16)):
+            act(v(x), v("ID"), AF.Copy, scale=k)
+
+    def constants2():
+        for x, k in (("N8", -8.0), ("N16", -16.0)):
+            act(v(x), v("ID"), AF.Copy, scale=k)
+        act(v("POS"), v("POS"), AF.Identity, bias=col(cF))
+        act(KC3, v("WK", 1, Q + 1), AF.Copy)
+        act(Ecols(E8), Ecols(ES), AF.Copy, scale=-8.0)
+        act(v("C112"), v("ZERO"), AF.Identity, bias=-112.0)
 
     p1, p2 = v("PV", 0, Q), v("PV", Q, 2 * Q)
     DRv = v("DR", 4, 196)
@@ -305,26 +320,25 @@ def rank_program(g, core, T, topo):
         else:
             act(v(out, Q * a, Q * b), src, AF.Copy)
 
-    def stay(c):
-        tt(p2, DRv, v("MG", 0, Q) if c == 1 else v("PC", Q, 2 * Q), A.min)
+    def stay(keys):
+        tt(p2, DRv, keys, A.min)
 
     for c in (1, 2, 3):
         XP, XI, YP, YI = "XP%d" % c, "XI%d" % c, "YP%d" % c, "YI%d" % c
         TB = "TB%d" % c
         if c == 1:
             tt(v("DH"), v("DL"), v("WK", 0, Q), A.min)
-        tt(p1, C, DRv, A.max)
+        tt(p1, C if c < 3 else p1, DRv, A.max)
         if c == 2:
+            act(MP, v("MK", 0, Q), AF.Copy)
             act(v("U8"), v(TB, 0, W), AF.Sign, bias=-7.5)
             mms([(D, v("IB"), v("C112"), True, False)])
             sums(D, ES, TB, range(16), False, False)
             sums(D, E8, "U8", range(16), False, True)
         if c == 3:
             columns("TB2", TB, "a", 0, 8)
-        if c != 2:
-            stay(c)
+        tt(v("NB", 1, 193), p1, v("DH" if c == 1 else "DL"), A.is_lt)
         tt(v("XM", 1, 193), p1, v("DH" if c == 1 else "DL"), A.min)
-        t1(v("NB", 1, 193), v("XM", 1, 193), 0.0, A.is_equal)
         scan(v("JK", 0, 579, 3), v("NB", 0, 193), v("MK", 0, 193), 0.0, A.mult, A.max)
         scan(v("JK", 2, 579, 3), v("NB", 193, 0, -1), v("XM", 193, 0, -1), 0.0, A.mult, A.add)
         t1(v("JK", 608, 611), v("KQ", 0, 3), v("JK", 576, 577), A.is_equal)
@@ -333,6 +347,8 @@ def rank_program(g, core, T, topo):
         scan(v("Z1", 62, 31, -1), v("Y1", 63, 32, -1), v("Y1", 31, 0, -1), 0.0, A.mult, A.add)
         scan(v("Z1", 1, 32), v("Y1", 32, 63), v("Y1", 0, 31), 0.0, A.mult, A.max)
         tr(v("U1"), v("Z1"))
+        if c != 2:
+            stay(KP if c == 1 else KC3)
         scan(v("GI", 193, 0, -1), v("NB", 193, 0, -1), v("XM", 193, 0, -1), v("U1", 50, 51), A.mult, A.add)
         scan(v("FN"), v("NB", 0, Q), v("MK", 0, Q), v("U1", 16, 17), A.mult, A.max)
         tt(p1, v("GI", 2, 194), p2, A.max)
@@ -347,58 +363,75 @@ def rank_program(g, core, T, topo):
         if c == 1:
             constants()
         if c == 3:
-            columns("TB2", TB, "a", 8, 16)
+            columns("TB2", TB, "a", 8, 15)
 
         scan(v("PR", 0, 193), v("NB", 0, 193), v("DR", 3, 196), v("U1", 17, 18), A.mult, A.max)
         tt(p2, p1, v("WK", 1, 193), A.is_equal)
-        tt(p1, v("FN"), v("MK", 0, Q), A.is_equal)
+        tt(p1, v("FN"), MP if c < 3 else v("MK", 0, Q), A.is_equal)
         tt(v("AA"), p2, v("PR", 1, 193), A.mult)
         tt(p1, p1, v("RL"), A.mult)
         tt(p1, p1, v("AA"), A.max)
-        tt(p2, p1, v("POS"), A.max)
+        if c < 3:
+            act(v("H0"), p1, AF.Copy)
+            dma("s", v("HW", r=0), v("H0"))
 
-        so = (c - 1) * 104
+        so = (c - 1) * 52
         ts(v("LG"), ind(v("WW"), v("S16", 0, 52)), M - 1538, col(cNF1), A.subtract, A.mult)
         act(v("RG"), ind(v("GG"), v("S16", 52, 104)), AF.Copy)
         mms([(PA, v("EH", 15 - b, 143 - b), v("LG", b, None, 16), False, b == 15) for b in range(16)])
         mms([(PB, E(E01, b), v("RG", b, None, 16), False, b == 15) for b in range(16)])
-        cp(v("HJ"), p2)
-        dma("s", v("JW", r=0), v("HJ"))
-        tt(v("LJ"), p2, v("HJ"), A.subtract)
-        dma("s", v("JW", r=1), v("LJ"))
-        PJ = v("MG" if c < 3 else "PC", 0, Q)
+        if c == 3:
+            cp(v("H0"), p1)
+            dma("s", v("HW", r=0), v("H0"))
+        tt(v("L0"), p1, v("H0"), A.subtract)
+        if c == 3:
+            dma("s", v("HW", r=1), v("L0"))
+            columns("TB2", TB, "v", 15, 16)
+        if c == 1:
+            clear(2)
 
         def jlist(a, b):
-            mms([(PJ, E(E01, x), v("JW", x, None, 16), x == 0, x == 15) for x in range(a, b)])
-        if c < 3:
-            jlist(0, 16)
-        if c == 1:
-            for o in (0, 52):
-                t1(v("STF", 2 * o, 2 * o + 52), v("SI32", o, o + 52), 3.0, A.mult)
-            cp(v("ST16"), v("STF"))
-        if c == 2:
-            t1(v("OC"), p2, W - 0.5, A.is_ge)
-            tt(v("T1"), D, v("OC"), A.mult)
+            mms([(C, E(E01, x), v("HW", x, None, 16), x == 0, x == 15) for x in range(a, b)])
+
+        def numbers():
+            tt(v("T1"), C, v("POS"), A.max)
+            cp(v("J16"), v("T1"))
+
+        def held(who, a, b):
+            src = ind(v("HW"), v("ST16", so + 2 * a, so + a + b))
+            if who == "v":
+                t1(v("FG", 16 * a, 16 * b), src, col(cH), A.mult)
+            else:
+                act(v("FG", 16 * a, 16 * b), src, AF.Copy, scale=col(cH))
         S0, S1 = ("INI" if c == 1 else "SS%d" % (c - 1)), "SS%d" % c
         SO, SI = "SO%d" % c, "SI%d" % c
         tab = v(TB, 0, W)
-
+        if c == 1:
+            cp(v("ST16"), v("STF"))
+        if c < 3:
+            held("a", 52, 104)
         cp(v("P16", 0, 52), PA)
         act(v("XH"), ind(tab, v("P16", 0, 26)), AF.Identity, scale=16.0, bias=1.0)
         if c < 3:
             tt(v(SO, 0, 52), PA, v(S0, 0, 52), A.is_equal)
-        cp(v(S1, 0, 52), PA)
-        if c < 3:
+            cp(v(S1, 0, 52), PA)
             tt(v(SO, 52, 104), PB, v(S0, 52, 104), A.is_equal)
             send([(up, down, v(SI, 52, 104), v(SO, 0, 52), "ra%d" % c), (down, up, v(SI, 0, 52), v(SO, 52, 104), "rs%d" % c)])
         cp(v("P16", 52, 104), PB)
         act(v("YH"), ind(tab, v("P16", 52, 78)), AF.Identity, scale=16.0, bias=1.0)
-        cp(v(S1, 52, 104), PB)
+        if c == 3:
+            cp(v(S1, 0, 52), PA)
+            cp(v(S1, 52, 104), PB)
+        if c == 1:
+            constants2()
+        if c == 2:
+            act(v("OC"), v("H0"), AF.Sign)
+        if c < 3:
+            cp(v(S1, 52, 104), PB)
+            held("v", 0, 52)
+            dma("s", v("HW", r=1), v("L0"))
         tt(v(XP), ind(tab, v("P16", 26, 52)), v("XH"), A.add)
         send([(up, down, v(XI), v(XP), "rx%d" % c)])
-        if c < 3:
-            act(v("FG", K, NL), ind(v("JW"), v("ST16", so + 52, so + 104)), AF.Copy, scale=2.0 ** -12)
-            t1(v("FG", 0, K), ind(v("JW"), v("ST16", so, so + 52)), 2.0 ** -12, A.mult)
         tt(v(YP), ind(tab, v("P16", 78, 104)), v("YH"), A.add)
         send([(down, up, v(YI), v(YP), "ry%d" % c)])
         S1 = v(S1)
@@ -414,78 +447,96 @@ def rank_program(g, core, T, topo):
 
         def side(s):
             x, xq = (v(XI), v("XQ")) if s else (v(YI), v("YQ"))
-            return [x, xq] + [v(b, 0, HB) for b in (("MT", "MA", "MF") if s else ("PL", "MB", "MG"))]
+            return [x, xq] + [v(b, 0, HB) for b in (("MT", "MF", "MA") if s else ("PL", "MG", "MB"))]
 
         def landed(s):
-            x, xq, bt, bv, bf = side(s)
-            mms([(bv, v("ID"), x, False, False)])
+            x, xq, bt, b0, b1 = side(s)
+            mms([(b1, v("ID"), x, False, False)])
 
-        def unpack(s):
-            x, xq, bt, bv, bf = side(s)
-            ts(xq, x, 1.0 / 16, 128.46875, A.mult, A.add)
-            mms([(bt, v("ID"), xq, False, True)])
-            mms([(bv, v("N16"), xq, False, True)])
+        def quot(s):
+            x, xq, bt, b0, b1 = side(s)
+            if s and c < 3:
+                act(xq, x, AF.Identity, scale=1.0 / 16, bias=128.46875)
+            else:
+                ts(xq, x, 1.0 / 16, 128.46875, A.mult, A.add)
 
         def test(s):
-            x, xq, bt, bv, bf = side(s)
-            mms([(bf, v("ID"), xq, False, False)])
+            x, xq, bt, b0, b1 = side(s)
+            mms([(bt, v("ID"), xq, False, True)])
             act(v("UU", s * K, s * K + HB), bt, AF.Sign, bias=-143.5625)
+            mms([(b1, v("N16"), xq, False, True)])
+            mms([(b0, v("ID"), xq, False, False)])
 
         def fold(s):
-            x, xq, bt, bv, bf = side(s)
+            x, xq, bt, b0, b1 = side(s)
             o = s * K
-            mms([(bf, v("N8"), v("UU", o, o + HB), False, True)])
-            ts(v("UU", o + HB, o + K), bv, 15.5, 16.0, A.is_ge, A.mult)
-            tt(v(TB, W + o + HB, W + o + K), bv, v("UU", o + HB, o + K), A.subtract)
-            act(v(TB, W + o, W + o + HB), bf, AF.Identity, bias=-136.0625)
+            mms([(b0, v("N8"), v("UU", o, o + HB), False, True)])
+            act(v(TB, W + o, W + o + HB), b0, AF.Identity, bias=-136.0625)
 
-        def owns():
-            for s, h in ((1, 0), (1, 1), (0, 1), (0, 0)) if c < 3 else ((0, 0), (0, 1), (1, 0), (1, 1)):
-                own(s, h)
+        def high(s, between=lambda: None):
+            x, xq, bt, b0, b1 = side(s)
+            o = s * K
+            ts(v("UU", o + HB, o + K), b1, 15.5, 16.0, A.is_ge, A.mult)
+            between()
+            tt(v(TB, W + o + HB, W + o + K), b1, v("UU", o + HB, o + K), A.subtract)
 
         if c < 3:
-            tt(v("DS"), v("STF", so, so + 104), S1, A.subtract)
-            tt(v("G2"), v(SO), v("DS"), A.mult)
-            cp(v("J16"), PJ)
+            for o in (0, 52):
+                tt(v("DS", o, o + 52), v("STF", so + 2 * o, so + 2 * o + 52), v("SS%d" % c, o, o + 52), A.subtract)
             if c == 2:
-                tt(C, C, v("T1"), A.add)
+                tt(v("T1"), D, v("OC"), A.mult)
+                tt(p1, C, v("T1"), A.add)
             mms([(v("PL", 104, 208), v("ID"), v("CL", 104, 208), True, False)])
             mms([(v("PL", 104, 208), E(E01, b), v("FG", b, None, 16), False, b == 15) for b in range(16)])
-            tt(v("G1"), v("PL", 104, 208), v(SI), A.is_lt)
-            owns()
-            tt(v("PV", 384, 488), v("G2"), v("G1"), A.mult)
+            tt(v("G1"), v("PL", 104, 208), v(SO), A.is_lt)
+            for s, h in ((0, 1), (1, 1), (1, 0), (0, 0)):
+                own(s, h)
+            jlist(0, 10)
+            tt(v("PV", 384, 488), v("G1"), v("DS"), A.mult)
+            tt(v("PV", 384, 488), v("PV", 384, 488), v(SI), A.mult)
             tt(v("DS"), v("PV", 384, 488), S1, A.add)
             cp(v("S16"), v("DS"))
-            scatter(c + 1)
-            for f in (landed, unpack, test, fold):
-                f(1)
-                f(0)
+            landed(1)
+            scatter(c + 1, lambda: quot(1))
+            test(1)
+            high(1, lambda: quot(0))
+            jlist(10, 16)
+            landed(0)
+            test(0)
+            fold(1)
+            numbers()
+            high(0)
+            fold(0)
             if c == 1:
                 clear(3)
-                stay(2)
                 mms([(C, v("IB"), v("THB"), True, False)])
-                for a, b in ((0, 2), (2, 5), (5, 7), (7, 8)):
+                for a, b in ((0, 1), (1, 3), (3, 5), (5, 7), (7, 8)):
                     columns(TB, "TB2", "a", 8 + a, 8 + b)
                     columns(TB, "TB2", "v", a, b)
                     sums(C, ES, "TB2", range(a, b), False, False)
                     sums(C, ES, "TB2", range(8 + a, 8 + b), False, b == 8)
+                stay(v("WK", 1, Q + 1))
         else:
-            owns()
-            jlist(0, 8)
+            for s, h in ((0, 0), (1, 0), (0, 1), (1, 1)):
+                own(s, h)
+            jlist(0, 13)
             dma("s", hbm(T.ya[:]), v("SS3", 0, 52))
             dma("s", hbm(T.yb[:]), v("SS3", 52, 104))
-            for f in (landed, unpack, test, fold):
-                f(1)
-            jlist(8, 16)
+            landed(1)
+            quot(1)
+            test(1)
+            high(1, lambda: quot(0))
+            fold(1)
+            jlist(13, 16)
             landed(0)
-            unpack(0)
-            cp(v("J16"), PJ)
             test(0)
+            numbers()
+            high(0)
             fold(0)
             for a, m, b in ((0, 2, 4), (4, 7, 10), (10, 13, 16)):
                 columns(TB, "YY", "a", m, b)
                 columns(TB, "YY", "v", a, m)
                 dma("s", hbm(T.ym[:, Q * a:Q * b]), v("YY", Q * a, Q * b))
-    for s in SEMAPHORES:
-        if count[s]:
+    for s in sorted(SEMAPHORES, key=lambda x: x[0] == "d"):
+        if known["s"].get(s, 0) < count[s]:
             g.sync.wait_ge(T.sem[s], count[s])

from concourse.bass import DstId, RemoteDMATransfer
from concourse.mybir import AluOpType, ActivationFunctionType

W, K, KC, Q = 3072, 832, 52, 192
NL = 2 * K
HB = 416
BIG = 8192.0
M = 4098.0

SCRATCH = {}


def _b(names, cols, d="float32", where="sbuf"):
    for x in names.split():
        SCRATCH[x] = (where, [128, cols], d)


_b("TB1 TB2 TB3", W + NL, "bfloat16")
_b("WL1 WL2 WL3 WR1 WR2 WR3 WW", W)
_b("GG HW YY U8", W, "bfloat16")
_b("LG", K, "float16")
_b("FG UU", NL, "bfloat16")
_b("RG", K, "bfloat16")
_b("XI1 XI2 XI3 YI1 YI2 YI3 XP1 XP2 XP3 YP1 YP2 YP3 XH YH XQ YQ CT", HB, "bfloat16")
_b("SO1 SO2 SI1 SI2", 2 * KC, "bfloat16")
_b("VAL", K)
_b("INI", 208, "int32")
_b("THI COLI", 4, "int32")
_b("COL", 16)
_b("ONE ID IB N8 N16 NI I16", 128, "bfloat16")
_b("BD1", 8, "bfloat16")
_b("EE", 3 * 144, "bfloat16")
_b("EH", 144, "float16")
_b("CL", 208, "bfloat16")
_b("WK MK NB XM GI PR", 194)
_b("DR", 196)
_b("KQ", 4)
_b("JK", 624)
_b("Y1 Z1 U1", 64)
_b("THB C112 HI LO H0 L0", Q, "bfloat16")
_b("ZERO FILL DL DH FN RL AA POS OC T1", Q)
_b("J16", Q, "uint16")
_b("S16 P16", 104, "uint16")
_b("ST16", 208, "uint16")
_b("STF", 208)
_b("LI SI32", 104, "int32")
_b("L1 KO SS1 SS2 SS3 DS G1", 104)
BANKS = ("PC", "PL", "PV", "MG", "MA", "MB", "MT", "MF")
_b(" ".join(BANKS), 512, "float32", "psum")

NDMA = 48
SEMAPHORES = ["qv", "qa", "qt", "qg", "sent"] + ["d%d" % i for i in range(NDMA)] + \
    ["rk", "ra1", "ra2", "rs1", "rs2", "rx1", "rx2", "rx3", "ry1", "ry2", "ry3"]

A = AluOpType
AF = ActivationFunctionType


def rank_program(g, core, T, topo):
    rank = T.rank_of(core)
    if rank is None:
        return
    n = len(T.cores)
    up, down = T.cores[(rank + 2) % n], T.cores[(rank - 2) % n]
    eng = {"v": g.vector, "a": g.scalar, "t": g.tensor, "g": g, "s": g.sync}
    qsem = {"v": "qv", "a": "qa", "t": "qt", "g": "qg"}
    count = {s: 0 for s in SEMAPHORES}
    known = {q: {} for q in eng}
    hist = {}
    ndma = [0]

    def v(name, a=None, b=None, s=None, r=None):
        cols = range(*slice(a, b, s).indices(SCRATCH[name][1][1]))
        ap = T[name][slice(None) if r is None else slice(r, None, 16), slice(a, b, s)]
        return (ap, [(name, min(cols), max(cols) + 1, abs(s or 1), r)])

    def ind(win, off):
        return (win[0].indirect(off[0]), win[1], off[1])

    def meet(x, y):
        if x[1] >= y[2] or y[1] >= x[2]:
            return False
        if x[4] is not None and y[4] is not None and x[4] != y[4]:
            return False
        return not (x[3] == y[3] and (x[1] - y[1]) % x[3])

    def need(q, ev):
        sem, val, src, snap = ev
        if known[q].get(sem, 0) >= val or (q == "t" and src == "t"):
            return
        eng[q].wait_ge(T.sem[sem], val)
        for s, x in snap.items():
            if known[q].get(s, 0) < x:
                known[q][s] = x
        known[q][sem] = val

    def regions(outs, ins):
        w = [x for o in outs for x in o[1]]
        r = [x for o in ins if isinstance(o, tuple) for x in o[1]]
        r += [x for o in list(outs) + list(ins) if isinstance(o, tuple) and len(o) > 2 for x in o[2]]
        return r, w

    def sync(q, r, w):
        evs = []
        for xs, wr in ((r, False), (w, True)):
            for x in xs:
                for y, ev, yw in hist.get(x[0], []):
                    if (x[0] in BANKS and ev[2] != q) or ((wr or yw) and meet(x, y)):
                        evs.append(ev)
        evs.sort(key=lambda ev: -ev[1])
        for ev in evs:
            need(q, ev)

    def done(ev, r, w):
        for xs, wr in ((r, False), (w, True)):
            for x in xs:
                hist.setdefault(x[0], []).append((x, ev, wr))

    def ap(x):
        return x[0] if isinstance(x, tuple) else x

    def op(q, fn, outs, ins):
        r, w = regions(outs, ins)
        sync(q, r, w)
        ins_ = fn()
        s = qsem[q]
        count[s] += 1
        ins_.then_inc(T.sem[s], 1)
        done((s, count[s], q, dict(known[q])), r, w)

    def hbm(x):
        return (x, [])

    def dma(q, out, in_):
        r, w = regions([out], [in_])
        sync(q, r, w)
        s = "d%d" % ndma[0]
        ndma[0] += 1
        eng[q].dma_start(out[0], in_[0]).then_inc(T.sem[s], 16)
        count[s] = 16
        done((s, 16, "dma", dict(known[q])), r, w)

    def send(trs):
        sync("g", [x for t in trs for x in t[3][1]], [])
        lst = []
        for j, (dst, src, out, in_, sem) in enumerate(trs):
            rid, pid = topo.addr(dst, core)
            es = topo.engines(core, dst)
            es = es[j * len(es) // len(trs):(j + 1) * len(es) // len(trs)]
            lst.append(RemoteDMATransfer(dst_ids=[DstId(rid=rid, pnc=pid)], dma_engine_mask=sum(1 << e for e in es),
                                         remote_sem=T.sem[sem], src=in_[0], dst=out[0]))
            count["sent"] += len(es)
            count[sem] += len(topo.engines(src, core)) // len(trs)
        g.remote_dma_fused(lst, local_sem=T.sem["sent"])
        for dst, src, out, in_, sem in trs:
            done((sem, count[sem], "dma", {}), [], out[1])

    def mms(lst):
        def fn():
            for o, l, r, st, sp in lst:
                ins_ = g.tensor.matmul(o[0], l[0], r[0], st, sp)
            return ins_
        op("t", fn, [x[0] for x in lst], [x[1] for x in lst] + [x[2] for x in lst])

    def ts(out, in0, s1, s2, o0, o1):
        op("v", lambda: g.vector.tensor_scalar(out[0], in0[0], ap(s1), ap(s2), o0, o1), [out], [in0, s1, s2])

    def t1(out, in0, s1, o0):
        op("v", lambda: g.vector.tensor_scalar(out[0], in0[0], ap(s1), None, o0), [out], [in0, s1])

    def tt(out, in0, in1, o):
        op("v", lambda: g.vector.tensor_tensor(out[0], in0[0], in1[0], o), [out], [in0, in1])

    def cp(out, in_):
        op("v", lambda: g.vector.tensor_copy(out[0], in_[0]), [out], [in_])

    def ms(out, val):
        op("v", lambda: g.vector.memset(out[0], val), [out], [])

    def scan(out, d0, d1, init, o0, o1):
        op("v", lambda: g.vector.tensor_tensor_scan(out[0], d0[0], d1[0], ap(init), o0, o1), [out], [d0, d1, init])

    def tr(out, in_):
        op("v", lambda: g.vector.transpose(out[0], in_[0]), [out], [in_])

    def act(out, in_, f, **kw):
        op("a", lambda: g.scalar.activation(out[0], in_[0], f, **{k: ap(x) for k, x in kw.items()}), [out],
           [in_] + list(kw.values()))

    def iota(out, pat, base, cm, **kw):
        op("g", lambda: g.iota(out[0], pat, base, cm, **kw), [out], [])

    def sel(out, in_, pat, o, base, cm):
        op("g", lambda: g.affine_select(out[0], in_[0], pat, o, 0.0, base, cm), [out], [in_])

    def col(j):
        return v("COL", j, j + 1)
    cI192, cNF1, c01, cT1, cX, cH, cF = range(7)
    ES, E8, E01 = range(3)

    def E(k, b):
        return v("EE", 144 * k + 15 - b, 144 * k + 143 - b)

    def Ecols(k):
        return v("EE", 144 * k + 15, 144 * k + 143, 16)

    small = dict(allow_small_or_imprecise_dtypes=True)
    dma("s", v("INI", 52, 104), hbm(T.lb[:]))
    dma("a", v("INI", 0, 52), hbm(T.la[:]))
    ms(v("FILL"), BIG)
    dma("a", v("WL1", r=0), v("FILL"))
    ms(v("ZERO"), 0.0)
    dma("s", v("WR1", r=0), v("ZERO"))
    ms(v("ONE"), 1.0)
    iota(v("COLI", 0, 1), [[0, 1]], 0, 1)
    iota(v("VAL"), [[1, K]], W + K, 0, **small)
    act(v("CL", 0, 52), v("ONE", 0, 52), AF.Silu, scale=1536.0)
    dma("s", v("INI", 104, 156), hbm(T.ka[:]))
    dma("s", v("INI", 156, 208), hbm(T.kb[:]))
    dma("s", v("THI", 0, 1), hbm(T.th[:]))
    dma("s", v("TB1", 0, W // 2), hbm(T.mk[:, 0:W // 2]))
    dma("s", v("TB1", W // 2, W), hbm(T.mk[:, W // 2:W]))
    ms(v("EE"), 0.0)
    ms(v("DR", 0, 4), 0.0)
    cI = v("COLI", 1, 2)
    t1(cI, v("COLI", 0, 1), 15, A.bitwise_and)
    t1(col(cI192), cI, 192.0, A.mult)
    ts(col(c01), cI, 1.5, 1 / BIG, A.is_lt, A.mult)
    ts(v("NB", 0, 1), cI, 0.5, 1.0, A.is_ge, A.mult)
    ts(v("NB", 193, 194), cI, 14.5, 1.0, A.is_lt, A.mult)
    ts(v("XM", 193, 194), cI, 14.5, W + 1.0, A.is_ge, A.mult)
    ts(col(cNF1), cI, 0.5, -1.0, A.is_lt, A.mult)
    iota(v("WK"), [[1, 194]], 1, 0, **small)
    sel(v("BD1"), v("FILL", 0, 8), [[-16, 8]], A.is_ge, 0, 1)
    sel(Ecols(ES), v("BD1"), [[16, 8]], A.is_ge, 15, -1)
    sel(v("ID"), v("ONE"), [[-1, 128]], A.is_equal, 0, 1)
    iota(v("GG", 0, W // 2), [[0, W // 2]], 0, 0, **small)

    def scatter(c, between):
        cut = 30 if between else 52
        act(ind(v("WR%d" % c), v("S16", 52, 52 + cut)), v("VAL", 0, 16 * cut), AF.Silu)
        if between:
            between()
            act(ind(v("WR%d" % c), v("S16", 52 + cut, 104)), v("VAL", 16 * cut, K), AF.Silu)
        ts(ind(v("WL%d" % c), v("S16", 0, 52)), v("VAL"), -1.0, float(K), A.mult, A.add)
        dma("s", v("DL"), v("WL%d" % c, r=0))
        dma("s", v("DR", 4, 196), v("WR%d" % c, r=0))

    def blank(name, a, b):
        for j in range(a, b):
            act(v(name, 768 * j, 768 * (j + 1)), v("VAL", 0, 768), AF.Copy, scale=0.0)

    def clear(c):
        dma("s", v("WR%d" % c, r=0), v("ZERO"))
        dma("s", v("WL%d" % c, r=0), v("WK", 0, Q))

    C, D = v("PC", 0, Q), v("MT", 0, Q)
    KP, MP, KC3 = v("MG", 0, Q), v("MG", Q, 2 * Q), v("PC", Q, 2 * Q)

    def sums(out, e, tb, blocks, first, last):
        mms([(out, E(e, b), v(tb, Q * b, Q * (b + 1)), first and b == blocks[0], last and b == blocks[-1]) for b in blocks])

    cp(v("S16"), v("INI", 0, 104))
    scatter(1, None)
    sums(C, ES, "TB1", range(8), True, False)
    sums(C, ES, "TB1", range(8, 16), False, False)
    act(v("WK"), v("WK"), AF.Identity, bias=col(cI192))
    act(v("MK"), v("WK"), AF.Identity, scale=-1.0, bias=M - 1)
    dma("s", v("HW", 0, 2304), hbm(T.mk[:, 0:2304]))
    act(v("IB"), v("ID"), AF.Copy, scale=BIG)
    act(KP, v("WK", 1, Q + 1), AF.Copy)
    t1(v("L1", 0, 52), v("INI", 104, 156), 2.0, A.mult)
    tt(v("LI", 0, 52), v("L1", 0, 52), v("INI", 156, 208), A.add)
    tt(col(cX), v("NB", 0, 1), v("NB", 193, 194), A.mult)
    tt(v("LI", 52, 104), v("LI", 0, 52), v("INI", 104, 156), A.add)
    t1(v("SI32"), v("LI"), 1023, A.bitwise_and)
    ts(v("KO"), v("SI32"), 3.0, 1.0, A.mult, A.add)
    send([(up, down, v("STF", 104, 208), v("KO"), "rk")])
    ts(col(cT1), v("THI", 0, 1), -1.0, 1.0, A.mult, A.add)
    act(v("THB"), v("ZERO"), AF.Identity, bias=col(cT1))
    mms([(C, v("IB"), v("THB"), False, True)])
    iota(v("GG", 2304, W), [[0, 768]], 0, 0, **small)
    iota(v("HW", 2304, W), [[0, 768]], 0, 0, **small)
    iota(v("POS"), [[16, Q]], 0, 0, **small)
    ms(v("JK", 560, 624), 0.0)
    ms(v("Z1"), 0.0)
    ts(col(cH), cI, 0.5, 2.0 ** -12, A.is_lt, A.mult)
    cp(col(cF), cI)
    ms(v("EH"), 0.0)
    ts(v("KQ"), v("ONE", 0, 4), v("MK", 0, 1), col(cX), A.mult, A.mult)
    t1(v("EH", 15, 143, 16), Ecols(ES), 1 / BIG, A.mult)
    act(MP, v("MK", 0, Q), AF.Copy)
    blank("WW", 0, 4)
    blank("GG", 2, 3)
    act(Ecols(E01), Ecols(ES), AF.Copy, scale=col(c01))
    act(v("CL", 52, 104), v("ZERO", 0, 52), AF.Identity, bias=-2.0)

    def constants():
        act(v("STF", 0, 104), v("KO"), AF.Identity, bias=-1.0)
        act(v("CL", 104, 208), v("ZERO", 0, 104), AF.Identity, bias=0.25)
        act(v("CT"), v("VAL", 0, HB), AF.Identity, scale=0.0, bias=2064.0)
        for x, k in (("NI", -1.0), ("I16", 1.0 / 16)):
            act(v(x), v("ID"), AF.Copy, scale=k)

    def constants2():
        for x, k in (("N8", -8.0), ("N16", -16.0)):
            act(v(x), v("ID"), AF.Copy, scale=k)
        act(v("POS"), v("POS"), AF.Identity, bias=col(cF))
        act(KC3, v("WK", 1, Q + 1), AF.Copy)
        act(Ecols(E8), Ecols(ES), AF.Copy, scale=-8.0)
        act(v("C112"), v("ZERO"), AF.Identity, bias=-112.0)

    p1, p2 = v("PV", 0, Q), v("PV", Q, 2 * Q)
    DRv = v("DR", 4, 196)

    def columns(tb, out, who, a, b):
        src = ind(v(tb), v("J16", 12 * a, 12 * b))
        if who == "v":
            cp(v(out, Q * a, Q * b), src)
        else:
            act(v(out, Q * a, Q * b), src, AF.Copy)

    def stay(keys):
        tt(p2, DRv, keys, A.min)

    for c in (1, 2, 3):
        XP, XI, YP, YI = "XP%d" % c, "XI%d" % c, "YP%d" % c, "YI%d" % c
        TB = "TB%d" % c
        if c == 1:
            tt(v("DH"), v("DL"), v("WK", 0, Q), A.min)
        tt(p1, C if c < 3 else p1, DRv, A.max)
        if c == 2:
            act(MP, v("MK", 0, Q), AF.Copy)
            act(v("U8"), v(TB, 0, W), AF.Sign, bias=-7.5)
            mms([(D, v("IB"), v("C112"), True, False)])
            sums(D, ES, TB, range(16), False, False)
            sums(D, E8, "U8", range(16), False, True)
        if c == 3:
            columns("TB2", TB, "a", 0, 8)
        tt(v("NB", 1, 193), p1, v("DH" if c == 1 else "DL"), A.is_lt)
        tt(v("XM", 1, 193), p1, v("DH" if c == 1 else "DL"), A.min)
        scan(v("JK", 0, 579, 3), v("NB", 0, 193), v("MK", 0, 193), 0.0, A.mult, A.max)
        scan(v("JK", 2, 579, 3), v("NB", 193, 0, -1), v("XM", 193, 0, -1), 0.0, A.mult, A.add)
        t1(v("JK", 608, 611), v("KQ", 0, 3), v("JK", 576, 577), A.is_equal)
        scan(v("JK", 1, 579, 3), v("NB", 0, 193), v("DR", 3, 196), 0.0, A.mult, A.max)
        tr(v("Y1"), v("JK", 560, 624))
        scan(v("Z1", 62, 31, -1), v("Y1", 63, 32, -1), v("Y1", 31, 0, -1), 0.0, A.mult, A.add)
        scan(v("Z1", 1, 32), v("Y1", 32, 63), v("Y1", 0, 31), 0.0, A.mult, A.max)
        tr(v("U1"), v("Z1"))
        if c != 2:
            stay(KP if c == 1 else KC3)
        scan(v("GI", 193, 0, -1), v("NB", 193, 0, -1), v("XM", 193, 0, -1), v("U1", 50, 51), A.mult, A.add)
        scan(v("FN"), v("NB", 0, Q), v("MK", 0, Q), v("U1", 16, 17), A.mult, A.max)
        tt(p1, v("GI", 2, 194), p2, A.max)
        dma("s", v("WW", r=0), v("FN"))
        cp(v("HI"), p1)
        dma("s", v("GG", r=0), v("HI"))
        tt(v("LO"), p1, v("HI"), A.subtract)
        dma("s", v("GG", r=1), v("LO"))
        PA, PB = v("PL", 0, 52), v("MB", 0, 52)
        mms([(PA, v("ID"), v("CL", 0, 52), True, False), (PB, v("ID"), v("CL", 52, 104), True, False)])
        act(v("RL"), v("GI", 1, 193), AF.Relu, scale=-1.0)
        if c == 1:
            constants()
        if c == 3:
            columns("TB2", TB, "a", 8, 15)

        scan(v("PR", 0, 193), v("NB", 0, 193), v("DR", 3, 196), v("U1", 17, 18), A.mult, A.max)
        tt(p2, p1, v("WK", 1, 193), A.is_equal)
        tt(p1, v("FN"), MP if c < 3 else v("MK", 0, Q), A.is_equal)
        tt(v("AA"), p2, v("PR", 1, 193), A.mult)
        tt(p1, p1, v("RL"), A.mult)
        tt(p1, p1, v("AA"), A.max)
        if c < 3:
            act(v("H0"), p1, AF.Copy)
            dma("s", v("HW", r=0), v("H0"))

        so = (c - 1) * 52
        ts(v("LG"), ind(v("WW"), v("S16", 0, 52)), M - 1538, col(cNF1), A.subtract, A.mult)
        act(v("RG"), ind(v("GG"), v("S16", 52, 104)), AF.Copy)
        mms([(PA, v("EH", 15 - b, 143 - b), v("LG", b, None, 16), False, b == 15) for b in range(16)])
        mms([(PB, E(E01, b), v("RG", b, None, 16), False, b == 15) for b in range(16)])
        if c == 3:
            cp(v("H0"), p1)
            dma("s", v("HW", r=0), v("H0"))
        tt(v("L0"), p1, v("H0"), A.subtract)
        if c == 3:
            dma("s", v("HW", r=1), v("L0"))
            columns("TB2", TB, "v", 15, 16)
        if c == 1:
            clear(2)

        def jlist(a, b):
            mms([(C, E(E01, x), v("HW", x, None, 16), x == 0, x == 15) for x in range(a, b)])

        def numbers():
            tt(v("T1"), C, v("POS"), A.max)
            cp(v("J16"), v("T1"))

        def held(who, a, b):
            src = ind(v("HW"), v("ST16", so + 2 * a, so + a + b))
            if who == "v":
                t1(v("FG", 16 * a, 16 * b), src, col(cH), A.mult)
            else:
                act(v("FG", 16 * a, 16 * b), src, AF.Copy, scale=col(cH))
        S0, S1 = ("INI" if c == 1 else "SS%d" % (c - 1)), "SS%d" % c
        SO, SI = "SO%d" % c, "SI%d" % c
        tab = v(TB, 0, W)
        if c == 1:
            cp(v("ST16"), v("STF"))
        if c < 3:
            held("a", 52, 104)
        cp(v("P16", 0, 52), PA)
        act(v("XH"), ind(tab, v("P16", 0, 26)), AF.Identity, scale=16.0, bias=1.0)
        if c < 3:
            tt(v(SO, 0, 52), PA, v(S0, 0, 52), A.is_equal)
            cp(v(S1, 0, 52), PA)
            tt(v(SO, 52, 104), PB, v(S0, 52, 104), A.is_equal)
            send([(up, down, v(SI, 52, 104), v(SO, 0, 52), "ra%d" % c), (down, up, v(SI, 0, 52), v(SO, 52, 104), "rs%d" % c)])
        cp(v("P16", 52, 104), PB)
        act(v("YH"), ind(tab, v("P16", 52, 78)), AF.Identity, scale=16.0, bias=1.0)
        if c == 3:
            cp(v(S1, 0, 52), PA)
            cp(v(S1, 52, 104), PB)
        if c == 1:
            constants2()
        if c == 2:
            act(v("OC"), v("H0"), AF.Sign)
        if c < 3:
            cp(v(S1, 52, 104), PB)
            held("v", 0, 52)
            dma("s", v("HW", r=1), v("L0"))
        tt(v(XP), ind(tab, v("P16", 26, 52)), v("XH"), A.add)
        send([(up, down, v(XI), v(XP), "rx%d" % c)])
        tt(v(YP), ind(tab, v("P16", 78, 104)), v("YH"), A.add)
        send([(down, up, v(YI), v(YP), "ry%d" % c)])
        S1 = v(S1)

        def own(s, h):
            x, xh = (v(YP), v("YH")) if s else (v(XP), v("XH"))
            if h:
                b = v("MA" if s else "MB", 0, HB)
                mms([(b, v("ID"), v("CT"), True, False), (b, v("NI"), xh, False, False), (b, v("ID"), x, False, False)])
            else:
                for b in (("MT", "MF") if s else ("PL", "MG")):
                    mms([(v(b, 0, HB), v("I16"), xh, True, False)])

        def side(s):
            x, xq = (v(XI), v("XQ")) if s else (v(YI), v("YQ"))
            return [x, xq] + [v(b, 0, HB) for b in (("MT", "MF", "MA") if s else ("PL", "MG", "MB"))]

        def landed(s):
            x, xq, bt, b0, b1 = side(s)
            mms([(b1, v("ID"), x, False, False)])

        def quot(s):
            x, xq, bt, b0, b1 = side(s)
            if s and c < 3:
                act(xq, x, AF.Identity, scale=1.0 / 16, bias=128.46875)
            else:
                ts(xq, x, 1.0 / 16, 128.46875, A.mult, A.add)

        def test(s):
            x, xq, bt, b0, b1 = side(s)
            mms([(bt, v("ID"), xq, False, True)])
            act(v("UU", s * K, s * K + HB), bt, AF.Sign, bias=-143.5625)
            mms([(b1, v("N16"), xq, False, True)])
            mms([(b0, v("ID"), xq, False, False)])

        def fold(s):
            x, xq, bt, b0, b1 = side(s)
            o = s * K
            mms([(b0, v("N8"), v("UU", o, o + HB), False, True)])
            act(v(TB, W + o, W + o + HB), b0, AF.Identity, bias=-136.0625)

        def high(s, between=lambda: None):
            x, xq, bt, b0, b1 = side(s)
            o = s * K
            ts(v("UU", o + HB, o + K), b1, 15.5, 16.0, A.is_ge, A.mult)
            between()
            tt(v(TB, W + o + HB, W + o + K), b1, v("UU", o + HB, o + K), A.subtract)

        if c < 3:
            for o in (0, 52):
                tt(v("DS", o, o + 52), v("STF", so + 2 * o, so + 2 * o + 52), v("SS%d" % c, o, o + 52), A.subtract)
            if c == 2:
                tt(v("T1"), D, v("OC"), A.mult)
                tt(p1, C, v("T1"), A.add)
            mms([(v("PL", 104, 208), v("ID"), v("CL", 104, 208), True, False)])
            mms([(v("PL", 104, 208), E(E01, b), v("FG", b, None, 16), False, b == 15) for b in range(16)])
            tt(v("G1"), v("PL", 104, 208), v(SO), A.is_lt)
            for s, h in ((0, 1), (1, 1), (1, 0), (0, 0)):
                own(s, h)
            jlist(0, 10)
            tt(v("PV", 384, 488), v("G1"), v("DS"), A.mult)
            tt(v("PV", 384, 488), v("PV", 384, 488), v(SI), A.mult)
            tt(v("DS"), v("PV", 384, 488), S1, A.add)
            cp(v("S16"), v("DS"))
            landed(1)
            scatter(c + 1, lambda: quot(1))
            test(1)
            high(1, lambda: quot(0))
            jlist(10, 16)
            landed(0)
            test(0)
            fold(1)
            numbers()
            high(0)
            fold(0)
            if c == 1:
                clear(3)
                mms([(C, v("IB"), v("THB"), True, False)])
                for a, b in ((0, 1), (1, 3), (3, 5), (5, 7), (7, 8)):
                    columns(TB, "TB2", "a", 8 + a, 8 + b)
                    columns(TB, "TB2", "v", a, b)
                    sums(C, ES, "TB2", range(a, b), False, False)
                    sums(C, ES, "TB2", range(8 + a, 8 + b), False, b == 8)
                stay(v("WK", 1, Q + 1))
        else:
            for s, h in ((0, 0), (1, 0), (0, 1), (1, 1)):
                own(s, h)
            jlist(0, 13)
            dma("s", hbm(T.ya[:]), v("SS3", 0, 52))
            dma("s", hbm(T.yb[:]), v("SS3", 52, 104))
            landed(1)
            quot(1)
            test(1)
            high(1, lambda: quot(0))
            fold(1)
            jlist(13, 16)
            landed(0)
            test(0)
            numbers()
            high(0)
            fold(0)
            for a, m, b in ((0, 2, 4), (4, 7, 10), (10, 13, 16)):
                columns(TB, "YY", "a", m, b)
                columns(TB, "YY", "v", a, m)
                dma("s", hbm(T.ym[:, Q * a:Q * b]), v("YY", Q * a, Q * b))
    for s in sorted(SEMAPHORES, key=lambda x: x[0] == "d"):
        if known["s"].get(s, 0) < count[s]:
            g.sync.wait_ge(T.sem[s], count[s])
